import numpy as np, ml_dtypes
CORES = [13,21,141,149]
N = 4
BF = ml_dtypes.bfloat16
def f(rng, *shape):
    return (rng.standard_normal(shape, dtype=np.float32) * np.exp2(rng.integers(-2, 3, shape[:-1] + (1,)))).astype(BF)
def wide(rng, *shape):
    v = f(rng, *shape).astype(np.float32); k = shape[:-2] + (1, shape[-1])
    return (v * np.exp2(rng.integers(-6, 7, k)) * (rng.random(k) > 0.0625)).astype(BF)
def gentries(a):
    return np.ascontiguousarray(a.reshape(8, 16, -1).transpose(0, 2, 1)).reshape(8, -1)
def gtable(e):
    e = np.asarray(e); return np.ascontiguousarray(e.reshape(8, -1, 16).transpose(0, 2, 1)).reshape(128, -1).astype(np.int32)
D, V, S, CL, W, B, M = 3, 2048, 256, 2, 3, 128, 128
def places(rng):
    v = rng.standard_normal((N, 8, 1, D * V), dtype=np.float32) + 0.5 * rng.standard_normal((N, 8, 16, D * V), dtype=np.float32)
    return (v * np.exp2(rng.integers(-1, 2, (N, 8, 1, 1)))).astype(BF).reshape(N, 128, D * V)
def draw(rng):
    e = np.argsort(rng.random((N, 8, CL, V)), -1)[..., :2 * S].reshape(N, 8, CL, 2, S)
    b = np.argsort(rng.random((N, 8, V)), -1)[..., :N * B].reshape(N, 8, N, B)
    return e, b, rng.integers(0, V, (N, 8, M))
def both(s):
    k = np.arange(N); return np.where(k[:, None, None, None] > k[None, None, :, None], s, s.transpose(2, 1, 0, 3))
def net(rng, pos, e, b, w):
    x = pos.astype(np.float32).reshape(N, 8, 16, D, V); own = np.zeros((N, 8, CL, S)); jo = np.zeros((N, 8, N, B))
    for r in range(N):
        for g in range(8):
            v = x[r, g][..., e[r, g]]; own[r, g] = np.mean(np.sum(np.square(v[..., 0, :] - v[..., 1, :]), 1), 0)
            for q in range(r):
                u = x[r, g][..., b[r, g, q]] - x[q, g][..., b[q, g, r]]
                jo[r, g, q] = np.mean(np.sum(np.square(u), 1), 0); jo[q, g, r] = jo[r, g, q]
    def stiffness(*shape):
        return rng.random(shape) * 0.375 * (rng.random(shape) > 0.03125)
    def inverse(m, t, z):
        return np.minimum(np.exp2(t - np.log2(m + 2.0 ** -12)), 4096) * (z > 0.03125)
    k = stiffness(N, 8, CL, S); h = inverse(own, rng.uniform(-2, 2, own.shape), rng.random(own.shape))
    kj = both(stiffness(N, 8, N, B)); hj = inverse(jo, both(rng.uniform(-2, 2, jo.shape)), both(rng.random(jo.shape)))
    return {"pos": pos, "ends": np.stack([gtable(a.reshape(8, -1)) for a in e]), "stiff": k.astype(BF).reshape(N, 8, CL * S), "inv": h.astype(BF).reshape(N, 8, CL * S),
            "bord": np.stack([gtable(a.reshape(8, -1)) for a in b]), "jstiff": kj.astype(BF).reshape(N, 8, N * B), "jinv": hj.astype(BF).reshape(N, 8, N * B), "watch": np.stack([gtable(a) for a in w])}
def setup_inputs(rng):
    return net(rng, places(rng), *draw(rng))
def setup_inputs_again(rng):
    H = max(2 * S, N * B); hub = np.argsort(rng.random((N, 8, V)), -1)[..., :H]
    e = np.take_along_axis(np.repeat(hub[:, :, None], CL, 2), np.argsort(rng.random((N, 8, CL, H)), -1)[..., :2 * S], -1).reshape(N, 8, CL, 2, S)
    b = np.take_along_axis(hub, np.argsort(rng.random((N, 8, H)), -1)[..., :N * B], -1).reshape(N, 8, N, B)
    return net(rng, places(rng), e, b, np.take_along_axis(hub, rng.integers(0, H, (N, 8, M)), -1))
def setup_inputs_ends(rng):
    e, b, w = draw(rng); s = np.arange(S); w = rng.integers(0, 2 * S, (N, 8, M))
    for c in range(CL):
        e[:, :, c, 0] = 2 * s + c; e[:, :, c, 1] = 2 * s + 1 + c
    b[:] = np.arange(N * B).reshape(N, B); w[:, :, 0] = 0
    for a in (e, b, w):
        a[:, 1::2] = V - 1 - a[:, 1::2]
    w[:, 0::2, -1] = V - 1; w[:, 1::2, -1] = 0
    return net(rng, places(rng), e, b, w)
def setup_inputs_still(rng):
    d = net(rng, rng.integers(-1, 2, (N, 128, D * V)).astype(np.float32).astype(BF), *draw(rng))
    ks = np.array([0, 0.125, 0.25, 0.375]); hs = np.array([0, 0.125, 0.25, 0.5, 1, 2])
    d["stiff"] = rng.choice(ks, (N, 8, CL * S)).astype(BF); d["inv"] = rng.choice(hs, (N, 8, CL * S)).astype(BF)
    d["jstiff"] = both(rng.choice(ks, (N, 8, N, B))).astype(BF).reshape(N, 8, N * B); d["jinv"] = both(rng.choice(hs, (N, 8, N, B))).astype(BF).reshape(N, 8, N * B)
    return d
def setup_inputs_border(rng):
    e, b, w = draw(rng); w = np.take_along_axis(b.reshape(N, 8, N * B), rng.integers(0, N * B, (N, 8, M)), -1)
    d = net(rng, places(rng), e, b, w); d["stiff"] = np.zeros((N, 8, CL * S), np.float32).astype(BF); return d
def setup_inputs_spread(rng):
    return net(rng, wide(rng, N, 128, D * V), *draw(rng))
def differ(a):
    s = np.sort(a, -1); return bool((s[..., 1:] != s[..., :-1]).all())
def check_inputs(d):
    bad = []; e, b, w = [np.stack([gentries(a) for a in d[n]]) for n in ("ends", "bord", "watch")]
    for n, a in (("ends", e), ("bord", b), ("watch", w)):
        if a.min() < 0 or a.max() >= V: bad.append(n + ": not a vertex")
    if not differ(e.reshape(N, 8, CL, 2 * S)): bad.append("a vertex twice in a class")
    if not differ(b.reshape(N, 8, N * B)): bad.append("a vertex twice in bord")
    if not (np.abs(d["pos"].astype(np.float32)) <= 8192).all(): bad.append("pos")
    for n, top in (("stiff", 0.375), ("jstiff", 0.375), ("inv", 4096), ("jinv", 4096)):
        a = d[n].astype(np.float32)
        if not ((a >= 0) & (a <= top)).all(): bad.append(n)
    for n in ("jstiff", "jinv"):
        a = d[n].astype(np.float32).reshape(N, 8, N, B)
        if not (a == a.transpose(2, 1, 0, 3)).all(): bad.append(n + ": not alike on both sides")
    return bad
def push(d, k, w):
    q = np.sum(d * d, 1, keepdims=True)
    return np.minimum(np.maximum(k * (1 - w * q), -0.25), 0.25) * d
def reference(pos, ends, stiff, inv, bord, jstiff, jinv, watch):
    x = pos.astype(np.float64).reshape(N, 8, 16, D, V)
    e = np.stack([gentries(a) for a in ends]).reshape(N, 8, CL, 2, S); b = np.stack([gentries(a) for a in bord]).reshape(N, 8, N, B); v = np.stack([gentries(a) for a in watch])
    k = stiff.astype(np.float64).reshape(N, 8, CL, S); w = inv.astype(np.float64).reshape(N, 8, CL, S)
    kj = jstiff.astype(np.float64).reshape(N, 8, N, B); wj = jinv.astype(np.float64).reshape(N, 8, N, B)
    for t in range(W):
        for c in range(CL):
            for r in range(N):
                for g in range(8):
                    i, j = e[r, g, c]; z = x[r, g]; m = push(z[..., i] - z[..., j], k[r, g, c], w[r, g, c])
                    z[..., i] += m; z[..., j] -= m
        h = np.stack([np.stack([x[r, g][..., b[r, g]] for g in range(8)]) for r in range(N)])
        for r in range(N):
            for g in range(8):
                d = h[r, g] - h[:, g, :, :, r].transpose(1, 2, 0, 3); z = x[r, g]
                z[..., b[r, g]] += push(d, kj[r, g], wj[r, g])
    y = np.stack([np.stack([x[r, g][..., v[r, g]] for g in range(8)]) for r in range(N)])
    return {"y": y.reshape(N, 128, D * M).astype(np.float32)}

@@ -1,0 +1,552 @@
+from concourse.bass import DstId, RemoteDMATransfer
+from concourse.mybir import AluOpType as ALU, ActivationFunctionType as ACT
+
+V, S = 2048, 256
+W0, J0, B0, A0, WIN = 0, 128, 512, 1024, 1536
+EPS = 1e-22
+SWEEPS = 3
+F = "float32"
+
+SCRATCH = {
+    "posb": ("sbuf", [128, 3 * V], "bfloat16"),
+    "li": ("sbuf", [128, 104], "int32"),
+    "lu": ("sbuf", [128, 96], "uint16"),
+    "ll": ("sbuf", [128, 144], "uint16"),
+    "sm": ("sbuf", [128, 192], F),
+    "tab": ("sbuf", [128, V], F),
+    "rr": ("sbuf", [128, 2688], F),
+    "ones": ("sbuf", [128, 144], F),
+    "wm": ("sbuf", [128, 144], F),
+    "eye": ("sbuf", [128, 128], F),
+    "sel": ("sbuf", [128, 512], F),
+    "kc": ("sbuf", [128, 256], "bfloat16"),
+    "wc": ("sbuf", [128, 256], "bfloat16"),
+    "wn": ("sbuf", [128, 256], F),
+    "rn": ("sbuf", [128, 256], F),
+    "kn": ("sbuf", [128, 256], F),
+    "kwo": ("sbuf", [128, 512], F),
+    "kwj": ("sbuf", [128, 392], F),
+    "rj": ("sbuf", [128, 392], F),
+    "kww": ("sbuf", [128, 128], F),
+    "rw": ("sbuf", [128, 128], F),
+    "st0": ("sbuf", [128, WIN], F),
+    "st1": ("sbuf", [128, WIN], F),
+    "st2": ("sbuf", [128, WIN], F),
+    "zz": ("sbuf", [128, 768], F),
+    "xx": ("sbuf", [128, 768], F),
+    "dd": ("sbuf", [128, 768], F),
+    "sq": ("sbuf", [128, 768], F),
+    "dj": ("sbuf", [128, 1152], F),
+    "sj": ("sbuf", [128, 1152], F),
+    "uu": ("sbuf", [128, 256], F),
+    "yb": ("sbuf", [128, 384], F),
+    "sb": ("sbuf", [128, SWEEPS * 1152], F),
+    "ld": ("sbuf", [128, SWEEPS * 1152], F),
+    "rl": ("sbuf", [128, SWEEPS * 192], F),
+}
+for _k in range(8):
+    SCRATCH["p%d" % _k] = ("psum", [128, 512], F)
+
+SEMAPHORES = (["qv", "qs", "qt", "qg", "sent"] + ["d%d" % k for k in range(14)]
+              + ["ar%d" % k for k in range(3 * SWEEPS)] + ["rin%d" % k for k in range(SWEEPS)])
+
+
+def bits(engines):
+    m = 0
+    for e in engines:
+        m |= 1 << e
+    return m
+
+
+def routes(T, topo, r):
+    me = T.cores[r]
+    others = [q for q in range(len(T.cores)) if q != r]
+    direct = [q for q in others if topo.may_write(me, T.cores[q])]
+    far = [q for q in others if q not in direct]
+    far.sort(key=lambda q: topo.host(T.cores[q]) != topo.host(me))
+    relays = {}
+    for i, q in enumerate(far):
+        can = [c for c in topo.cores_of(me) if c != me and topo.may_write(c, T.cores[q])]
+        near = [c for c in can if topo.die(c) == topo.die(me)]
+        away = [c for c in can if topo.die(c) != topo.die(me)]
+        relays[1 + i] = (near[i], away[i])
+    return direct + far, relays
+
+
+def first_hop(topo, me, direct, relay, slot, t):
+    every = topo.engines(me, relay)
+    if slot == 2 and t < SWEEPS - 1:
+        every = [e for e in every if e not in topo.engines(me, direct)]
+    return every[:len(every) // 2], every[len(every) // 2:]
+
+
+def relay_program(g, core, T, topo):
+    for r, me in enumerate(T.cores):
+        if core not in topo.cores_of(me):
+            continue
+        part, relays = routes(T, topo, r)
+        for slot in (1, 2):
+            for h in (0, 1):
+                if relays[slot][h] != core:
+                    continue
+                dst = T.cores[part[slot]]
+                rid, pid = topo.addr(dst, core)
+                for t in range(SWEEPS):
+                    g.wait_ge(T.sem["rin%d" % t], len(first_hop(topo, me, T.cores[part[0]], core, slot, t)[h]))
+                    o = t * 1152 + slot * 384 + h * 192
+                    g.remote_dma(T.ld[:, o:o + 192], T.rl[:, t * 192:(t + 1) * 192], T.sem["ar%d" % (3 * t + slot)],
+                                 T.sem.sent, pid, rid, topo.mask(core, dst))
+                g.wait_ge(T.sem.sent, SWEEPS * len(topo.engines(core, dst)))
+
+
+def emit(g, T, ops):
+    queues = {"v": g.vector, "s": g.scalar, "t": g.tensor, "g": g, "y": g.sync}
+    hist, known, waits, clocks, place, counts, marked = {}, {q: {} for q in queues}, [], [], [], {}, set()
+    for i, o in enumerate(ops):
+        q, own = o["q"], o["own"]
+        deps = set(o["after"])
+        for write, views in ((False, o["r"]), (True, o["w"])):
+            for (name, lo, hi) in views:
+                bank = SCRATCH[name][0] == "psum"
+                for (j, w2, lo2, hi2) in hist.get(name, ()):
+                    p = ops[j]
+                    same = p["q"] == q and p["own"] is None and own is None
+                    if same:
+                        if q != "t" and w2 and not write and lo < hi2 and lo2 < hi:
+                            deps.add(j)
+                    elif bank or ((w2 or write) and lo < hi2 and lo2 < hi):
+                        deps.add(j)
+        for write, views in ((False, o["r"]), (True, o["w"])):
+            for (name, lo, hi) in views:
+                hist.setdefault(name, []).append((i, write, lo, hi))
+        ws = []
+        if q is not None:
+            k = known[q]
+            for j in sorted(deps, reverse=True):
+                key, pos = place[j]
+                if k.get(key, -1) >= pos:
+                    continue
+                ws.append(j)
+                marked.add(j)
+                for a, b in clocks[j].items():
+                    if k.get(a, -1) < b:
+                        k[a] = b
+                k[key] = pos
+            clocks.append(dict(k))
+        else:
+            clocks.append({})
+        waits.append(ws)
+        if own is None:
+            counts[q] = counts.get(q, 0) + 1
+            place.append((q, counts[q]))
+        else:
+            place.append((("op", i), 0))
+    n, value = {}, {}
+    for i, o in enumerate(ops):
+        if o["own"] is not None:
+            value[i] = o["own"]
+        elif i in marked:
+            n[o["q"]] = n.get(o["q"], 0) + 1
+            value[i] = ("q" + o["q"], n[o["q"]])
+    for i, o in enumerate(ops):
+        if o["q"] is None:
+            continue
+        e = queues[o["q"]]
+        for j in waits[i]:
+            e.wait_ge(T.sem[value[j][0]], value[j][1])
+        if o["fn"] is None:
+            continue
+        ins = o["fn"](e)
+        if o["dma"]:
+            ins.then_inc(T.sem[o["own"][0]], 16)
+        elif o["own"] is None and i in marked:
+            ins.then_inc(T.sem[value[i][0]], 1)
+
+
+def rank_program(g, core, T, topo):
+    rank = T.rank_of(core)
+    if rank is None:
+        relay_program(g, core, T, topo)
+        return
+    part, relays = routes(T, topo, rank)
+    ops = []
+
+    def vw(name, lo, hi, step=1, parts=128):
+        return (name, lo, hi, step, parts)
+
+    def ap(v):
+        if len(v) == 2:
+            return ap(v[0]).indirect(ap(v[1]))
+        if v[3] == 1:
+            return T[v[0]][0:v[4], v[1]:v[2]]
+        return T[v[0]][0:v[4], v[1]:v[2]:v[3]]
+
+    def span(v):
+        return [span(v[0])[0], span(v[1])[0]] if len(v) == 2 else [v[0:3]]
+
+    def add(q, fn, ins, out, own=None, dma=False, after=()):
+        r, w = [], []
+        for v in ins:
+            r += span(v)
+        if out is not None:
+            w += span(out)[0:1]
+            r += span(out)[1:]
+        ops.append({"q": q, "fn": fn, "r": r, "w": w, "own": own, "dma": dma, "after": list(after)})
+        return len(ops) - 1
+
+    ndma = [0]
+
+    def load(q, out, src):
+        ndma[0] += 1
+        return add(q, lambda e: e.dma_start(ap(out), src), [], out, ("d%d" % (ndma[0] - 1), 16), True)
+
+    def store(q, dst, src):
+        ndma[0] += 1
+        return add(q, lambda e: e.dma_start(dst, ap(src)), [src], None, ("d%d" % (ndma[0] - 1), 16), True)
+
+    def tt(out, a, b, op):
+        add("v", lambda e: e.tensor_tensor(ap(out), ap(a), ap(b), op), [a, b], out)
+
+    def ts(out, a, s1, op0, s2=None, op1=None):
+        if op1 is None:
+            add("v", lambda e: e.tensor_scalar(ap(out), ap(a), s1, None, op0), [a], out)
+        else:
+            add("v", lambda e: e.tensor_scalar(ap(out), ap(a), s1, s2, op0, op1), [a], out)
+
+    def cp(q, out, a):
+        if q == "v":
+            add("v", lambda e: e.tensor_copy(ap(out), ap(a)), [a], out)
+        else:
+            add("s", lambda e: e.activation(ap(out), ap(a), ACT.Copy), [a], out)
+
+    def square(out, a):
+        add("s", lambda e: e.activation(ap(out), ap(a), ACT.Square), [a], out)
+
+    def fill(out, c):
+        add("v", lambda e: e.memset(ap(out), c), [], out)
+
+    def mm(out, lhs, rhs, start, stop):
+        add("t", lambda e: e.matmul(ap(out), ap(lhs), ap(rhs), start, stop), [lhs, rhs], out)
+
+    def select(out, pattern, base):
+        src = vw("ones", 0, out[2] - out[1], 1, out[4])
+        add("g", lambda e: e.affine_select(ap(out), ap(src), pattern, ALU.is_equal, 0.0, base, 1), [src], out)
+
+    def clamp(out, a):
+        ts(out, a, -0.25, ALU.max, 0.25, ALU.min)
+
+    def st(p, lo, hi):
+        return vw("st%d" % p, lo, hi)
+
+    def pos(p):
+        return vw("posb", p * V, (p + 1) * V)
+
+    def table_scatter(lo, hi, base):
+        ts((vw("tab", 0, V), vw("lu", lo, hi)), vw("rr", 512, 512 + 16 * (hi - lo)), 1.0, ALU.mult, float(base), ALU.add)
+
+    def table_gather(q, at, lo, hi):
+        cp(q, vw("rr", at, at + 16 * (hi - lo)), (vw("tab", 0, V), vw("lu", lo, hi)))
+
+    def to_lists(col, at, n):
+        for a in range(16):
+            mm(vw("p7", col, col + n), vw("wm", 15 - a, 143 - a), vw("rr", at + a, at + 16 * n, 16), a == 0, a == 15)
+
+    def spread(out, block, src):
+        return (out, vw("sel", block * 128, block * 128 + 128, 1, 32), src)
+
+    def negative(lo):
+        a, src = vw("wn", lo, lo + 128, 1, 32), vw("wc", lo, lo + 128, 1, 32)
+        add("s", lambda e: e.activation(ap(a), ap(src), ACT.Identity, bias=-EPS, scale=-1.0), [src], a)
+
+    def product(lo):
+        tt(vw("kn", lo, lo + 128, 1, 32), vw("kc", lo, lo + 128, 1, 32), vw("wn", lo, lo + 128, 1, 32), ALU.mult)
+
+    def inverse(lo):
+        a, r = vw("wn", lo, lo + 128, 1, 32), vw("rn", lo, lo + 128, 1, 32)
+        add("v", lambda e: e.reciprocal(ap(r), ap(a)), [a], r)
+
+    def pieces(c, win, lst):
+        def at(name, p, h):
+            return vw(name, p * S, (p + 1) * S) if h is None else vw(name, p * S + h * 128, p * S + h * 128 + 128)
+
+        def ends(p, z, h):
+            o = lst[1] + 16 * z
+            return (win(p), vw(lst[0], o, o + 16) if h is None else vw(lst[0], o + 8 * h, o + 8 * h + 8))
+
+        def mcol(p, h):
+            name, o = ("p5", p * S) if p < 2 else ("p6", 0)
+            return vw(name, o, o + S) if h is None else vw(name, o + h * 128, o + h * 128 + 128)
+
+        def to(p, z, h):
+            o = (A0, B0)[c] + z * S
+            return st(p, o, o + S) if h is None else st(p, o + h * 128, o + h * 128 + 128)
+
+        acc = lambda h: vw("p%d" % (2 + h), 0, 128)
+        f = {}
+        f["Z"] = lambda p, h=None: cp("s", at("zz", p, h), ends(p, 1, h))
+        f["Y"] = lambda p, h=None: cp("v", at("zz", p, h), ends(p, 1, h))
+        f["X"] = lambda p, h=None: cp("s", at("xx", p, h), ends(p, 0, h))
+        f["d"] = lambda p, h=None: tt(at("dd", p, h), ends(p, 0, h), at("zz", p, h), ALU.subtract)
+        f["q"] = lambda p, h=None: square(at("sq", p, h), at("dd", p, h))
+        f["r"] = lambda h: mm(*spread(acc(h), 2 * c + h, vw("rn", 0, 128, 1, 32)), True, False)
+        f["a"] = lambda p, h: mm(acc(h), vw("eye", 0, 128), at("sq", p, h), False, p == 2)
+        f["u"] = lambda h: tt(vw("uu", h * 128, h * 128 + 128), acc(h), vw("kwo", c * S + h * 128, c * S + h * 128 + 128), ALU.mult)
+        f["c"] = lambda h: clamp(vw("p4", h * 128, h * 128 + 128), vw("uu", h * 128, h * 128 + 128))
+        f["m"] = lambda p, h: tt(mcol(p, h), vw("p4", h * 128, h * 128 + 128), at("dd", p, h), ALU.mult)
+        f["x"] = lambda p, h=None: tt(to(p, 0, h), at("xx", p, h), mcol(p, h), ALU.add)
+        f["z"] = lambda p, h=None: tt(to(p, 1, h), at("zz", p, h), mcol(p, h), ALU.subtract)
+        return f
+
+    def run(f, text, hooks=None):
+        for w in text.split():
+            if w[0] == "@":
+                hooks[w[1:]]()
+                continue
+            f[w[0]](*[int(ch) if ch.isdigit() else "ab".index(ch) for ch in w[1:]])
+
+    def border(q, t, slot, p):
+        o = t * 1152 + slot * 384 + p * 128
+        cp(q, vw("sb", o, o + 128), (st(p, J0, WIN), vw("ll", 32 + 8 * slot, 40 + 8 * slot)))
+
+    sent = [0]
+
+    def exchange(t):
+        dcore = T.cores[part[0]]
+        off = topo.engines(core, dcore)
+
+        def relayed(slot):
+            src = vw("sb", t * 1152 + slot * 384, t * 1152 + slot * 384 + 384)
+            masks = first_hop(topo, core, dcore, relays[slot][0], slot, t)
+
+            def fn(e):
+                trs = []
+                for h in (0, 1):
+                    rid, pid = topo.addr(relays[slot][h], core)
+                    o = src[1] + h * 192
+                    trs.append(RemoteDMATransfer(dst_ids=[DstId(rid=rid, pnc=pid)], dma_engine_mask=bits(masks[h]),
+                                                 remote_sem=T.sem["rin%d" % t], src=T.sb[:, o:o + 192],
+                                                 dst=T.rl[:, t * 192:(t + 1) * 192]))
+                return e.remote_dma_fused(trs, local_sem=T.sem.sent)
+            add("g", fn, [src], None, ("sent", 0))
+            sent[0] += len(masks[0]) + len(masks[1])
+
+        def direct():
+            src = vw("sb", t * 1152, t * 1152 + 384)
+            rid, pid = topo.addr(dcore, core)
+            add("g", lambda e: e.remote_dma(T.ld[:, src[1]:src[2]], ap(src), T.sem["ar%d" % (3 * t)], T.sem.sent,
+                                            pid, rid, bits(off)), [src], None, ("sent", 0))
+            sent[0] += len(off)
+
+        relayed(1)
+        if t < SWEEPS - 1:
+            direct()
+            relayed(2)
+        else:
+            relayed(2)
+            direct()
+        for slot in range(3):
+            o = t * 1152 + slot * 384
+            n = len(off) if slot == 0 else sum(len(topo.engines(c, T.cores[part[slot]])) for c in relays[slot])
+            add(None, None, [], vw("ld", o, o + 384), ("ar%d" % (3 * t + slot), n))
+
+    xbank = ("p2", "p3", "p0")
+
+    def own_side(t, slot):
+        o = t * 1152 + slot * 384
+        cp("s", vw(xbank[slot], 0, 384), vw("sb", o, o + 384))
+
+    def coefficient(sqv, r, kw):
+        return [lambda: tt(vw("p4", 0, 128), r, sqv(0), ALU.add),
+                lambda: tt(vw("p4", 128, 256), vw("p4", 0, 128), sqv(1), ALU.add),
+                lambda: tt(vw("p4", 256, 384), vw("p4", 128, 256), sqv(2), ALU.add),
+                lambda: tt(vw("uu", 0, 128), vw("p4", 256, 384), kw, ALU.mult),
+                lambda: clamp(vw("p4", 384, 512), vw("uu", 0, 128))]
+
+    def joint(t, between, done):
+        col = lambda name, p, b: vw(name, b + p * 128, b + p * 128 + 128)
+
+        def moves(slot):
+            o = t * 1152 + slot * 384
+            m = lambda p: lambda: tt(col("p5", p, 0), vw("p4", 384, 512), col("dj", p, slot * 384), ALU.mult)
+
+            def x(p):
+                def fn():
+                    tt(st(p, J0 + slot * 128, J0 + slot * 128 + 128), col("sb", p, o), col("p5", p, 0), ALU.add)
+                    if slot == 2:
+                        done(p)
+                return fn
+            return [m(0), m(1), x(0), m(2), x(1), x(2)]
+
+        for slot in range(3):
+            o = t * 1152 + slot * 384
+            if slot == 2:
+                between()
+            for p in range(3):
+                tt(col("dj", p, slot * 384), col(xbank[slot], p, 0), col("ld", p, o), ALU.subtract)
+                square(col("sj", p, slot * 384), col("dj", p, slot * 384))
+            chain = coefficient(lambda p: col("sj", p, slot * 384), col("p1", slot, 0), col("kwj", slot, 8))
+            other = moves(slot - 1) if slot else []
+            for k in range(6):
+                if other:
+                    other[k]()
+                if k:
+                    chain[k - 1]()
+        for fn in moves(2):
+            fn()
+
+    sm = lambda lo, hi: vw("sm", lo, hi)
+    p7 = lambda lo, hi: vw("p7", lo, hi)
+    ll = lambda lo, hi: vw("ll", lo, hi)
+
+    load("y", vw("li", 0, 64), T.ends[:, :])
+    load("s", vw("wc", 0, 128, 1, 32), T.inv[:, :])
+    load("s", vw("kc", 0, 128, 1, 32), T.stiff[:, :])
+    for p in range(3):
+        load("y", pos(p), T.pos[:, p * V:(p + 1) * V])
+    load("s", vw("li", 72, 104), T.bord[:, :])
+    load("s", vw("li", 64, 72), T.watch[:, :])
+    load("y", vw("wc", 128, 256, 1, 32), T.jinv[:, :])
+    load("y", vw("kc", 128, 256, 1, 32), T.jstiff[:, :])
+    fill(vw("ones", 0, 144), 1.0)
+    ramp = vw("rr", 512, 1024)
+    add("g", lambda e: e.iota(ap(ramp), [[1, 512]], 0, 0, allow_small_or_imprecise_dtypes=True), [], ramp)
+    fill(vw("tab", 0, V), 0.0)
+    for a in range(4):
+        select(vw("sel", a * 128, a * 128 + 128, 1, 32), [[-4, 8], [0, 16]], -a)
+    select(vw("wm", 0, 144), [[-16, 9], [256, 16]], -15 * 256)
+    select(vw("eye", 0, 128), [[-1, 128]], 0)
+    cp("v", vw("lu", 0, 64), vw("li", 0, 64))
+    negative(0)
+    product(0)
+    table_scatter(0, 32, A0)
+    for a in range(4):
+        mm(*spread(vw("p0", a * 128, a * 128 + 128), a, vw("kn", 0, 128, 1, 32)), True, True)
+    cp("s", vw("kwo", 0, 512), vw("p0", 0, 512))
+    table_gather("s", 0, 32, 64)
+    to_lists(0, 0, 64)
+    inverse(0)
+
+    def first_list():
+        ts(sm(0, 32), p7(32, 64), float(B0), ALU.add)
+        ts(sm(64, 88), p7(32, 56), float(J0), ALU.add)
+        tt(sm(32, 64), p7(0, 32), sm(0, 32), ALU.max)
+        cp("v", sm(88, 96), p7(32, 40))
+        ts(ll(0, 32), sm(32, 64), float(B0), ALU.subtract)
+
+    def other_lists():
+        cp("v", vw("lu", 64, 72), vw("li", 64, 72))
+        for s in range(3):
+            cp("v", vw("lu", 72 + 8 * s, 80 + 8 * s), vw("li", 72 + 8 * part[s], 80 + 8 * part[s]))
+
+    def border_list():
+        tt(sm(96, 120), p7(72, 96), sm(64, 88), ALU.max)
+        ts(ll(32, 56), sm(96, 120), float(J0), ALU.subtract)
+
+    def later_lists():
+        tt(sm(160, 192), p7(128, 160), sm(120, 152), ALU.max)
+        ts(ll(56, 88), p7(96, 128), float(J0), ALU.subtract)
+        ts(ll(88, 120), sm(160, 192), float(J0), ALU.subtract)
+
+    def start(p, region, n, col, q="s"):
+        cp(q, st(p, region, region + 16 * n), (pos(p), vw("lu", col, col + n)))
+
+    hooks = {
+        "B0": lambda: start(0, B0, 32, 32), "B1": lambda: start(1, B0, 32, 32), "B2": lambda: start(2, B0, 32, 32, "v"),
+        "J0": lambda: start(0, J0, 24, 72), "J1": lambda: start(1, J0, 24, 72), "J2": lambda: start(2, J0, 24, 72),
+        "sB": lambda: table_scatter(32, 64, B0), "l1": first_list, "ol": other_lists,
+        "g2": lambda: table_gather("s", 1024, 64, 96), "t2": lambda: to_lists(64, 1024, 32), "bl": border_list,
+    }
+
+    def into(f):
+        return {k: (lambda text: lambda: run(f, text))(v) for k, v in PRE.items()}
+
+    def send_hooks(t):
+        def some(text):
+            return lambda: [border(w[0], t, int(w[1]), int(w[2])) for w in text.split()]
+        return {"n%d" % p: some(SENDS[t][p]) for p in range(3)}
+
+    TAIL = "ua ca m0a m1a m2a ub x0a cb z0a m0b m1b x0b z0b @n0 m2b x1 z1 @n1 x2 z2 @n2"
+    PRE = {"n0": "Z0 X0", "n1": "Z1", "n2": "Z2a"}
+    HEAD = "ra rb d0a q0a d1a q1a Z2b a0a d2a q2a a1a a2a d0b q0b d1b q1b a0b d2b q2b a1b a2b X1 X2 "
+    JPRE = ("Z0a", "Z1a", "Z2a")
+    JHEAD = "ra rb d0a q0a Y0b d1a q1a a0a d2a Z1b q2a Z2b a1a a2a d0b q0b d1b q1b a0b d2b q2b a1b a2b X0 X1 X2 "
+    FIRST = ("Z0 d0 X0 q0 @sB Z1 @B0 X1 d1 ra rb a0a a0b Z2a d2a Z2b q1 q2a d2b q2b a1a a2a a1b a2b "
+             "@ol @l1 X2 @B1 @B2 @g2 @t2 @J0 ")
+    SECOND = HEAD + "@J1 @J2 @bl "
+    SENDS = (("s10", "s11 s00 s01", "v12 v02 s20 s21 v22"),
+             ("s10 s00 s20", "s11 s01 s21", "v12 s02 v22"),
+             ("s10 s20 s00", "s11 s21", "v12 v22 s01 s02"))
+
+    c0 = pieces(0, pos, ("lu", 0))
+    c1 = pieces(1, lambda p: st(p, B0, WIN), ("ll", 0))
+    run(c0, FIRST + TAIL, dict(hooks, **into(c1)))
+    run(c1, SECOND + TAIL, dict(hooks, **send_hooks(0)))
+    c0 = pieces(0, lambda p: st(p, J0, WIN), ("ll", 56))
+    c1 = pieces(1, lambda p: st(p, J0, WIN), ("ll", 88))
+
+    for t in range(SWEEPS):
+        if t > 0:
+            run(c0, JHEAD + TAIL, into(c1))
+            run(c1, HEAD + TAIL, send_hooks(t))
+        exchange(t)
+        if t == SWEEPS - 1:
+            break
+        if t == 0:
+            negative(128)
+            cp("v", sm(120, 152), p7(0, 32))
+            fill(vw("kwj", 0, 8), 0.0)
+            fill(vw("rj", 0, 8), 0.0)
+            product(128)
+            inverse(128)
+            for s in range(3):
+                mm(*spread(vw("p6", s * 128, s * 128 + 128), part[s], vw("kn", 128, 256, 1, 32)), True, True)
+            for s in range(3):
+                mm(*spread(vw("p1", s * 128, s * 128 + 128), part[s], vw("rn", 128, 256, 1, 32)), True, True)
+            table_scatter(72, 96, J0)
+        own_side(t, 0)
+        own_side(t, 1)
+        if t == 0:
+            cp("s", vw("kwj", 8, 392), vw("p6", 0, 384))
+        own_side(t, 2)
+        if t == 0:
+            table_gather("v", 1536, 0, 32)
+            table_gather("s", 2048, 32, 72)
+            to_lists(96, 1536, 72)
+        else:
+            cp("s", vw("rj", 8, 392), vw("p1", 0, 384))
+            for p in range(3):
+                start(p, W0, 8, 64)
+            tt(sm(0, 8), p7(64, 72), sm(88, 96), ALU.max)
+            ts(sm(8, 16), p7(160, 168), float(B0), ALU.is_lt)
+            tt(sm(16, 24), p7(160, 168), sm(0, 8), ALU.max)
+            tt(sm(24, 32), p7(160, 168), sm(8, 16), ALU.mult)
+            cp("v", ll(120, 128), sm(16, 24))
+            ts(ll(128, 136), sm(24, 32), float(J0 - 8), ALU.subtract, 0.0, ALU.max)
+            ts(sm(32, 40), sm(24, 32), float(J0), ALU.subtract, 0.0, ALU.max)
+            ts(sm(40, 48), sm(24, 32), float(J0 + 128), ALU.is_ge, 256.0, ALU.mult)
+            ts(sm(48, 56), sm(24, 32), float(J0 + 256), ALU.is_ge, 256.0, ALU.mult)
+            tt(sm(56, 64), sm(32, 40), sm(40, 48), ALU.add)
+            tt(sm(152, 160), sm(56, 64), sm(48, 56), ALU.add)
+            cp("v", ll(136, 144), sm(152, 160))
+        joint(t, later_lists if t == 0 else (lambda: None), lambda p: run(c0, JPRE[p]))
+
+    o = (SWEEPS - 1) * 1152
+    col = lambda name, p: vw(name, p * 128, p * 128 + 128)
+    cp("v", vw("rw", 0, 128), (vw("rj", 0, 392), ll(128, 136)))
+    cp("v", vw("kww", 0, 128), (vw("kwj", 0, 392), ll(128, 136)))
+    for p in range(3):
+        cp("s", col("xx", p), (st(p, 0, WIN), ll(120, 128)))
+    cp("v", vw("p2", 0, 128), vw("rw", 0, 128))
+    for p in range(3):
+        tt(col("dj", p), (vw("ld", o + p * 128, o + p * 128 + 896), ll(136, 144)), col("xx", p), ALU.subtract)
+        square(col("sj", p), col("dj", p))
+    for fn in coefficient(lambda p: col("sj", p), vw("p2", 0, 128), vw("kww", 0, 128)):
+        fn()
+    m = lambda p: tt(col("p5", p), vw("p4", 384, 512), col("dj", p), ALU.mult)
+    x = lambda p: tt(col("yb", p), col("xx", p), col("p5", p), ALU.subtract)
+    m(0); m(1); x(0); m(2); x(1); x(2)
+    stored = store("y", T.y[:, :], vw("yb", 0, 384))
+    add("y", None, [], None, after=[stored])
+    total = add(None, None, [], None, ("sent", sent[0]))
+    add("g", None, [], None, after=[total])
+    emit(g, T, ops)

@@ -6,24 +6,30 @@ W0, J0, B0, A0, WIN = 0, 128, 512, 1024, 1536
 EPS = 1e-22
 SWEEPS = 3
 F = "float32"
+GATHER, SCATTER, MATMUL, FIXED, HOP, SELF = 1.56, 3.8, 3, {"v": 30, "s": 140}, 200, 70
+DMA, LOAD, ISSUE, WRITE, COLD = 1300, 170, 300, (3600, 5000, 5800), 3000
 
 SCRATCH = {
     "posb": ("sbuf", [128, 3 * V], "bfloat16"),
-    "li": ("sbuf", [128, 104], "int32"),
+    "li": ("sbuf", [128, 96], "int32"),
     "lu": ("sbuf", [128, 96], "uint16"),
     "ll": ("sbuf", [128, 144], "uint16"),
-    "sm": ("sbuf", [128, 192], F),
+    "sm": ("sbuf", [128, 224], F),
     "tab": ("sbuf", [128, V], F),
-    "rr": ("sbuf", [128, 2688], F),
-    "ones": ("sbuf", [128, 144], F),
-    "wm": ("sbuf", [128, 144], F),
+    "ramp": ("sbuf", [128, 512], F),
+    "rv": ("sbuf", [128, 2176], "float16"),
+    "ones": ("sbuf", [128, 128], F),
+    "oneb": ("sbuf", [128, 272], "bfloat16"),
+    "eyeb": ("sbuf", [128, 256], "bfloat16"),
+    "wv": ("sbuf", [128, 144], "bfloat16"),
+    "row": ("sbuf", [128, 160], "bfloat16"),
     "eye": ("sbuf", [128, 128], F),
     "sel": ("sbuf", [128, 512], F),
-    "kc": ("sbuf", [128, 256], "bfloat16"),
-    "wc": ("sbuf", [128, 256], "bfloat16"),
-    "wn": ("sbuf", [128, 256], F),
-    "rn": ("sbuf", [128, 256], F),
-    "kn": ("sbuf", [128, 256], F),
+    "kc": ("sbuf", [128, 128], "bfloat16"),
+    "wc": ("sbuf", [128, 128], "bfloat16"),
+    "wn": ("sbuf", [128, 128], F),
+    "rn": ("sbuf", [128, 128], F),
+    "kn": ("sbuf", [128, 128], F),
     "kwo": ("sbuf", [128, 512], F),
     "kwj": ("sbuf", [128, 392], F),
     "rj": ("sbuf", [128, 392], F),
@@ -32,6 +38,8 @@ SCRATCH = {
     "st0": ("sbuf", [128, WIN], F),
     "st1": ("sbuf", [128, WIN], F),
     "st2": ("sbuf", [128, WIN], F),
+    "xb": ("sbuf", [128, 768], "bfloat16"),
+    "zb": ("sbuf", [128, 768], "bfloat16"),
     "zz": ("sbuf", [128, 768], F),
     "xx": ("sbuf", [128, 768], F),
     "dd": ("sbuf", [128, 768], F),
@@ -39,16 +47,37 @@ SCRATCH = {
     "dj": ("sbuf", [128, 1152], F),
     "sj": ("sbuf", [128, 1152], F),
     "uu": ("sbuf", [128, 256], F),
+    "cc": ("sbuf", [128, 256], F),
     "yb": ("sbuf", [128, 384], F),
     "sb": ("sbuf", [128, SWEEPS * 1152], F),
     "ld": ("sbuf", [128, SWEEPS * 1152], F),
-    "rl": ("sbuf", [128, SWEEPS * 192], F),
+    "rl": ("sbuf", [128, SWEEPS * 384], F),
 }
 for _k in range(8):
     SCRATCH["p%d" % _k] = ("psum", [128, 512], F)
 
 SEMAPHORES = (["qv", "qs", "qt", "qg", "sent"] + ["d%d" % k for k in range(14)]
-              + ["ar%d" % k for k in range(3 * SWEEPS)] + ["rin%d" % k for k in range(SWEEPS)])
+              + ["ar%d" % k for k in range(3 * SWEEPS)] + ["rin%d" % k for k in range(2 * SWEEPS)])
+
+FIRST = ("@kn @sA Z0 X0 d0 @g1 @rn @sB q0 Z1 X1 d1 @kw X2 Z2 q1 d2a d2b q2a q2b a0a ra e1a a0b rb a1b e2b @t1 "
+         "@ol @g3 @l1 @B0 @B1 @B2 @J0 @J1 @t3 ")
+SECOND = "@J2 @bl"
+HEAD = "ra rb Z2b d0a q0a d1a q1a a0a d2a q2a e1a d0b q0b d1b q1b a0b d2b q2b a1b e2b "
+JHEAD = "ra rb Y0b d0a Z1b q0a d1a q1a a0a d2a q2a e1a d0b q0b d1b q1b a0b Y2b d2b q2b a1b e2b "
+FTAIL = "Aa . Ua . ca . m0a m1a m2a ub x0a cb z0a m0b m1b x0b z0b @n0 m2b x1 z1 @n1 x2 z2 @n2"
+TAIL = "X0 X1 X2 " + FTAIL
+PRE = ("Z0", "Z1", "Z2a")
+JPRE = ("Z0a", "Z1a", "Z2a")
+CUT = 72
+ZERO = 640
+SENDS = (("G10 G00 G20", "G11 G01 G21", "H12 s1 H02 s0 H22 s2"),
+         ("G10 G00 G20", "G11 G01 G21", "H12 s1 H02 s0 H22 s2"),
+         ("G10 G20 G00", "G11 G21 G01", "H12 s1 H22 s2 H02 s0"))
+PLAN = (((1,), (0,), (2,)), ((1,), (0,), (2,)), ((1,), (2,), (0,)))
+REST = ((2,), (2,), ())
+JOINTS = ("R0 d00 d01 d02 s00 S01 S02 @ U0 . c0 r1 d10 a10 d11 a11 d12 e12 m00 m01 x00 m02 x01 x02 "
+          "r2 d20 a20 d21 a21 d22 e22 u1 . c1 . m10 m11 x10 m12 x11 x12 u2 c2 m20 m21 x20 m22 x21 x22")
+ACC = ("p2", "p6", "p2")
 
 
 def bits(engines):
@@ -73,52 +102,94 @@ def routes(T, topo, r):
     return direct + far, relays
 
 
-def first_hop(topo, me, direct, relay, slot, t):
-    every = topo.engines(me, relay)
-    if slot == 2 and t < SWEEPS - 1:
-        every = [e for e in every if e not in topo.engines(me, direct)]
-    return every[:len(every) // 2], every[len(every) // 2:]
+def calls(T, topo, r, t):
+    me = T.cores[r]
+    part, relays = routes(T, topo, r)
+    direct = T.cores[part[0]]
+    every, off = topo.engines(me, relays[1][0]), topo.engines(me, direct)
+    rest = [e for e in every if e not in off]
+    out, gone = [], False
+    for slots in PLAN[t]:
+        trs = []
+        gone = gone or 0 in slots
+        for k, slot in enumerate(slots):
+            if slot == 0:
+                trs += [(0, 0, 384, direct, off)] if len(slots) == 1 else [(0, 0, 192, direct, off[0::2]), (0, 192, 384, direct, off[1::2])]
+            else:
+                use = rest if gone and (slot in REST[t] or 0 in slots) else every if len(slots) == 1 else (rest, off)[k]
+                trs += [(slot, 0, 192, relays[slot][1], use[1::2]), (slot, 192, 384, relays[slot][0], use[0::2])]
+        out.append(trs)
+    return out
 
 
 def relay_program(g, core, T, topo):
     for r, me in enumerate(T.cores):
         if core not in topo.cores_of(me):
             continue
-        part, relays = routes(T, topo, r)
-        for slot in (1, 2):
-            for h in (0, 1):
-                if relays[slot][h] != core:
-                    continue
-                dst = T.cores[part[slot]]
-                rid, pid = topo.addr(dst, core)
-                for t in range(SWEEPS):
-                    g.wait_ge(T.sem["rin%d" % t], len(first_hop(topo, me, T.cores[part[0]], core, slot, t)[h]))
-                    o = t * 1152 + slot * 384 + h * 192
-                    g.remote_dma(T.ld[:, o:o + 192], T.rl[:, t * 192:(t + 1) * 192], T.sem["ar%d" % (3 * t + slot)],
+        part, sent = routes(T, topo, r)[0], 0
+        for t in range(SWEEPS):
+            for trs in calls(T, topo, r, t):
+                for slot, lo, hi, to, engines in trs:
+                    if to != core:
+                        continue
+                    dst = T.cores[part[slot]]
+                    rid, pid = topo.addr(dst, core)
+                    g.wait_ge(T.sem["rin%d" % t], len(engines))
+                    o = t * 1152 + slot * 384
+                    g.remote_dma(T.ld[:, o + lo:o + hi], T.rl[:, t * 384 + lo:t * 384 + hi], T.sem["ar%d" % (3 * t + slot)],
                                  T.sem.sent, pid, rid, topo.mask(core, dst))
-                g.wait_ge(T.sem.sent, SWEEPS * len(topo.engines(core, dst)))
+                    sent += len(topo.engines(core, dst))
+        if sent:
+            g.wait_ge(T.sem.sent, sent)
+
+
+def meetings(ops):
+    hist, out = {}, []
+    for i, o in enumerate(ops):
+        met = {}
+        for write, views in ((False, o["r"]), (True, o["w"])):
+            for (name, lo, hi, pa, pb) in views:
+                bank = SCRATCH[name][0] == "psum"
+                for (j, w2, lo2, hi2, pa2, pb2) in hist.get(name, ()):
+                    p = ops[j]
+                    over = (w2 or write) and lo < hi2 and lo2 < hi and pa < pb2 and pa2 < pb
+                    if p["q"] == o["q"] and p["own"] is None and o["own"] is None:
+                        if over or (bank and o["q"] == "t"):
+                            met[j] = met.get(j, False) or (o["q"] != "t" and over)
+                    elif bank or over:
+                        met[j] = True
+        for write, views in ((False, o["r"]), (True, o["w"])):
+            for v in views:
+                hist.setdefault(v[0], []).append((i, write) + v[1:])
+        out.append(met)
+    return out
+
+
+def arrange(ops):
+    begin, busy = {}, {}
+    for i, (o, met) in enumerate(zip(ops, meetings(ops))):
+        need = {j: (HOP if ops[j]["q"] != o["q"] else SELF) if waited else 0 for j, waited in met.items()}
+        need.update({j: HOP for j in o["after"] + o["soft"]})
+        t = max([begin[j] + ops[j]["takes"] + lag for j, lag in need.items()] + [0])
+        if o["q"] is not None:
+            if o["stay"] or any(v[0] == "ld" for v in o["r"]):
+                t = max([t] + [hi for lo, hi in busy[o["q"]]])
+            for lo, hi in sorted(busy.setdefault(o["q"], [])):
+                if t + o["holds"] <= lo:
+                    break
+                t = max(t, hi)
+            busy[o["q"]].append((t, t + o["holds"]))
+        begin[i] = t
+    return [ops[i] for i in sorted(range(len(ops)), key=lambda i: (begin[i], i))]
 
 
 def emit(g, T, ops):
     queues = {"v": g.vector, "s": g.scalar, "t": g.tensor, "g": g, "y": g.sync}
-    hist, known, waits, clocks, place, counts, marked = {}, {q: {} for q in queues}, [], [], [], {}, set()
-    for i, o in enumerate(ops):
+    known, waits, clocks, place, counts, marked = {q: {} for q in queues}, [], [], [], {}, set()
+    at = {o["n"]: i for i, o in enumerate(ops)}
+    for i, (o, met) in enumerate(zip(ops, meetings(ops))):
         q, own = o["q"], o["own"]
-        deps = set(o["after"])
-        for write, views in ((False, o["r"]), (True, o["w"])):
-            for (name, lo, hi) in views:
-                bank = SCRATCH[name][0] == "psum"
-                for (j, w2, lo2, hi2) in hist.get(name, ()):
-                    p = ops[j]
-                    same = p["q"] == q and p["own"] is None and own is None
-                    if same:
-                        if q != "t" and w2 and not write and lo < hi2 and lo2 < hi:
-                            deps.add(j)
-                    elif bank or ((w2 or write) and lo < hi2 and lo2 < hi):
-                        deps.add(j)
-        for write, views in ((False, o["r"]), (True, o["w"])):
-            for (name, lo, hi) in views:
-                hist.setdefault(name, []).append((i, write, lo, hi))
+        deps = set(at[n] for n in o["after"]) | set(j for j, waited in met.items() if waited)
         ws = []
         if q is not None:
             k = known[q]
@@ -169,40 +240,53 @@ def rank_program(g, core, T, topo):
         relay_program(g, core, T, topo)
         return
     part, relays = routes(T, topo, rank)
-    ops = []
+    ops, floor, small = [], [], []
 
-    def vw(name, lo, hi, step=1, parts=128):
+    def vw(name, lo, hi, step=1, parts=(0, 128)):
         return (name, lo, hi, step, parts)
 
     def ap(v):
         if len(v) == 2:
             return ap(v[0]).indirect(ap(v[1]))
         if v[3] == 1:
-            return T[v[0]][0:v[4], v[1]:v[2]]
-        return T[v[0]][0:v[4], v[1]:v[2]:v[3]]
+            return T[v[0]][v[4][0]:v[4][1], v[1]:v[2]]
+        return T[v[0]][v[4][0]:v[4][1], v[1]:v[2]:v[3]]
 
     def span(v):
-        return [span(v[0])[0], span(v[1])[0]] if len(v) == 2 else [v[0:3]]
+        return [span(v[0])[0], span(v[1])[0]] if len(v) == 2 else [v[0:3] + v[4]]
 
-    def add(q, fn, ins, out, own=None, dma=False, after=()):
+    def cycles(q, ins, out):
+        if len(out) == 2:
+            return 60 + SCATTER * 16 * (out[1][2] - out[1][1])
+        n = (out[2] - out[1] + out[3] - 1) // out[3]
+        if any(len(v) == 2 for v in ins):
+            return 60 + GATHER * n
+        if q == "t":
+            return (MATMUL if SCRATCH[ins[0][0]][2] == F else MATMUL / 4) * max(64, n)
+        if q == "g":
+            return 200 + 2 * n
+        return FIXED[q] + max(64, n * (2 if [SCRATCH[v[0]][0] for v in ins] == ["sbuf", "sbuf"] else 1))
+
+    def add(q, fn, ins, out, own=None, dma=False, after=(), soft=(), holds=None, takes=None):
         r, w = [], []
         for v in ins:
             r += span(v)
         if out is not None:
             w += span(out)[0:1]
             r += span(out)[1:]
-        ops.append({"q": q, "fn": fn, "r": r, "w": w, "own": own, "dma": dma, "after": list(after)})
+        holds = cycles(q, ins, out) if holds is None else holds
+        ops.append({"n": len(ops), "q": q, "fn": fn, "r": r, "w": w, "own": own, "dma": dma, "after": list(after),
+                    "soft": list(soft) + floor, "stay": False, "holds": holds, "takes": holds if takes is None else takes})
         return len(ops) - 1
 
-    ndma = [0]
+    loaded = [0]
 
     def load(q, out, src):
-        ndma[0] += 1
-        return add(q, lambda e: e.dma_start(ap(out), src), [], out, ("d%d" % (ndma[0] - 1), 16), True)
+        loaded[0] += 150 + (out[2] - out[1]) * (out[4][1] - out[4][0]) // LOAD
+        add(q, lambda e: e.dma_start(ap(out), src), [], out, ("d%d" % len(ops), 16), True, holds=1, takes=DMA + loaded[0])
 
-    def store(q, dst, src):
-        ndma[0] += 1
-        return add(q, lambda e: e.dma_start(dst, ap(src)), [src], None, ("d%d" % (ndma[0] - 1), 16), True)
+    def store(q, dst, src, sem):
+        return add(q, lambda e: e.dma_start(dst, ap(src)), [src], None, (sem, 16), True, holds=1, takes=DMA)
 
     def tt(out, a, b, op):
         add("v", lambda e: e.tensor_tensor(ap(out), ap(a), ap(b), op), [a, b], out)
@@ -228,307 +312,281 @@ def rank_program(g, core, T, topo):
     def mm(out, lhs, rhs, start, stop):
         add("t", lambda e: e.matmul(ap(out), ap(lhs), ap(rhs), start, stop), [lhs, rhs], out)
 
-    def select(out, pattern, base):
-        src = vw("ones", 0, out[2] - out[1], 1, out[4])
-        add("g", lambda e: e.affine_select(ap(out), ap(src), pattern, ALU.is_equal, 0.0, base, 1), [src], out)
+    def select(out, src, pattern, base, after=()):
+        return add("g", lambda e: e.affine_select(ap(out), ap(src), pattern, ALU.is_equal, 0.0, base, 1), [src], out, after=after)
+
+    def count(out, pattern, base):
+        return add("g", lambda e: e.iota(ap(out), pattern, base, 0, allow_small_or_imprecise_dtypes=True), [], out)
 
     def clamp(out, a):
         ts(out, a, -0.25, ALU.max, 0.25, ALU.min)
 
-    def st(p, lo, hi):
-        return vw("st%d" % p, lo, hi)
-
-    def pos(p):
-        return vw("posb", p * V, (p + 1) * V)
+    st = lambda p, lo, hi: vw("st%d" % p, lo, hi)
+    pos = lambda p: vw("posb", p * V, (p + 1) * V)
+    sm = lambda lo, hi: vw("sm", lo, hi)
+    p7 = lambda lo, hi: vw("p7", lo, hi)
+    ll = lambda lo, hi: vw("ll", lo, hi)
+    eye = vw("eye", 0, 128)
 
     def table_scatter(lo, hi, base):
-        ts((vw("tab", 0, V), vw("lu", lo, hi)), vw("rr", 512, 512 + 16 * (hi - lo)), 1.0, ALU.mult, float(base), ALU.add)
+        ts((vw("tab", 0, V), vw("lu", lo, hi)), vw("ramp", 0, 16 * (hi - lo)), 1.0, ALU.mult, float(base - B0), ALU.add)
 
-    def table_gather(q, at, lo, hi):
-        cp(q, vw("rr", at, at + 16 * (hi - lo)), (vw("tab", 0, V), vw("lu", lo, hi)))
+    def table_gather(at, lo, hi, q="v"):
+        cp(q, vw("r" + q, at, at + 16 * (hi - lo)), (vw("tab", 0, V), vw("lu", lo, hi)))
 
-    def to_lists(col, at, n):
+    def to_lists(col, at, n, q="v"):
         for a in range(16):
-            mm(vw("p7", col, col + n), vw("wm", 15 - a, 143 - a), vw("rr", at + a, at + 16 * n, 16), a == 0, a == 15)
+            mm(p7(col, col + n), vw("w" + q, 15 - a, 143 - a), vw("r" + q, at + a, at + 16 * n, 16), a == 0, a == 15)
 
-    def spread(out, block, src):
-        return (out, vw("sel", block * 128, block * 128 + 128, 1, 32), src)
+    OWN, JOINT = (0, 32), (32, 64)
 
-    def negative(lo):
-        a, src = vw("wn", lo, lo + 128, 1, 32), vw("wc", lo, lo + 128, 1, 32)
-        add("s", lambda e: e.activation(ap(a), ap(src), ACT.Identity, bias=-EPS, scale=-1.0), [src], a)
+    def spread(out, block, name, parts):
+        return (out, vw("sel", block * 128, block * 128 + 128, 1, parts), vw(name, 0, 128, 1, parts))
 
-    def product(lo):
-        tt(vw("kn", lo, lo + 128, 1, 32), vw("kc", lo, lo + 128, 1, 32), vw("wn", lo, lo + 128, 1, 32), ALU.mult)
-
-    def inverse(lo):
-        a, r = vw("wn", lo, lo + 128, 1, 32), vw("rn", lo, lo + 128, 1, 32)
-        add("v", lambda e: e.reciprocal(ap(r), ap(a)), [a], r)
-
-    def pieces(c, win, lst):
-        def at(name, p, h):
-            return vw(name, p * S, (p + 1) * S) if h is None else vw(name, p * S + h * 128, p * S + h * 128 + 128)
+    def pieces(c, win, lst, drawn=False):
+        def at(name, p, h, o=0):
+            o += p * S
+            return vw(name, o, o + S) if h is None else vw(name, o + h * 128, o + h * 128 + 128)
 
         def ends(p, z, h):
             o = lst[1] + 16 * z
             return (win(p), vw(lst[0], o, o + 16) if h is None else vw(lst[0], o + 8 * h, o + 8 * h + 8))
 
-        def mcol(p, h):
-            name, o = ("p5", p * S) if p < 2 else ("p6", 0)
-            return vw(name, o, o + S) if h is None else vw(name, o + h * 128, o + h * 128 + 128)
-
-        def to(p, z, h):
-            o = (A0, B0)[c] + z * S
-            return st(p, o, o + S) if h is None else st(p, o + h * 128, o + h * 128 + 128)
-
+        mcol = lambda p, h: at("p5", p, h) if p < 2 else at("p6", 0, h)
+        to = lambda p, z, h: at("st%d" % p, 0, h, (A0, B0)[c] + z * S)
         acc = lambda h: vw("p%d" % (2 + h), 0, 128)
-        f = {}
-        f["Z"] = lambda p, h=None: cp("s", at("zz", p, h), ends(p, 1, h))
-        f["Y"] = lambda p, h=None: cp("v", at("zz", p, h), ends(p, 1, h))
-        f["X"] = lambda p, h=None: cp("s", at("xx", p, h), ends(p, 0, h))
-        f["d"] = lambda p, h=None: tt(at("dd", p, h), ends(p, 0, h), at("zz", p, h), ALU.subtract)
-        f["q"] = lambda p, h=None: square(at("sq", p, h), at("dd", p, h))
-        f["r"] = lambda h: mm(*spread(acc(h), 2 * c + h, vw("rn", 0, 128, 1, 32)), True, False)
-        f["a"] = lambda p, h: mm(acc(h), vw("eye", 0, 128), at("sq", p, h), False, p == 2)
-        f["u"] = lambda h: tt(vw("uu", h * 128, h * 128 + 128), acc(h), vw("kwo", c * S + h * 128, c * S + h * 128 + 128), ALU.mult)
-        f["c"] = lambda h: clamp(vw("p4", h * 128, h * 128 + 128), vw("uu", h * 128, h * 128 + 128))
-        f["m"] = lambda p, h: tt(mcol(p, h), vw("p4", h * 128, h * 128 + 128), at("dd", p, h), ALU.mult)
-        f["x"] = lambda p, h=None: tt(to(p, 0, h), at("xx", p, h), mcol(p, h), ALU.add)
-        f["z"] = lambda p, h=None: tt(to(p, 1, h), at("zz", p, h), mcol(p, h), ALU.subtract)
-        return f
+        xx, zz, cc = ("xb", "zb", "cc") if drawn else ("xx", "zz", "p4")
+        diff = lambda p, h: at("dd", p, h) if not drawn else at("p1", p, h) if p < 2 else at("p0", 0, h)
+
+        def d(p, h=None):
+            if drawn:
+                mm(diff(p, h), vw("eyeb", 0, 128), at(xx, p, h), True, False)
+                mm(diff(p, h), vw("eyeb", 128, 256), at(zz, p, h), False, True)
+            else:
+                tt(diff(p, h), ends(p, 0, h), at(zz, p, h), ALU.subtract)
+        return {
+            "Z": lambda p, h=None: cp("s", at(zz, p, h), ends(p, 1, h)),
+            "Y": lambda p, h=None: cp("v", at(zz, p, h), ends(p, 1, h)),
+            "X": lambda p, h=None: cp("s", at(xx, p, h), ends(p, 0, h)),
+            "W": lambda p, h=None: cp("v", at(xx, p, h), ends(p, 0, h)),
+            "d": d,
+            "q": lambda p, h=None: square(at("sq", p, h), diff(p, h)),
+            "r": lambda h: mm(*spread(acc(h), 2 * c + h, "rn", OWN), not drawn, False),
+            "a": lambda p, h: mm(acc(h), eye, at("sq", p, h), drawn and p == 0, False),
+            "e": lambda p, h: mm(acc(h), eye, at("sq", p, h), False, True),
+            "A": lambda h: tt(at("p4", 1, h), acc(h), at("sq", 2, h), ALU.add),
+            "U": lambda h: tt(at("uu", 0, h), at("p4", 1, h), at("kwo", c, h), ALU.mult),
+            "u": lambda h: tt(at("uu", 0, h), acc(h), at("kwo", c, h), ALU.mult),
+            "c": lambda h: clamp(at(cc, 0, h), at("uu", 0, h)),
+            "m": lambda p, h: tt(mcol(p, h), at(cc, 0, h), diff(p, h), ALU.mult),
+            "x": lambda p, h=None: tt(to(p, 0, h), at(xx, p, h), mcol(p, h), ALU.add),
+            "z": lambda p, h=None: tt(to(p, 1, h), at(zz, p, h), mcol(p, h), ALU.subtract),
+        }
 
     def run(f, text, hooks=None):
         for w in text.split():
+            if w == ".":
+                if small:
+                    small.pop(0)()
+                    ops[-1]["stay"] = True
+                continue
             if w[0] == "@":
                 hooks[w[1:]]()
                 continue
             f[w[0]](*[int(ch) if ch.isdigit() else "ab".index(ch) for ch in w[1:]])
 
-    def border(q, t, slot, p):
-        o = t * 1152 + slot * 384 + p * 128
-        cp(q, vw("sb", o, o + 128), (st(p, J0, WIN), vw("ll", 32 + 8 * slot, 40 + 8 * slot)))
+    def into(f, words):
+        return {"n%d" % p: (lambda text: lambda: run(f, text))(words[p]) for p in range(3)}
 
     sent = [0]
 
-    def exchange(t):
-        dcore = T.cores[part[0]]
-        off = topo.engines(core, dcore)
-
-        def relayed(slot):
-            src = vw("sb", t * 1152 + slot * 384, t * 1152 + slot * 384 + 384)
-            masks = first_hop(topo, core, dcore, relays[slot][0], slot, t)
-
-            def fn(e):
-                trs = []
-                for h in (0, 1):
-                    rid, pid = topo.addr(relays[slot][h], core)
-                    o = src[1] + h * 192
-                    trs.append(RemoteDMATransfer(dst_ids=[DstId(rid=rid, pnc=pid)], dma_engine_mask=bits(masks[h]),
-                                                 remote_sem=T.sem["rin%d" % t], src=T.sb[:, o:o + 192],
-                                                 dst=T.rl[:, t * 192:(t + 1) * 192]))
-                return e.remote_dma_fused(trs, local_sem=T.sem.sent)
-            add("g", fn, [src], None, ("sent", 0))
-            sent[0] += len(masks[0]) + len(masks[1])
-
-        def direct():
-            src = vw("sb", t * 1152, t * 1152 + 384)
-            rid, pid = topo.addr(dcore, core)
-            add("g", lambda e: e.remote_dma(T.ld[:, src[1]:src[2]], ap(src), T.sem["ar%d" % (3 * t)], T.sem.sent,
-                                            pid, rid, bits(off)), [src], None, ("sent", 0))
-            sent[0] += len(off)
-
-        relayed(1)
-        if t < SWEEPS - 1:
-            direct()
-            relayed(2)
-        else:
-            relayed(2)
-            direct()
-        for slot in range(3):
+    def send(t, last):
+        k = [slots[-1] for slots in PLAN[t]].index(last) if last in [slots[-1] for slots in PLAN[t]] else None
+        if k is None:
+            return
+        plan = calls(T, topo, rank, t)
+        srcs, trs = [], []
+        for slot, lo, hi, to, engines in plan[k]:
             o = t * 1152 + slot * 384
-            n = len(off) if slot == 0 else sum(len(topo.engines(c, T.cores[part[slot]])) for c in relays[slot])
-            add(None, None, [], vw("ld", o, o + 384), ("ar%d" % (3 * t + slot), n))
+            rid, pid = topo.addr(to, core)
+            srcs.append(vw("sb", o + lo, o + hi))
+            dst, sem = (T.ld[:, o + lo:o + hi], "ar%d" % (3 * t)) if slot == 0 else (
+                T.rl[:, t * 384 + lo:t * 384 + hi], "rin%d" % t)
+            trs.append(RemoteDMATransfer(dst_ids=[DstId(rid=rid, pnc=pid)], dma_engine_mask=bits(engines),
+                                         remote_sem=T.sem[sem], src=ap(srcs[-1]), dst=dst))
+            sent[0] += len(engines)
+        call = add("g", lambda e: e.remote_dma_fused(trs, local_sem=T.sem.sent), srcs, None, ("sent", 0), holds=ISSUE)
+        for name in PLAN[t][k]:
+            n = sum(len(topo.engines(to, T.cores[part[name]]) if name else engines)
+                    for slot, lo, hi, to, engines in plan[k] if slot == name)
+            add(None, None, [], vw("ld", t * 1152 + name * 384, t * 1152 + name * 384 + 384), ("ar%d" % (3 * t + name), n),
+                soft=[call], holds=WRITE[name] + (COLD if t == 0 else 0))
+        if k == 0:
+            floor[:] = [call]
 
-    xbank = ("p2", "p3", "p0")
+    def sends(t):
+        def border(q, slot, p):
+            o = t * 1152 + slot * 384 + p * 128
+            cp(q, vw("sb", o, o + 128), (st(p, J0, WIN), ll(32 + 8 * slot, 40 + 8 * slot)))
+        return into({"G": lambda slot, p: border("s", slot, p), "H": lambda slot, p: border("v", slot, p),
+                     "s": lambda slot: send(t, slot)}, SENDS[t])
+
+    xbank = ("p3", "p0", "p1")
 
     def own_side(t, slot):
         o = t * 1152 + slot * 384
         cp("s", vw(xbank[slot], 0, 384), vw("sb", o, o + 384))
 
-    def coefficient(sqv, r, kw):
-        return [lambda: tt(vw("p4", 0, 128), r, sqv(0), ALU.add),
-                lambda: tt(vw("p4", 128, 256), vw("p4", 0, 128), sqv(1), ALU.add),
-                lambda: tt(vw("p4", 256, 384), vw("p4", 128, 256), sqv(2), ALU.add),
-                lambda: tt(vw("uu", 0, 128), vw("p4", 256, 384), kw, ALU.mult),
-                lambda: clamp(vw("p4", 384, 512), vw("uu", 0, 128))]
-
     def joint(t, between, done):
         col = lambda name, p, b: vw(name, b + p * 128, b + p * 128 + 128)
+        acc = lambda slot: vw(ACC[slot], 256, 384)
 
-        def moves(slot):
-            o = t * 1152 + slot * 384
-            m = lambda p: lambda: tt(col("p5", p, 0), vw("p4", 384, 512), col("dj", p, slot * 384), ALU.mult)
+        def differ(slot, p):
+            tt(col("dj", p, slot * 384), col(xbank[slot], p, 0), col("ld", p, t * 1152 + slot * 384), ALU.subtract)
+            square(col("sj", p, slot * 384), col("dj", p, slot * 384))
 
-            def x(p):
-                def fn():
-                    tt(st(p, J0 + slot * 128, J0 + slot * 128 + 128), col("sb", p, o), col("p5", p, 0), ALU.add)
-                    if slot == 2:
-                        done(p)
-                return fn
-            return [m(0), m(1), x(0), m(2), x(1), x(2)]
-
-        for slot in range(3):
-            o = t * 1152 + slot * 384
+        def x(slot, p):
+            tt(st(p, J0 + slot * 128, J0 + slot * 128 + 128), col("sb", p, t * 1152 + slot * 384), col("p4", p, 0), ALU.add)
             if slot == 2:
-                between()
-            for p in range(3):
-                tt(col("dj", p, slot * 384), col(xbank[slot], p, 0), col("ld", p, o), ALU.subtract)
-                square(col("sj", p, slot * 384), col("dj", p, slot * 384))
-            chain = coefficient(lambda p: col("sj", p, slot * 384), col("p1", slot, 0), col("kwj", slot, 8))
-            other = moves(slot - 1) if slot else []
-            for k in range(6):
-                if other:
-                    other[k]()
-                if k:
-                    chain[k - 1]()
-        for fn in moves(2):
-            fn()
+                done(p)
 
-    sm = lambda lo, hi: vw("sm", lo, hi)
-    p7 = lambda lo, hi: vw("p7", lo, hi)
-    ll = lambda lo, hi: vw("ll", lo, hi)
+        run({"d": differ, "x": x,
+             "r": lambda slot: mm(*spread(acc(slot), part[slot], "rn", JOINT), True, False),
+             "R": lambda slot: mm(*spread(acc(slot), part[slot], "rn", JOINT), True, True),
+             "a": lambda slot, p: mm(acc(slot), eye, col("sj", p, slot * 384), False, False),
+             "e": lambda slot, p: mm(acc(slot), eye, col("sj", p, slot * 384), False, True),
+             "s": lambda slot, p: tt(col("p5", p, 0), acc(slot), col("sj", p, slot * 384), ALU.add),
+             "S": lambda slot, p: tt(col("p5", p, 0), col("p5", p - 1, 0), col("sj", p, slot * 384), ALU.add),
+             "u": lambda slot: tt(vw("uu", 0, 128), acc(slot), col("kwj", slot, 8), ALU.mult),
+             "U": lambda slot: tt(vw("uu", 0, 128), col("p5", 2, 0), col("kwj", slot, 8), ALU.mult),
+             "c": lambda slot: clamp(vw("p4", 384, 512), vw("uu", 0, 128)),
+             "m": lambda slot, p: tt(col("p4", p, 0), vw("p4", 384, 512), col("dj", p, slot * 384), ALU.mult)},
+            JOINTS, {"": between})
 
+    both, one = (0, 64), (0, 1)
     load("y", vw("li", 0, 64), T.ends[:, :])
-    load("s", vw("wc", 0, 128, 1, 32), T.inv[:, :])
-    load("s", vw("kc", 0, 128, 1, 32), T.stiff[:, :])
+    load("s", vw("wc", 0, 128, 1, OWN), T.inv[:, :])
+    load("y", vw("wc", 0, 128, 1, JOINT), T.jinv[:, :])
+    load("s", vw("kc", 0, 128, 1, OWN), T.stiff[:, :])
+    load("s", vw("kc", 0, 128, 1, JOINT), T.jstiff[:, :])
     for p in range(3):
         load("y", pos(p), T.pos[:, p * V:(p + 1) * V])
-    load("s", vw("li", 72, 104), T.bord[:, :])
-    load("s", vw("li", 64, 72), T.watch[:, :])
-    load("y", vw("wc", 128, 256, 1, 32), T.jinv[:, :])
-    load("y", vw("kc", 128, 256, 1, 32), T.jstiff[:, :])
-    fill(vw("ones", 0, 144), 1.0)
-    ramp = vw("rr", 512, 1024)
-    add("g", lambda e: e.iota(ap(ramp), [[1, 512]], 0, 0, allow_small_or_imprecise_dtypes=True), [], ramp)
-    fill(vw("tab", 0, V), 0.0)
+    for s in range(3):
+        load("y", vw("li", 72 + 8 * s, 80 + 8 * s), T.bord[:, 8 * part[s]:8 * part[s] + 8])
+    load("y", vw("li", 64, 72), T.watch[:, :])
+    fill(vw("ones", 0, 128), 1.0)
+    count(vw("ramp", 0, 512), [[1, 512]], B0)
+    fill(vw("oneb", 0, 144), 1.0)
+    fill(vw("oneb", 144, 272), -1.0)
+    fill(vw("tab", 0, ZERO), 0.0)
+    fill(vw("tab", ZERO, V - ZERO), 0.0)
+    cp("s", vw("tab", V - ZERO, V), vw("tab", 0, ZERO))
     for a in range(4):
-        select(vw("sel", a * 128, a * 128 + 128, 1, 32), [[-4, 8], [0, 16]], -a)
-    select(vw("wm", 0, 144), [[-16, 9], [256, 16]], -15 * 256)
-    select(vw("eye", 0, 128), [[-1, 128]], 0)
+        select(vw("sel", a * 128, a * 128 + 128, 1, OWN), vw("ones", 0, 128, 1, OWN), [[-4, 8], [0, 16]], -a)
+    for k in (0, 1):
+        select(vw("eyeb", k * 128, k * 128 + 128), vw("oneb", k * 144, k * 144 + 128), [[-1, 128]], 0)
+    select(vw("wv", 0, 144), vw("oneb", 0, 144), [[-16, 9], [256, 16]], -15 * 256)
+    count(vw("row", 0, 128, 1, one), [[0, 8], [1, 16]], 0)
+    count(vw("row", 128, 160, 1, one), [[16, 32]], B0)
+    last = select(eye, vw("ones", 0, 128), [[-1, 128]], 0)
+    for a in range(4):
+        select(vw("sel", a * 128, a * 128 + 128, 1, JOINT), vw("ones", 0, 128, 1, JOINT), [[-4, 8], [0, 16]], -a, [last])
     cp("v", vw("lu", 0, 64), vw("li", 0, 64))
-    negative(0)
-    product(0)
-    table_scatter(0, 32, A0)
-    for a in range(4):
-        mm(*spread(vw("p0", a * 128, a * 128 + 128), a, vw("kn", 0, 128, 1, 32)), True, True)
-    cp("s", vw("kwo", 0, 512), vw("p0", 0, 512))
-    table_gather("s", 0, 32, 64)
-    to_lists(0, 0, 64)
-    inverse(0)
+    wn, wc, rn = (vw(n, 0, 128, 1, both) for n in ("wn", "wc", "rn"))
+    add("s", lambda e: e.activation(ap(wn), ap(wc), ACT.Identity, bias=-EPS, scale=-1.0), [wc], wn)
+
+    def product():
+        tt(vw("kn", 0, 128, 1, both), vw("kc", 0, 128, 1, both), wn, ALU.mult)
+        for a in range(4):
+            mm(*spread(vw("p0", a * 128, a * 128 + 128), a, "kn", OWN), True, True)
 
     def first_list():
-        ts(sm(0, 32), p7(32, 64), float(B0), ALU.add)
-        ts(sm(64, 88), p7(32, 56), float(J0), ALU.add)
-        tt(sm(32, 64), p7(0, 32), sm(0, 32), ALU.max)
-        cp("v", sm(88, 96), p7(32, 40))
-        ts(ll(0, 32), sm(32, 64), float(B0), ALU.subtract)
+        to_lists(0, 0, 32)
+        mm(p7(32, 64), vw("row", 0, 128, 1, one), vw("oneb", 0, 32, 1, one), True, False)
+        mm(p7(32, 64), vw("oneb", 0, 128, 1, one), vw("row", 128, 160, 1, one), False, True)
 
-    def other_lists():
-        cp("v", vw("lu", 64, 72), vw("li", 64, 72))
-        for s in range(3):
-            cp("v", vw("lu", 72 + 8 * s, 80 + 8 * s), vw("li", 72 + 8 * part[s], 80 + 8 * part[s]))
+    def first_places():
+        cp("s", sm(0, 64), p7(0, 64))
+        small.extend([lambda: tt(sm(64, 96), sm(0, 32), sm(32, 64), ALU.max),
+                      lambda: ts(ll(0, 32), sm(64, 96), float(B0), ALU.subtract),
+                      lambda: ts(sm(96, 120), sm(32, 56), float(J0 - B0), ALU.add)])
 
     def border_list():
-        tt(sm(96, 120), p7(72, 96), sm(64, 88), ALU.max)
-        ts(ll(32, 56), sm(96, 120), float(J0), ALU.subtract)
+        small.extend([lambda: tt(sm(120, 144), p7(72, 96), sm(96, 120), ALU.max),
+                      lambda: ts(ll(32, 56), sm(120, 144), float(J0), ALU.subtract)])
 
     def later_lists():
-        tt(sm(160, 192), p7(128, 160), sm(120, 152), ALU.max)
-        ts(ll(56, 88), p7(96, 128), float(J0), ALU.subtract)
-        ts(ll(88, 120), sm(160, 192), float(J0), ALU.subtract)
+        small.extend([lambda: ts(ll(56, 88), p7(96, 128), float(J0), ALU.subtract),
+                      lambda: tt(sm(144, 176), p7(128, 160), sm(0, 32), ALU.max),
+                      lambda: ts(ll(88, 120), sm(144, 176), float(J0), ALU.subtract)])
 
     def start(p, region, n, col, q="s"):
         cp(q, st(p, region, region + 16 * n), (pos(p), vw("lu", col, col + n)))
 
     hooks = {
-        "B0": lambda: start(0, B0, 32, 32), "B1": lambda: start(1, B0, 32, 32), "B2": lambda: start(2, B0, 32, 32, "v"),
-        "J0": lambda: start(0, J0, 24, 72), "J1": lambda: start(1, J0, 24, 72), "J2": lambda: start(2, J0, 24, 72),
-        "sB": lambda: table_scatter(32, 64, B0), "l1": first_list, "ol": other_lists,
-        "g2": lambda: table_gather("s", 1024, 64, 96), "t2": lambda: to_lists(64, 1024, 32), "bl": border_list,
+        "sA": lambda: table_scatter(0, 32, A0), "sB": lambda: table_scatter(32, 64, B0),
+        "g1": lambda: table_gather(0, 32, 64), "g2": lambda: table_gather(512, 64, 96),
+        "G2": lambda: table_gather(512, 64, 96, "s"), "T2": lambda: to_lists(64, 512, 32, "s"),
+        "+": lambda: floor.append(len(ops) - 1), "-": floor.clear,
+        "g3": lambda: table_gather(640, 72, 96), "t3": lambda: to_lists(72, 640, 24),
+        "t1": first_list, "t2": lambda: to_lists(64, 512, 32), "l1": first_places, "bl": border_list,
+        "kn": product, "kw": lambda: cp("s", vw("kwo", 0, 512), vw("p0", 0, 512)),
+        "rn": lambda: add("v", lambda e: e.reciprocal(ap(rn), ap(wn)), [wn], rn, holds=200 + 6 * 128),
+        "ol": lambda: cp("v", vw("lu", 64, 96), vw("li", 64, 96)),
     }
+    for p in range(3):
+        for q in "sv":
+            hooks["BC"[q == "v"] + str(p)] = (lambda p, q: lambda: start(p, B0, 32, 32, q))(p, q)
+            hooks["JK"[q == "v"] + str(p)] = (lambda p, q: lambda: start(p, J0, 24, 72, q))(p, q)
 
-    def into(f):
-        return {k: (lambda text: lambda: run(f, text))(v) for k, v in PRE.items()}
-
-    def send_hooks(t):
-        def some(text):
-            return lambda: [border(w[0], t, int(w[1]), int(w[2])) for w in text.split()]
-        return {"n%d" % p: some(SENDS[t][p]) for p in range(3)}
-
-    TAIL = "ua ca m0a m1a m2a ub x0a cb z0a m0b m1b x0b z0b @n0 m2b x1 z1 @n1 x2 z2 @n2"
-    PRE = {"n0": "Z0 X0", "n1": "Z1", "n2": "Z2a"}
-    HEAD = "ra rb d0a q0a d1a q1a Z2b a0a d2a q2a a1a a2a d0b q0b d1b q1b a0b d2b q2b a1b a2b X1 X2 "
-    JPRE = ("Z0a", "Z1a", "Z2a")
-    JHEAD = "ra rb d0a q0a Y0b d1a q1a a0a d2a Z1b q2a Z2b a1a a2a d0b q0b d1b q1b a0b d2b q2b a1b a2b X0 X1 X2 "
-    FIRST = ("Z0 d0 X0 q0 @sB Z1 @B0 X1 d1 ra rb a0a a0b Z2a d2a Z2b q1 q2a d2b q2b a1a a2a a1b a2b "
-             "@ol @l1 X2 @B1 @B2 @g2 @t2 @J0 ")
-    SECOND = HEAD + "@J1 @J2 @bl "
-    SENDS = (("s10", "s11 s00 s01", "v12 v02 s20 s21 v22"),
-             ("s10 s00 s20", "s11 s01 s21", "v12 s02 v22"),
-             ("s10 s20 s00", "s11 s21", "v12 v22 s01 s02"))
-
-    c0 = pieces(0, pos, ("lu", 0))
+    c0 = pieces(0, pos, ("lu", 0), True)
     c1 = pieces(1, lambda p: st(p, B0, WIN), ("ll", 0))
-    run(c0, FIRST + TAIL, dict(hooks, **into(c1)))
-    run(c1, SECOND + TAIL, dict(hooks, **send_hooks(0)))
-    c0 = pieces(0, lambda p: st(p, J0, WIN), ("ll", 56))
-    c1 = pieces(1, lambda p: st(p, J0, WIN), ("ll", 88))
-
+    run(c0, FIRST + FTAIL, dict(hooks, **into(c1, PRE)))
     for t in range(SWEEPS):
         if t > 0:
-            run(c0, JHEAD + TAIL, into(c1))
-            run(c1, HEAD + TAIL, send_hooks(t))
-        exchange(t)
+            run(c0, JHEAD + TAIL, into(c1, PRE))
+        run(c1, HEAD + (SECOND + " " if t == 0 else "") + TAIL, dict(hooks, **sends(t)))
         if t == SWEEPS - 1:
             break
         if t == 0:
-            negative(128)
-            cp("v", sm(120, 152), p7(0, 32))
             fill(vw("kwj", 0, 8), 0.0)
-            fill(vw("rj", 0, 8), 0.0)
-            product(128)
-            inverse(128)
+            if "@g3" in FIRST + SECOND:
+                table_gather(512, 64, 72)
+                to_lists(64, 512, 8)
             for s in range(3):
-                mm(*spread(vw("p6", s * 128, s * 128 + 128), part[s], vw("kn", 128, 256, 1, 32)), True, True)
-            for s in range(3):
-                mm(*spread(vw("p1", s * 128, s * 128 + 128), part[s], vw("rn", 128, 256, 1, 32)), True, True)
+                mm(*spread(vw("p0", s * 128, s * 128 + 128), part[s], "kn", JOINT), True, True)
             table_scatter(72, 96, J0)
         own_side(t, 0)
+        if t == 0:
+            table_gather(1024, 0, 72)
+            cp("s", vw("kwj", 8, 392), vw("p0", 0, 384))
+            to_lists(96, 1024, 72)
         own_side(t, 1)
-        if t == 0:
-            cp("s", vw("kwj", 8, 392), vw("p6", 0, 384))
         own_side(t, 2)
-        if t == 0:
-            table_gather("v", 1536, 0, 32)
-            table_gather("s", 2048, 32, 72)
-            to_lists(96, 1536, 72)
-        else:
-            cp("s", vw("rj", 8, 392), vw("p1", 0, 384))
-            for p in range(3):
-                start(p, W0, 8, 64)
-            tt(sm(0, 8), p7(64, 72), sm(88, 96), ALU.max)
-            ts(sm(8, 16), p7(160, 168), float(B0), ALU.is_lt)
-            tt(sm(16, 24), p7(160, 168), sm(0, 8), ALU.max)
-            tt(sm(24, 32), p7(160, 168), sm(8, 16), ALU.mult)
-            cp("v", ll(120, 128), sm(16, 24))
-            ts(ll(128, 136), sm(24, 32), float(J0 - 8), ALU.subtract, 0.0, ALU.max)
-            ts(sm(32, 40), sm(24, 32), float(J0), ALU.subtract, 0.0, ALU.max)
-            ts(sm(40, 48), sm(24, 32), float(J0 + 128), ALU.is_ge, 256.0, ALU.mult)
-            ts(sm(48, 56), sm(24, 32), float(J0 + 256), ALU.is_ge, 256.0, ALU.mult)
-            tt(sm(56, 64), sm(32, 40), sm(40, 48), ALU.add)
-            tt(sm(152, 160), sm(56, 64), sm(48, 56), ALU.add)
-            cp("v", ll(136, 144), sm(152, 160))
+        c0 = pieces(0, lambda p: st(p, J0, WIN), ("ll", 56))
+        c1 = pieces(1, lambda p: st(p, J0, WIN), ("ll", 88))
         joint(t, later_lists if t == 0 else (lambda: None), lambda p: run(c0, JPRE[p]))
+
+    fill(vw("rj", 0, 8), 0.0)
+    for s in range(3):
+        mm(*spread(vw("p1", s * 128, s * 128 + 128), part[s], "rn", JOINT), True, True)
+    cp("s", vw("rj", 8, 392), vw("p1", 0, 384))
+    for p in range(3):
+        start(p, W0, 8, 64)
+    late = p7(160, 168)
+    ts(sm(64, 72), sm(32, 40), float(W0 - B0), ALU.add)
+    ts(sm(72, 80), late, float(B0), ALU.is_lt)
+    tt(sm(80, 88), p7(64, 72), sm(64, 72), ALU.max)
+    tt(sm(96, 104), late, sm(72, 80), ALU.mult)
+    tt(sm(88, 96), late, sm(80, 88), ALU.max)
+    ts(ll(128, 136), sm(96, 104), float(J0 - 8), ALU.subtract, 0.0, ALU.max)
+    cp("v", ll(120, 128), sm(88, 96))
+    ts(sm(104, 112), sm(96, 104), float(J0), ALU.subtract, 0.0, ALU.max)
+    ts(sm(112, 120), sm(96, 104), float(J0 + 128), ALU.is_ge, 256.0, ALU.mult)
+    ts(sm(120, 128), sm(96, 104), float(J0 + 256), ALU.is_ge, 256.0, ALU.mult)
+    tt(sm(128, 136), sm(104, 112), sm(112, 120), ALU.add)
+    tt(sm(136, 144), sm(128, 136), sm(120, 128), ALU.add)
+    cp("v", ll(136, 144), sm(136, 144))
 
     o = (SWEEPS - 1) * 1152
     col = lambda name, p: vw(name, p * 128, p * 128 + 128)
@@ -540,13 +598,17 @@ def rank_program(g, core, T, topo):
     for p in range(3):
         tt(col("dj", p), (vw("ld", o + p * 128, o + p * 128 + 896), ll(136, 144)), col("xx", p), ALU.subtract)
         square(col("sj", p), col("dj", p))
-    for fn in coefficient(lambda p: col("sj", p), vw("p2", 0, 128), vw("kww", 0, 128)):
-        fn()
+    tt(vw("p4", 0, 128), vw("p2", 0, 128), col("sj", 0), ALU.add)
+    tt(vw("p4", 128, 256), vw("p4", 0, 128), col("sj", 1), ALU.add)
+    tt(vw("p4", 256, 384), vw("p4", 128, 256), col("sj", 2), ALU.add)
+    tt(vw("uu", 0, 128), vw("p4", 256, 384), vw("kww", 0, 128), ALU.mult)
+    clamp(vw("p4", 384, 512), vw("uu", 0, 128))
     m = lambda p: tt(col("p5", p), vw("p4", 384, 512), col("dj", p), ALU.mult)
     x = lambda p: tt(col("yb", p), col("xx", p), col("p5", p), ALU.subtract)
-    m(0); m(1); x(0); m(2); x(1); x(2)
-    stored = store("y", T.y[:, :], vw("yb", 0, 384))
-    add("y", None, [], None, after=[stored])
-    total = add(None, None, [], None, ("sent", sent[0]))
-    add("g", None, [], None, after=[total])
-    emit(g, T, ops)
+    m(0); m(1); x(0); x(1); m(2); x(2)
+    first = store("y", T.y[:, 0:256], vw("yb", 0, 256), "d12")
+    stored = store("s", T.y[:, 256:384], vw("yb", 256, 384), "d13")
+    add("y", None, [], None, after=[first, stored], holds=1)
+    total = add(None, None, [], None, ("sent", sent[0]), soft=[stored], holds=1)
+    add("g", None, [], None, after=[total], holds=1)
+    emit(g, T, arrange(ops))

@@ -3,6 +3,7 @@ from concourse.mybir import AluOpType as ALU, ActivationFunctionType as ACT
 
 V, S = 2048, 256
 W0, J0, B0, A0, WIN = 0, 128, 512, 1024, 1536
+MW = 1032
 EPS = 1e-22
 SWEEPS = 3
 F = "float32"
@@ -13,12 +14,16 @@ SCRATCH = {
     "posb": ("sbuf", [128, 3 * V], "bfloat16"),
     "li": ("sbuf", [128, 96], "int32"),
     "lu": ("sbuf", [128, 96], "uint16"),
-    "ll": ("sbuf", [128, 144], "uint16"),
-    "sm": ("sbuf", [128, 224], F),
+    "ll": ("sbuf", [128, 200], "uint16"),
+    "mw": ("sbuf", [128, 3 * MW], F),
+    "aw": ("sbuf", [128, MW], F),
+    "pb": ("sbuf", [128, 1152], F),
+    "sm": ("sbuf", [128, 368], F),
     "tab": ("sbuf", [128, V], F),
     "ramp": ("sbuf", [128, 512], F),
     "rv": ("sbuf", [128, 2176], "float16"),
     "ones": ("sbuf", [128, 128], F),
+    "rs": ("sbuf", [128, 1024], "bfloat16"),
     "oneb": ("sbuf", [128, 272], "bfloat16"),
     "eyeb": ("sbuf", [128, 256], "bfloat16"),
     "wv": ("sbuf", [128, 144], "bfloat16"),
@@ -51,21 +56,22 @@ SCRATCH = {
     "yb": ("sbuf", [128, 384], F),
     "sb": ("sbuf", [128, SWEEPS * 1152], F),
     "ld": ("sbuf", [128, SWEEPS * 1152], F),
-    "rl": ("sbuf", [128, SWEEPS * 384], F),
 }
 for _k in range(8):
     SCRATCH["p%d" % _k] = ("psum", [128, 512], F)
 
-SEMAPHORES = (["qv", "qs", "qt", "qg", "sent"] + ["d%d" % k for k in range(14)]
-              + ["ar%d" % k for k in range(3 * SWEEPS)] + ["rin%d" % k for k in range(2 * SWEEPS)])
+SEMAPHORES = (["qv", "qs", "qt", "qg", "sent"] + ["d%d" % k for k in range(15)]
+              + ["ar%d" % k for k in range(3 * SWEEPS)] + ["rin%d" % k for k in range(10 * SWEEPS)])
 
-FIRST = ("@kn @sA Z0 X0 d0 @g1 @rn @sB q0 Z1 X1 d1 @kw X2 Z2 q1 d2a d2b q2a q2b a0a ra e1a a0b rb a1b e2b @t1 "
+FIRST = ("@kn @sA Z0 X0 d0 @g1 @rn @sB q0 a0a a0b Z1 X1 d1 @kw X2 Z2 q1 d2a d2b @+ q2a q2b ra e1a rb a1b e2b @t1 @- "
          "@ol @g3 @l1 @B0 @B1 @B2 @J0 @J1 @t3 ")
 SECOND = "@J2 @bl"
-HEAD = "ra rb Z2b d0a q0a d1a q1a a0a d2a q2a e1a d0b q0b d1b q1b a0b d2b q2b a1b e2b "
-JHEAD = "ra rb Y0b d0a Z1b q0a d1a q1a a0a d2a q2a e1a d0b q0b d1b q1b a0b Y2b d2b q2b a1b e2b "
-FTAIL = "Aa . Ua . ca . m0a m1a m2a ub x0a cb z0a m0b m1b x0b z0b @n0 m2b x1 z1 @n1 x2 z2 @n2"
+HEAD = "ra rb d0a q0a d1a q1a a0a Z2b d2a q2a e1a d0b q0b d1b q1b a0b a1b d2b q2b e2b "
+JHEAD = "ra rb Y0b d0a Z1b q0a d1a q1a a0a d2a Z2b q2a e1a d0b q0b d1b q1b a0b a1b d2b q2b e2b "
+FTAIL = "Ba0 Ba1 Va0 Va1 Ca0 Ca1 . m0a . m1a . m2a ub . x0a cb . z0a m0b . m1b x0b z0b @n0 m2b x1 z1 @n1 x2 z2 @n2"
 TAIL = "X0 X1 X2 " + FTAIL
+WN = "v"
+STORES = (("y", 0, 128), ("s", 128, 384))
 PRE = ("Z0", "Z1", "Z2a")
 JPRE = ("Z0a", "Z1a", "Z2a")
 CUT = 72
@@ -73,11 +79,24 @@ ZERO = 640
 SENDS = (("G10 G00 G20", "G11 G01 G21", "H12 s1 H02 s0 H22 s2"),
          ("G10 G00 G20", "G11 G01 G21", "H12 s1 H02 s0 H22 s2"),
          ("G10 G20 G00", "G11 G21 G01", "H12 s1 H22 s2 H02 s0"))
-PLAN = (((1,), (0,), (2,)), ((1,), (0,), (2,)), ((1,), (2,), (0,)))
-REST = ((2,), (2,), ())
-JOINTS = ("R0 d00 d01 d02 s00 S01 S02 @ U0 . c0 r1 d10 a10 d11 a11 d12 e12 m00 m01 x00 m02 x01 x02 "
-          "r2 d20 a20 d21 a21 d22 e22 u1 . c1 . m10 m11 x10 m12 x11 x12 u2 c2 m20 m21 x20 m22 x21 x22")
-ACC = ("p2", "p6", "p2")
+WORLD = 256
+ROUTE = ("1n:128:all 1a:256:all 0d:384:off 2a:192:rest1 2n:192:rest0",
+         "1a:256:all 0d:384:off 1n:128:rest 2n:192:rest0 2a:192:rest1",
+         "1n:128:all 1a:256:all 2a:256:all 2n:128:all 0d:384:off")
+JOINTS = ("R0 d00 d01 d02 !X2 s00 S01 B00 B01 @ V00 V01 C00 C01 @1 r1 d10 a10 d11 a11 d12 e12 !o2 !x2 m00 m01 x00 m02 x01 x02 "
+          "r2 d20 a20 d21 a21 d22 e22 @2 v10 v11 C10 C11 . m10 m11 x10 m12 x11 x12 v20 v21 C20 C21 m20 m21 x20 m22 x21 x22")
+JOINT0 = ("R0 d00 d01 d02 s00 S01 S02 @ U0 . c0 @1 R1 m00 m01 x00 m02 x01 x02 r2 d10 d11 d12 d20 a20 s10 d21 a21 S11 d22 e22 S12 "
+          "@2 U1 c1 m10 m11 x10 m12 x11 u2 x12 c2 m20 m21 x20 m22 x21 x22")
+PLAIN = (0,)
+STAY = (False, True)
+MOVES = (None,
+         "E012 E112 E001 Ba0 Ba1 Va0 Va1 Ca0 Ca1 M0a M1a M2a vb0 vb1 N0a Cb0 Cb1 N1a M0b N2a M1b N0b M2b N1b N2b "
+         "E101 b10 E201 b11 E212 b00 b01 b02 s0 E023 b12 s1 E123 E223 b20 b21 b22 s2",
+         "E012 E112 E212 Ba0 Ba1 Va0 Va1 Ca0 Ca1 M0a M1a M2a vb0 vb1 N0a Cb0 Cb1 N1a M0b N2a M1b N0b M2b N1b N2b "
+         "E023 b10 E123 b11 E223 b12 s1 E001 b20 E101 b21 E201 b22 s2 b00 b01 b02 s0")
+SHADE = "X0 P0 z0 x0 X1 P1 z1 x1 o0 P2 z2 o1"
+LOADS = "0 1 2 b w"
+BYPE = ((), ())
 
 
 def bits(engines):
@@ -98,45 +117,45 @@ def routes(T, topo, r):
         can = [c for c in topo.cores_of(me) if c != me and topo.may_write(c, T.cores[q])]
         near = [c for c in can if topo.die(c) == topo.die(me)]
         away = [c for c in can if topo.die(c) != topo.die(me)]
-        relays[1 + i] = (near[i], away[i])
+        mate = [c for c in range(WORLD) if topo.mates(c, T.cores[q]) and topo.may_write(c, T.cores[q]) and topo.die(c) == topo.die(me)]
+        relays[1 + i] = {"n": near[i], "a": away[i], "m": mate[i], "N": near[1 - i], "A": away[1 - i]}
+    free = [c for c in topo.cores_of(me) if c != me and not topo.may_write(c, T.cores[far[0]])]
+    relays[0] = {"d": T.cores[direct[0]], "a": [c for c in free if topo.die(c) != topo.die(me)][0],
+                 "n": [c for c in free if topo.die(c) == topo.die(me)][0]}
     return direct + far, relays
 
 
-def calls(T, topo, r, t):
+def pieces_of(T, topo, r, t):
     me = T.cores[r]
     part, relays = routes(T, topo, r)
-    direct = T.cores[part[0]]
-    every, off = topo.engines(me, relays[1][0]), topo.engines(me, direct)
+    every, off = topo.engines(me, relays[1]["n"]), topo.engines(me, T.cores[part[0]])
     rest = [e for e in every if e not in off]
-    out, gone = [], False
-    for slots in PLAN[t]:
-        trs = []
-        gone = gone or 0 in slots
-        for k, slot in enumerate(slots):
-            if slot == 0:
-                trs += [(0, 0, 384, direct, off)] if len(slots) == 1 else [(0, 0, 192, direct, off[0::2]), (0, 192, 384, direct, off[1::2])]
-            else:
-                use = rest if gone and (slot in REST[t] or 0 in slots) else every if len(slots) == 1 else (rest, off)[k]
-                trs += [(slot, 0, 192, relays[slot][1], use[1::2]), (slot, 192, 384, relays[slot][0], use[0::2])]
-        out.append(trs)
+    sets = {"all": every, "off": off, "rest": rest}
+    out = {}
+    for k, w in enumerate(ROUTE[t].split()):
+        head, n, name = w.split(":")
+        slot = int(head[0])
+        lo = out[slot][-1][1] if slot in out else 0
+        engines = sets[name[:-1]][int(name[-1])::2] if name[-1] in "01" else sets[name]
+        out.setdefault(slot, []).append((lo, lo + int(n), relays[slot][head[1]], engines, "rin%d" % (10 * t + k)))
     return out
 
 
 def relay_program(g, core, T, topo):
     for r, me in enumerate(T.cores):
-        if core not in topo.cores_of(me):
+        part, relays = routes(T, topo, r)
+        sent = 0
+        if not any(core in ways.values() for ways in relays.values()):
             continue
-        part, sent = routes(T, topo, r)[0], 0
         for t in range(SWEEPS):
-            for trs in calls(T, topo, r, t):
-                for slot, lo, hi, to, engines in trs:
-                    if to != core:
-                        continue
+            mine = [(x[4], slot) + x[:4] for slot, trs in pieces_of(T, topo, r, t).items() for x in trs if x[2] == core]
+            for _ in (0,):
+                for sem, slot, lo, hi, to, engines in sorted(mine):
                     dst = T.cores[part[slot]]
                     rid, pid = topo.addr(dst, core)
-                    g.wait_ge(T.sem["rin%d" % t], len(engines))
+                    g.wait_ge(T.sem[sem], len(engines))
                     o = t * 1152 + slot * 384
-                    g.remote_dma(T.ld[:, o + lo:o + hi], T.rl[:, t * 384 + lo:t * 384 + hi], T.sem["ar%d" % (3 * t + slot)],
+                    g.remote_dma(T.ld[:, o + lo:o + hi], T.ld[:, o + lo:o + hi], T.sem["ar%d" % (3 * t + slot)],
                                  T.sem.sent, pid, rid, topo.mask(core, dst))
                     sent += len(topo.engines(core, dst))
         if sent:
@@ -303,6 +322,12 @@ def rank_program(g, core, T, topo):
         else:
             add("s", lambda e: e.activation(ap(out), ap(a), ACT.Copy), [a], out)
 
+    def affine(out, a, scale, bias, func=ACT.Identity):
+        add("s", lambda e: e.activation(ap(out), ap(a), func, bias=float(bias), scale=float(scale)), [a], out)
+
+    def negate(out, a):
+        affine(out, a, -1, 0)
+
     def square(out, a):
         add("s", lambda e: e.activation(ap(out), ap(a), ACT.Square), [a], out)
 
@@ -327,16 +352,17 @@ def rank_program(g, core, T, topo):
     p7 = lambda lo, hi: vw("p7", lo, hi)
     ll = lambda lo, hi: vw("ll", lo, hi)
     eye = vw("eye", 0, 128)
+    cut = lambda v, k: vw(v[0], v[1] + 64 * k, v[1] + 64 * k + 64)
 
     def table_scatter(lo, hi, base):
         ts((vw("tab", 0, V), vw("lu", lo, hi)), vw("ramp", 0, 16 * (hi - lo)), 1.0, ALU.mult, float(base - B0), ALU.add)
 
-    def table_gather(at, lo, hi, q="v"):
-        cp(q, vw("r" + q, at, at + 16 * (hi - lo)), (vw("tab", 0, V), vw("lu", lo, hi)))
+    def table_gather(at, lo, hi):
+        cp("v", vw("rv", at, at + 16 * (hi - lo)), (vw("tab", 0, V), vw("lu", lo, hi)))
 
-    def to_lists(col, at, n, q="v"):
+    def to_lists(col, at, n, q="v", bank="p7"):
         for a in range(16):
-            mm(p7(col, col + n), vw("w" + q, 15 - a, 143 - a), vw("r" + q, at + a, at + 16 * n, 16), a == 0, a == 15)
+            mm(vw(bank, col, col + n), vw("wv", 15 - a, 143 - a), vw("r" + q, at + a, at + 16 * n, 16), a == 0, a == 15)
 
     OWN, JOINT = (0, 32), (32, 64)
 
@@ -345,6 +371,8 @@ def rank_program(g, core, T, topo):
 
     def pieces(c, win, lst, drawn=False):
         def at(name, p, h, o=0):
+            if name in ("dd", "sq") and not drawn:
+                return vw(name, h * 384 + p * 128, h * 384 + p * 128 + 128)
             o += p * S
             return vw(name, o, o + S) if h is None else vw(name, o + h * 128, o + h * 128 + 128)
 
@@ -354,6 +382,7 @@ def rank_program(g, core, T, topo):
 
         mcol = lambda p, h: at("p5", p, h) if p < 2 else at("p6", 0, h)
         to = lambda p, z, h: at("st%d" % p, 0, h, (A0, B0)[c] + z * S)
+        move = lambda p, h, sign: at("mw", 0, h, p * MW + 8 + sign * S)
         acc = lambda h: vw("p%d" % (2 + h), 0, 128)
         xx, zz, cc = ("xb", "zb", "cc") if drawn else ("xx", "zz", "p4")
         diff = lambda p, h: at("dd", p, h) if not drawn else at("p1", p, h) if p < 2 else at("p0", 0, h)
@@ -371,6 +400,7 @@ def rank_program(g, core, T, topo):
             "W": lambda p, h=None: cp("v", at(xx, p, h), ends(p, 0, h)),
             "d": d,
             "q": lambda p, h=None: square(at("sq", p, h), diff(p, h)),
+            "Q": lambda p, h: square(vw("sq", h * 384 + p * 128, h * 384 + p * 128 + 256), vw("dd", h * 384 + p * 128, h * 384 + p * 128 + 256)),
             "r": lambda h: mm(*spread(acc(h), 2 * c + h, "rn", OWN), not drawn, False),
             "a": lambda p, h: mm(acc(h), eye, at("sq", p, h), drawn and p == 0, False),
             "e": lambda p, h: mm(acc(h), eye, at("sq", p, h), False, True),
@@ -381,6 +411,13 @@ def rank_program(g, core, T, topo):
             "m": lambda p, h: tt(mcol(p, h), at(cc, 0, h), diff(p, h), ALU.mult),
             "x": lambda p, h=None: tt(to(p, 0, h), at(xx, p, h), mcol(p, h), ALU.add),
             "z": lambda p, h=None: tt(to(p, 1, h), at(zz, p, h), mcol(p, h), ALU.subtract),
+            "B": lambda h, k: tt(cut(at("p4", 1, h), k), cut(acc(h), k), cut(at("sq", 2, h), k), ALU.add),
+            "V": lambda h, k: tt(cut(at("uu", 0, h), k), cut(at("p4", 1, h), k), cut(at("kwo", c, h), k), ALU.mult),
+            "v": lambda h, k: tt(cut(at("uu", 0, h), k), cut(acc(h), k), cut(at("kwo", c, h), k), ALU.mult),
+            "C": lambda h, k: clamp(cut(at(cc, 0, h), k), cut(at("uu", 0, h), k)),
+            "M": lambda p, h: tt(move(p, h, 0), at(cc, 0, h), diff(p, h), ALU.mult),
+            "N": lambda p, h=None: negate(move(p, h, 1), move(p, h, 0)),
+            "P": lambda p, h=None: cp("s", mcol(p, h), move(p, h, 0)),
         }
 
     def run(f, text, hooks=None):
@@ -393,6 +430,9 @@ def rank_program(g, core, T, topo):
             if w[0] == "@":
                 hooks[w[1:]]()
                 continue
+            if w[0] == "!":
+                hooks["!"](w[1:])
+                continue
             f[w[0]](*[int(ch) if ch.isdigit() else "ab".index(ch) for ch in w[1:]])
 
     def into(f, words):
@@ -401,27 +441,25 @@ def rank_program(g, core, T, topo):
     sent = [0]
 
     def send(t, last):
-        k = [slots[-1] for slots in PLAN[t]].index(last) if last in [slots[-1] for slots in PLAN[t]] else None
-        if k is None:
-            return
-        plan = calls(T, topo, rank, t)
-        srcs, trs = [], []
-        for slot, lo, hi, to, engines in plan[k]:
-            o = t * 1152 + slot * 384
+        slot, o, dcore = last, t * 1152 + last * 384, T.cores[part[last]]
+        groups, n = [], 0
+        for lo, hi, to, engines, sem in pieces_of(T, topo, rank, t)[slot]:
             rid, pid = topo.addr(to, core)
-            srcs.append(vw("sb", o + lo, o + hi))
-            dst, sem = (T.ld[:, o + lo:o + hi], "ar%d" % (3 * t)) if slot == 0 else (
-                T.rl[:, t * 384 + lo:t * 384 + hi], "rin%d" % t)
-            trs.append(RemoteDMATransfer(dst_ids=[DstId(rid=rid, pnc=pid)], dma_engine_mask=bits(engines),
-                                         remote_sem=T.sem[sem], src=ap(srcs[-1]), dst=dst))
+            tr = RemoteDMATransfer(dst_ids=[DstId(rid=rid, pnc=pid)], dma_engine_mask=bits(engines),
+                                   remote_sem=T.sem["ar%d" % (3 * t + slot) if to == dcore else sem],
+                                   src=T.sb[:, o + lo:o + hi], dst=T.ld[:, o + lo:o + hi])
+            if groups and groups[-1][0] == hi - lo == 192 and not set(groups[-1][1]) & set(engines):
+                groups[-1] = (hi - lo, groups[-1][1] + engines, groups[-1][2] + [tr], groups[-1][3] + [vw("sb", o + lo, o + hi)])
+            else:
+                groups.append((hi - lo, engines, [tr], [vw("sb", o + lo, o + hi)]))
             sent[0] += len(engines)
-        call = add("g", lambda e: e.remote_dma_fused(trs, local_sem=T.sem.sent), srcs, None, ("sent", 0), holds=ISSUE)
-        for name in PLAN[t][k]:
-            n = sum(len(topo.engines(to, T.cores[part[name]]) if name else engines)
-                    for slot, lo, hi, to, engines in plan[k] if slot == name)
-            add(None, None, [], vw("ld", t * 1152 + name * 384, t * 1152 + name * 384 + 384), ("ar%d" % (3 * t + name), n),
-                soft=[call], holds=WRITE[name] + (COLD if t == 0 else 0))
-        if k == 0:
+            n += len(engines) if to == dcore else len(topo.engines(to, dcore))
+        for _, _, trs, srcs in groups:
+            call = add("g", (lambda l: lambda e: e.remote_dma_fused(l, local_sem=T.sem.sent))(trs), srcs, None, ("sent", 0),
+                       holds=ISSUE)
+            ops[-1]["soft"] = []
+        add(None, None, [], vw("ld", o, o + 384), ("ar%d" % (3 * t + slot), n), soft=[call], holds=WRITE[slot] + (COLD if t == 0 else 0))
+        if slot == 1:
             floor[:] = [call]
 
     def sends(t):
@@ -431,15 +469,29 @@ def rank_program(g, core, T, topo):
         return into({"G": lambda slot, p: border("s", slot, p), "H": lambda slot, p: border("v", slot, p),
                      "s": lambda slot: send(t, slot)}, SENDS[t])
 
+    def moves(t, f):
+        def before(q, p, lo, hi):
+            cp(q, vw("pb", p * 384 + lo * 128, p * 384 + hi * 128), (st(p, J0, WIN), ll(176 + 8 * lo, 176 + 8 * hi)))
+
+        def border(slot, p):
+            o, b = t * 1152 + slot * 384 + p * 128, p * 384 + slot * 128
+            tt(vw("sb", o, o + 128), (vw("mw", p * MW, (p + 1) * MW), ll(152 + 8 * slot, 160 + 8 * slot)),
+               vw("pb", b, b + 128), ALU.add)
+        return dict(f, E=lambda p, lo, hi: before("s", p, lo, hi), F=lambda p, lo, hi: before("v", p, lo, hi),
+                    b=border, s=lambda slot: send(t, slot))
+
     xbank = ("p3", "p0", "p1")
 
     def own_side(t, slot):
         o = t * 1152 + slot * 384
-        cp("s", vw(xbank[slot], 0, 384), vw("sb", o, o + 384))
+        if slot in BYPE[t]:
+            mm(vw(xbank[slot], 0, 384), eye, vw("sb", o, o + 384), True, True)
+        else:
+            cp("s", vw(xbank[slot], 0, 384), vw("sb", o, o + 384))
 
-    def joint(t, between, done):
+    def joint(t, between, rest, done):
         col = lambda name, p, b: vw(name, b + p * 128, b + p * 128 + 128)
-        acc = lambda slot: vw(ACC[slot], 256, 384)
+        acc = lambda slot: vw(("p2", ("p6", "p7")[t], "p2")[slot], 256, 384)
 
         def differ(slot, p):
             tt(col("dj", p, slot * 384), col(xbank[slot], p, 0), col("ld", p, t * 1152 + slot * 384), ALU.subtract)
@@ -450,18 +502,27 @@ def rank_program(g, core, T, topo):
             if slot == 2:
                 done(p)
 
-        run({"d": differ, "x": x,
+        def wide(slot, lo, hi):
+            w = lambda name, b: vw(name, b + lo * 128, b + hi * 128)
+            tt(w("dj", slot * 384), w(xbank[slot], 0), w("ld", t * 1152 + slot * 384), ALU.subtract)
+            square(w("sj", slot * 384), w("dj", slot * 384))
+
+        run({"d": differ, "x": x, "D": wide,
+             "B": lambda slot, k: tt(cut(col("p4", 2, 0), k), cut(col("p4", 1, 0), k), cut(col("sj", 2, slot * 384), k), ALU.add),
+             "V": lambda slot, k: tt(cut(vw("uu", 0, 128), k), cut(col("p4", 2, 0), k), cut(col("kwj", slot, 8), k), ALU.mult),
+             "v": lambda slot, k: tt(cut(vw("uu", 0, 128), k), cut(acc(slot), k), cut(col("kwj", slot, 8), k), ALU.mult),
+             "C": lambda slot, k: clamp(cut(vw("p4", 384, 512), k), cut(vw("uu", 0, 128), k)),
              "r": lambda slot: mm(*spread(acc(slot), part[slot], "rn", JOINT), True, False),
              "R": lambda slot: mm(*spread(acc(slot), part[slot], "rn", JOINT), True, True),
              "a": lambda slot, p: mm(acc(slot), eye, col("sj", p, slot * 384), False, False),
              "e": lambda slot, p: mm(acc(slot), eye, col("sj", p, slot * 384), False, True),
-             "s": lambda slot, p: tt(col("p5", p, 0), acc(slot), col("sj", p, slot * 384), ALU.add),
-             "S": lambda slot, p: tt(col("p5", p, 0), col("p5", p - 1, 0), col("sj", p, slot * 384), ALU.add),
+             "s": lambda slot, p: tt(col("p4", p, 0), acc(slot), col("sj", p, slot * 384), ALU.add),
+             "S": lambda slot, p: tt(col("p4", p, 0), col("p4", p - 1, 0), col("sj", p, slot * 384), ALU.add),
              "u": lambda slot: tt(vw("uu", 0, 128), acc(slot), col("kwj", slot, 8), ALU.mult),
-             "U": lambda slot: tt(vw("uu", 0, 128), col("p5", 2, 0), col("kwj", slot, 8), ALU.mult),
+             "U": lambda slot: tt(vw("uu", 0, 128), col("p4", 2, 0), col("kwj", slot, 8), ALU.mult),
              "c": lambda slot: clamp(vw("p4", 384, 512), vw("uu", 0, 128)),
              "m": lambda slot, p: tt(col("p4", p, 0), vw("p4", 384, 512), col("dj", p, slot * 384), ALU.mult)},
-            JOINTS, {"": between})
+            JOINTS, {"": between, "!": rest, "1": scalar_lists if t == 0 else lambda: None, "2": scalar_lists2 if t == 0 else lambda: None})
 
     both, one = (0, 64), (0, 1)
     load("y", vw("li", 0, 64), T.ends[:, :])
@@ -469,11 +530,14 @@ def rank_program(g, core, T, topo):
     load("y", vw("wc", 0, 128, 1, JOINT), T.jinv[:, :])
     load("s", vw("kc", 0, 128, 1, OWN), T.stiff[:, :])
     load("s", vw("kc", 0, 128, 1, JOINT), T.jstiff[:, :])
-    for p in range(3):
-        load("y", pos(p), T.pos[:, p * V:(p + 1) * V])
-    for s in range(3):
-        load("y", vw("li", 72 + 8 * s, 80 + 8 * s), T.bord[:, 8 * part[s]:8 * part[s] + 8])
-    load("y", vw("li", 64, 72), T.watch[:, :])
+    for w in LOADS.split():
+        if w == "b":
+            for s in range(3):
+                load("y", vw("li", 72 + 8 * s, 80 + 8 * s), T.bord[:, 8 * part[s]:8 * part[s] + 8])
+        elif w == "w":
+            load("y", vw("li", 64, 72), T.watch[:, :])
+        else:
+            load("y", pos(int(w)), T.pos[:, int(w) * V:(int(w) + 1) * V])
     fill(vw("ones", 0, 128), 1.0)
     count(vw("ramp", 0, 512), [[1, 512]], B0)
     fill(vw("oneb", 0, 144), 1.0)
@@ -488,12 +552,22 @@ def rank_program(g, core, T, topo):
     select(vw("wv", 0, 144), vw("oneb", 0, 144), [[-16, 9], [256, 16]], -15 * 256)
     count(vw("row", 0, 128, 1, one), [[0, 8], [1, 16]], 0)
     count(vw("row", 128, 160, 1, one), [[16, 32]], B0)
-    last = select(eye, vw("ones", 0, 128), [[-1, 128]], 0)
+    select(eye, vw("ones", 0, 128), [[-1, 128]], 0)
+    for name in ("kwj", "rj"):
+        last = count(vw(name, 0, 8), [[0, 8]], 0)
+    for p in range(3 if len(PLAIN) < 3 else 0):
+        count(vw("aw", 0, 8), [[0, 8]], 0)
+        count(vw("aw", 520, MW), [[1, 512]], A0)
+        count(vw("mw", p * MW, p * MW + 8), [[0, 8]], 0)
+        last = count(vw("mw", p * MW + 520, (p + 1) * MW), [[0, 512]], 0)
     for a in range(4):
         select(vw("sel", a * 128, a * 128 + 128, 1, JOINT), vw("ones", 0, 128, 1, JOINT), [[-4, 8], [0, 16]], -a, [last])
     cp("v", vw("lu", 0, 64), vw("li", 0, 64))
     wn, wc, rn = (vw(n, 0, 128, 1, both) for n in ("wn", "wc", "rn"))
-    add("s", lambda e: e.activation(ap(wn), ap(wc), ACT.Identity, bias=-EPS, scale=-1.0), [wc], wn)
+    if WN == "s":
+        add("s", lambda e: e.activation(ap(wn), ap(wc), ACT.Identity, bias=-EPS, scale=-1.0), [wc], wn)
+    else:
+        ts(wn, wc, -1.0, ALU.mult, -EPS, ALU.add)
 
     def product():
         tt(vw("kn", 0, 128, 1, both), vw("kc", 0, 128, 1, both), wn, ALU.mult)
@@ -501,12 +575,16 @@ def rank_program(g, core, T, topo):
             mm(*spread(vw("p0", a * 128, a * 128 + 128), a, "kn", OWN), True, True)
 
     def first_list():
-        to_lists(0, 0, 32)
+        to_lists(0, 0, 32, "s" if "@G1" in FIRST else "v")
         mm(p7(32, 64), vw("row", 0, 128, 1, one), vw("oneb", 0, 32, 1, one), True, False)
         mm(p7(32, 64), vw("oneb", 0, 128, 1, one), vw("row", 128, 160, 1, one), False, True)
 
     def first_places():
-        cp("s", sm(0, 64), p7(0, 64))
+        if "@G1" in FIRST:
+            affine(sm(0, 32), p7(0, 32), 1, 1280)
+            cp("s", sm(32, 64), p7(32, 64))
+        else:
+            cp("s", sm(0, 64), p7(0, 64))
         small.extend([lambda: tt(sm(64, 96), sm(0, 32), sm(32, 64), ALU.max),
                       lambda: ts(ll(0, 32), sm(64, 96), float(B0), ALU.subtract),
                       lambda: ts(sm(96, 120), sm(32, 56), float(J0 - B0), ALU.add)])
@@ -516,9 +594,32 @@ def rank_program(g, core, T, topo):
                       lambda: ts(ll(32, 56), sm(120, 144), float(J0), ALU.subtract)])
 
     def later_lists():
-        small.extend([lambda: ts(ll(56, 88), p7(96, 128), float(J0), ALU.subtract),
-                      lambda: tt(sm(144, 176), p7(128, 160), sm(0, 32), ALU.max),
+        small.append(lambda: ts(ll(56, 88), p7(96, 128), float(J0), ALU.subtract))
+
+    def scalar_lists():
+        affine(vw("rs", 0, 512), (vw("tab", 0, V), vw("lu", 32, 64)), 1, -384)
+        ops[-1]["stay"] = STAY[0]
+
+    def scalar_lists2():
+        if len(PLAIN) == 3:
+            return to_lists(0, 0, 32, "s", "p5")
+        affine(vw("rs", 512, 1024), (vw("aw", 0, MW), ll(144, 176)), 1, -1280)
+        ops[-1]["stay"] = STAY[1]
+        to_lists(0, 0, 64, "s", "p5")
+
+    def last_lists():
+        affine(sm(176, 208), vw("p5", 0, 32), 1, 384)
+        ops[-1]["stay"] = True
+        affine(sm(208, 240), vw("p5", 0, 32), 16, -127 * 16, ACT.Relu)
+        small.extend([lambda: tt(sm(240, 272), sm(176, 208), sm(208, 240), ALU.add),
+                      lambda: tt(sm(328, 360), sm(240, 272), sm(32, 64), ALU.min),
+                      lambda: tt(sm(144, 176), sm(328, 360), sm(0, 32), ALU.max),
                       lambda: ts(ll(88, 120), sm(144, 176), float(J0), ALU.subtract)])
+        if len(PLAIN) == 3:
+            return
+        affine(sm(272, 304), vw("p5", 32, 64), 1, 1280)
+        small.extend([lambda: tt(sm(304, 328), sm(280, 304), sm(96, 120), ALU.max),
+                      lambda: ts(ll(176, 200), sm(304, 328), float(J0), ALU.subtract)])
 
     def start(p, region, n, col, q="s"):
         cp(q, st(p, region, region + 16 * n), (pos(p), vw("lu", col, col + n)))
@@ -529,6 +630,7 @@ def rank_program(g, core, T, topo):
         "G2": lambda: table_gather(512, 64, 96, "s"), "T2": lambda: to_lists(64, 512, 32, "s"),
         "+": lambda: floor.append(len(ops) - 1), "-": floor.clear,
         "g3": lambda: table_gather(640, 72, 96), "t3": lambda: to_lists(72, 640, 24),
+        "G1": lambda: affine(vw("rs", 0, 512), (vw("tab", 0, V), vw("lu", 32, 64)), 1, -1280),
         "t1": first_list, "t2": lambda: to_lists(64, 512, 32), "l1": first_places, "bl": border_list,
         "kn": product, "kw": lambda: cp("s", vw("kwo", 0, 512), vw("p0", 0, 512)),
         "rn": lambda: add("v", lambda e: e.reciprocal(ap(rn), ap(wn)), [wn], rn, holds=200 + 6 * 128),
@@ -544,39 +646,60 @@ def rank_program(g, core, T, topo):
     run(c0, FIRST + FTAIL, dict(hooks, **into(c1, PRE)))
     for t in range(SWEEPS):
         if t > 0:
-            run(c0, JHEAD + TAIL, into(c1, PRE))
-        run(c1, HEAD + (SECOND + " " if t == 0 else "") + TAIL, dict(hooks, **sends(t)))
+            run(c0, JHEAD)
+            if t == 1:
+                last_lists()
+            run(c0, TAIL, into(c1, PRE))
+        if t in PLAIN:
+            run(c1, HEAD + (SECOND + " " if t == 0 else "") + TAIL, dict(hooks, **sends(t)))
+        else:
+            run(moves(t, c1), HEAD + MOVES[t])
         if t == SWEEPS - 1:
             break
+        if t == 0 and len(PLAIN) < 3:
+            mm(vw("p5", 0, 512), vw("eyeb", 0, 128), vw("rv", 0, 512), True, True)
+            cp("s", vw("aw", 8, 520), vw("p5", 0, 512))
         if t == 0:
-            fill(vw("kwj", 0, 8), 0.0)
             if "@g3" in FIRST + SECOND:
                 table_gather(512, 64, 72)
                 to_lists(64, 512, 8)
             for s in range(3):
                 mm(*spread(vw("p0", s * 128, s * 128 + 128), part[s], "kn", JOINT), True, True)
             table_scatter(72, 96, J0)
-        own_side(t, 0)
+        if t in PLAIN:
+            own_side(t, 0)
         if t == 0:
-            table_gather(1024, 0, 72)
             cp("s", vw("kwj", 8, 392), vw("p0", 0, 384))
-            to_lists(96, 1024, 72)
-        own_side(t, 1)
-        own_side(t, 2)
+            own_side(t, 1)
+            if len(PLAIN) < 3:
+                ts(ll(144, 176), p7(64, 96), float(B0 - 8), ALU.subtract, 0.0, ALU.max)
+            table_gather(1024, 0, 32)
+            table_gather(1536, 64, 72)
+            to_lists(96, 1024, 40)
+            own_side(t, 2)
+        elif t in PLAIN:
+            own_side(t, 1)
+            own_side(t, 2)
+        else:
+            run(dict(c1, o=lambda slot: own_side(t, slot)), SHADE)
         c0 = pieces(0, lambda p: st(p, J0, WIN), ("ll", 56))
-        c1 = pieces(1, lambda p: st(p, J0, WIN), ("ll", 88))
-        joint(t, later_lists if t == 0 else (lambda: None), lambda p: run(c0, JPRE[p]))
 
-    fill(vw("rj", 0, 8), 0.0)
+        def rest(w):
+            if t not in PLAIN:
+                run(dict(c1, o=lambda slot: own_side(t, slot)), w)
+                ops[-1]["stay"] = True
+        joint(t, later_lists if t == 0 else (lambda: None), rest, lambda p: run(c0, JPRE[p]))
+        c1 = pieces(1, lambda p: st(p, J0, WIN), ("ll", 88))
+
     for s in range(3):
         mm(*spread(vw("p1", s * 128, s * 128 + 128), part[s], "rn", JOINT), True, True)
     cp("s", vw("rj", 8, 392), vw("p1", 0, 384))
     for p in range(3):
         start(p, W0, 8, 64)
-    late = p7(160, 168)
+    late = p7(128, 136)
     ts(sm(64, 72), sm(32, 40), float(W0 - B0), ALU.add)
     ts(sm(72, 80), late, float(B0), ALU.is_lt)
-    tt(sm(80, 88), p7(64, 72), sm(64, 72), ALU.max)
+    tt(sm(80, 88), p7(64, 72) if 2 in PLAIN else sm(272, 280), sm(64, 72), ALU.max)
     tt(sm(96, 104), late, sm(72, 80), ALU.mult)
     tt(sm(88, 96), late, sm(80, 88), ALU.max)
     ts(ll(128, 136), sm(96, 104), float(J0 - 8), ALU.subtract, 0.0, ALU.max)
@@ -593,22 +716,28 @@ def rank_program(g, core, T, topo):
     cp("v", vw("rw", 0, 128), (vw("rj", 0, 392), ll(128, 136)))
     cp("v", vw("kww", 0, 128), (vw("kwj", 0, 392), ll(128, 136)))
     for p in range(3):
-        cp("s", col("xx", p), (st(p, 0, WIN), ll(120, 128)))
+        cp("s", col("xx" if 2 in PLAIN else "zz", p), (st(p, 0, WIN), ll(120, 128)))
+        if 2 not in PLAIN:
+            tt(col("xx", p), (vw("mw", p * MW, (p + 1) * MW), ll(144, 152)), col("zz", p), ALU.add)
     cp("v", vw("p2", 0, 128), vw("rw", 0, 128))
     for p in range(3):
         tt(col("dj", p), (vw("ld", o + p * 128, o + p * 128 + 896), ll(136, 144)), col("xx", p), ALU.subtract)
         square(col("sj", p), col("dj", p))
     tt(vw("p4", 0, 128), vw("p2", 0, 128), col("sj", 0), ALU.add)
     tt(vw("p4", 128, 256), vw("p4", 0, 128), col("sj", 1), ALU.add)
-    tt(vw("p4", 256, 384), vw("p4", 128, 256), col("sj", 2), ALU.add)
-    tt(vw("uu", 0, 128), vw("p4", 256, 384), vw("kww", 0, 128), ALU.mult)
-    clamp(vw("p4", 384, 512), vw("uu", 0, 128))
+    half = lambda name, o, h: vw(name, o + 64 * h, o + 64 * h + 64)
+    for h in (0, 1):
+        tt(half("p4", 256, h), half("p4", 128, h), half("sj", 256, h), ALU.add)
+    for h in (0, 1):
+        tt(half("uu", 0, h), half("p4", 256, h), half("kww", 0, h), ALU.mult)
+    for h in (0, 1):
+        clamp(half("p4", 384, h), half("uu", 0, h))
     m = lambda p: tt(col("p5", p), vw("p4", 384, 512), col("dj", p), ALU.mult)
     x = lambda p: tt(col("yb", p), col("xx", p), col("p5", p), ALU.subtract)
-    m(0); m(1); x(0); x(1); m(2); x(2)
-    first = store("y", T.y[:, 0:256], vw("yb", 0, 256), "d12")
-    stored = store("s", T.y[:, 256:384], vw("yb", 256, 384), "d13")
-    add("y", None, [], None, after=[first, stored], holds=1)
+    m(0); m(1); x(0); m(2); x(1); x(2)
+    done = [store(q, T.y[:, lo:hi], vw("yb", lo, hi), "d%d" % (12 + k)) for k, (q, lo, hi) in enumerate(STORES)]
+    stored = done[-1]
+    add("y", None, [], None, after=done, holds=1)
     total = add(None, None, [], None, ("sent", sent[0]), soft=[stored], holds=1)
     add("g", None, [], None, after=[total], holds=1)
     emit(g, T, arrange(ops))

@@ -3,100 +3,86 @@ from concourse.mybir import AluOpType as ALU, ActivationFunctionType as ACT
 
 V, S = 2048, 256
 W0, J0, B0, A0, WIN = 0, 128, 512, 1024, 1536
-MW = 1032
 EPS = 1e-22
 SWEEPS = 3
 F = "float32"
-GATHER, SCATTER, MATMUL, FIXED, HOP, SELF = 1.56, 3.8, 3, {"v": 30, "s": 140}, 200, 70
-DMA, LOAD, ISSUE, WRITE, COLD = 1300, 170, 300, (3600, 5000, 5800), 3000
+GATHER, SCATTER, MATMUL, FIXED, HOP, SELF = 1.56, 3.8, 3, {"v": 30, "s": 140}, 170, 60
+DMA, ISSUE, LOAD, TURN = 1150, 250, 1330, 3900
+TILES = {"mc": ("ll", 0, 32), "mb": ("ll", 32, 56), "md": ("ll", 56, 128)}
+for _p in range(3):
+    TILES.update({"X%d" % _p: ("xz", _p * 512, _p * 512 + S), "Z%d" % _p: ("xz", _p * 512 + S, _p * 512 + 512),
+                  "B%d" % _p: ("st%d" % _p, B0, B0 + S), "b%d" % _p: ("st%d" % _p, B0 + S, A0),
+                  "J%d" % _p: ("st%d" % _p, W0, S), "j%d" % _p: ("st%d" % _p, S, B0), "y%d" % _p: ("yb", _p * 128, _p * 128 + 128)})
+TILES.update({"y2": ("yb", 256, 320), "y3": ("yb", 320, 384)})
+WHOLE = ("md", "y2", "y3")
 
 SCRATCH = {
     "posb": ("sbuf", [128, 3 * V], "bfloat16"),
-    "li": ("sbuf", [128, 96], "int32"),
-    "lu": ("sbuf", [128, 96], "uint16"),
-    "ll": ("sbuf", [128, 200], "uint16"),
-    "mw": ("sbuf", [128, 3 * MW], F),
-    "aw": ("sbuf", [128, MW], F),
-    "pb": ("sbuf", [128, 1152], F),
-    "sm": ("sbuf", [128, 368], F),
+    "li": ("sbuf", [128, 104], "int32"),
+    "lo": ("sbuf", [128, 96], "uint16"),
+    "ki": ("sbuf", [128, 8], "int32"),
+    "sm": ("sbuf", [128, 256], F),
     "tab": ("sbuf", [128, V], F),
     "ramp": ("sbuf", [128, 512], F),
     "rv": ("sbuf", [128, 2176], "float16"),
-    "ones": ("sbuf", [128, 128], F),
-    "rs": ("sbuf", [128, 1024], "bfloat16"),
-    "oneb": ("sbuf", [128, 272], "bfloat16"),
-    "eyeb": ("sbuf", [128, 256], "bfloat16"),
+    "rf": ("sbuf", [128, 1152], F),
     "wv": ("sbuf", [128, 144], "bfloat16"),
-    "row": ("sbuf", [128, 160], "bfloat16"),
-    "eye": ("sbuf", [128, 128], F),
-    "sel": ("sbuf", [128, 512], F),
     "kc": ("sbuf", [128, 128], "bfloat16"),
     "wc": ("sbuf", [128, 128], "bfloat16"),
     "wn": ("sbuf", [128, 128], F),
     "rn": ("sbuf", [128, 128], F),
     "kn": ("sbuf", [128, 128], F),
+    "tk": ("dram", [16, 128, 16], "bfloat16"),
+    "xz": ("sbuf", [128, 1536], "bfloat16"),
+    "ll": ("sbuf", [128, 128], "uint16"),
+    "selb": ("sbuf", [128, 512], "bfloat16"),
+    "oneb": ("sbuf", [128, 272], "bfloat16"),
+    "eyeb": ("sbuf", [128, 256], "bfloat16"),
+    "eye": ("sbuf", [128, 128], F),
+    "sel": ("sbuf", [128, 10 * 128], F),
+    "qq": ("sbuf", [128, 384], F),
     "kwo": ("sbuf", [128, 512], F),
-    "kwj": ("sbuf", [128, 392], F),
-    "rj": ("sbuf", [128, 392], F),
-    "kww": ("sbuf", [128, 128], F),
-    "rw": ("sbuf", [128, 128], F),
     "st0": ("sbuf", [128, WIN], F),
     "st1": ("sbuf", [128, WIN], F),
     "st2": ("sbuf", [128, WIN], F),
-    "xb": ("sbuf", [128, 768], "bfloat16"),
-    "zb": ("sbuf", [128, 768], "bfloat16"),
     "zz": ("sbuf", [128, 768], F),
     "xx": ("sbuf", [128, 768], F),
     "dd": ("sbuf", [128, 768], F),
     "sq": ("sbuf", [128, 768], F),
-    "dj": ("sbuf", [128, 1152], F),
+    "gb": ("sbuf", [128, 1152], F),
     "sj": ("sbuf", [128, 1152], F),
     "uu": ("sbuf", [128, 256], F),
     "cc": ("sbuf", [128, 256], F),
+    "dj": ("sbuf", [128, 1152], F),
     "yb": ("sbuf", [128, 384], F),
-    "sb": ("sbuf", [128, SWEEPS * 1152], F),
-    "ld": ("sbuf", [128, SWEEPS * 1152], F),
 }
 for _k in range(8):
     SCRATCH["p%d" % _k] = ("psum", [128, 512], F)
+for _k, (_b, _lo, _hi) in TILES.items():
+    if _k in WHOLE:
+        SCRATCH["t" + _k] = ("dram", [4, 128, _hi - _lo], SCRATCH[_b][2])
+    else:
+        SCRATCH["t" + _k] = ("dram", [8, 128, (_hi - _lo) // 4], SCRATCH[_b][2])
+        SCRATCH["u" + _k] = ("dram", [128, _hi - _lo], SCRATCH[_b][2])
 
-SEMAPHORES = (["qv", "qs", "qt", "qg", "sent"] + ["d%d" % k for k in range(15)]
-              + ["ar%d" % k for k in range(3 * SWEEPS)] + ["rin%d" % k for k in range(10 * SWEEPS)])
+SEMAPHORES = (["qv", "qs", "qt", "qg", "sent", "kar0", "kar1"] + ["d%d" % k for k in range(56)]
+              + [w + str(k) for w in ("ar", "rin") for k in range(len(TILES) + 1)] + ["out%d" % k for k in range(20)])
 
-FIRST = ("@kn @sA Z0 X0 d0 @g1 @rn @sB q0 a0a a0b Z1 X1 d1 @kw X2 Z2 q1 d2a d2b @+ q2a q2b ra e1a rb a1b e2b @t1 @- "
-         "@ol @g3 @l1 @B0 @B1 @B2 @J0 @J1 @t3 ")
-SECOND = "@J2 @bl"
+FIRST = "d0 Q d1 q1 d2a d2b q2a q2b D Ea Eb Va Vb Ka Kb La Lb m0 @j2 @jr @lk m1 x0 z0 @n0 m2 x1 z1 @n1 x2 z2 @n2"
 HEAD = "ra rb d0a q0a d1a q1a a0a Z2b d2a q2a e1a d0b q0b d1b q1b a0b a1b d2b q2b e2b "
 JHEAD = "ra rb Y0b d0a Z1b q0a d1a q1a a0a d2a Z2b q2a e1a d0b q0b d1b q1b a0b a1b d2b q2b e2b "
-FTAIL = "Ba0 Ba1 Va0 Va1 Ca0 Ca1 . m0a . m1a . m2a ub . x0a cb . z0a m0b . m1b x0b z0b @n0 m2b x1 z1 @n1 x2 z2 @n2"
+FTAIL = "Ba0 Ba1 Va0 Va1 Ca0 Ca1 m0a m1a m2a ub x0a cb z0a m0b m1b x0b z0b @n0 m2b x1 z1 @n1 x2 z2 @n2"
 TAIL = "X0 X1 X2 " + FTAIL
-WN = "v"
-STORES = (("y", 0, 128), ("s", 128, 384))
 PRE = ("Z0", "Z1", "Z2a")
 JPRE = ("Z0a", "Z1a", "Z2a")
-CUT = 72
-ZERO = 640
-SENDS = (("G10 G00 G20", "G11 G01 G21", "H12 s1 H02 s0 H22 s2"),
-         ("G10 G00 G20", "G11 G01 G21", "H12 s1 H02 s0 H22 s2"),
-         ("G10 G20 G00", "G11 G21 G01", "H12 s1 H22 s2 H02 s0"))
-WORLD = 256
-ROUTE = ("1n:128:all 1a:256:all 0d:384:off 2a:192:rest1 2n:192:rest0",
-         "1a:256:all 0d:384:off 1n:128:rest 2n:192:rest0 2a:192:rest1",
-         "1n:128:all 1a:256:all 2a:256:all 2n:128:all 0d:384:off")
-JOINTS = ("R0 d00 d01 d02 !X2 s00 S01 B00 B01 @ V00 V01 C00 C01 @1 r1 d10 a10 d11 a11 d12 e12 !o2 !x2 m00 m01 x00 m02 x01 x02 "
-          "r2 d20 a20 d21 a21 d22 e22 @2 v10 v11 C10 C11 . m10 m11 x10 m12 x11 x12 v20 v21 C20 C21 m20 m21 x20 m22 x21 x22")
-JOINT0 = ("R0 d00 d01 d02 s00 S01 S02 @ U0 . c0 @1 R1 m00 m01 x00 m02 x01 x02 r2 d10 d11 d12 d20 a20 s10 d21 a21 S11 d22 e22 S12 "
-          "@2 U1 c1 m10 m11 x10 m12 x11 u2 x12 c2 m20 m21 x20 m22 x21 x22")
-PLAIN = (0,)
-STAY = (False, True)
-MOVES = (None,
-         "E012 E112 E001 Ba0 Ba1 Va0 Va1 Ca0 Ca1 M0a M1a M2a vb0 vb1 N0a Cb0 Cb1 N1a M0b N2a M1b N0b M2b N1b N2b "
-         "E101 b10 E201 b11 E212 b00 b01 b02 s0 E023 b12 s1 E123 E223 b20 b21 b22 s2",
-         "E012 E112 E212 Ba0 Ba1 Va0 Va1 Ca0 Ca1 M0a M1a M2a vb0 vb1 N0a Cb0 Cb1 N1a M0b N2a M1b N0b M2b N1b N2b "
-         "E023 b10 E123 b11 E223 b12 s1 E001 b20 E101 b21 E201 b22 s2 b00 b01 b02 s0")
-SHADE = "X0 P0 z0 x0 X1 P1 z1 x1 o0 P2 z2 o1"
-LOADS = "0 1 2 b w"
-BYPE = ((), ())
+BORDER = ("t0 P0 g0", "t1 P1 g1", "T2 P2 g2 D0 q0 D1 q1 A0 d0 d1 S1 A1 s0 o0 o1 o2")
+JOINT = "B0 B1 V0 V1 C0 C1 m0 R0 m1 R1 m2 R2 x0 x1 z0 @n0 x2 z1 @n1 z2 @n2"
+LAST = ("w0", "w1", "u2")
+NEAR = "p3"
+CALLS = "k X0:0,Z0:2 X1:1,Z1:3 X2:0,Z2:2 B0:1,b0:3 mc:0 B1:0,b1:2 B2:1,b2:3 mb:1 J0:0,j0:2 J1:1,j1:3 J2:0,j2:2 md:0 y0:1 y1:3 y2:0,y3:2 y2:d,y3:d"
+LANDS = "X0,Z0 X1,Z1 X2,Z2 mc B0,b0 B1,b1 B2,b2 mb"
+WAY = {"MD": 3000, "Y0": 3600, "Y1": 3500, "Y2": 2600, "Y3": 2600, "K": 7500, "X0": 6000, "Z0": 6000, "X1": 5000, "Z1": 5000, "X2": 4500, "Z2": 4500, "B0": 5500, "B1": 5500, "B2": 5500, "J0": 5500, "J1": 5500, "J2": 6500}
+NAMES = ["k"] + list(TILES)
 
 
 def bits(engines):
@@ -106,58 +92,78 @@ def bits(engines):
     return m
 
 
-def routes(T, topo, r):
-    me = T.cores[r]
-    others = [q for q in range(len(T.cores)) if q != r]
-    direct = [q for q in others if topo.may_write(me, T.cores[q])]
-    far = [q for q in others if q not in direct]
-    far.sort(key=lambda q: topo.host(T.cores[q]) != topo.host(me))
-    relays = {}
-    for i, q in enumerate(far):
-        can = [c for c in topo.cores_of(me) if c != me and topo.may_write(c, T.cores[q])]
-        near = [c for c in can if topo.die(c) == topo.die(me)]
-        away = [c for c in can if topo.die(c) != topo.die(me)]
-        mate = [c for c in range(WORLD) if topo.mates(c, T.cores[q]) and topo.may_write(c, T.cores[q]) and topo.die(c) == topo.die(me)]
-        relays[1 + i] = {"n": near[i], "a": away[i], "m": mate[i], "N": near[1 - i], "A": away[1 - i]}
-    free = [c for c in topo.cores_of(me) if c != me and not topo.may_write(c, T.cores[far[0]])]
-    relays[0] = {"d": T.cores[direct[0]], "a": [c for c in free if topo.die(c) != topo.die(me)][0],
-                 "n": [c for c in free if topo.die(c) == topo.die(me)][0]}
-    return direct + far, relays
+def transfer(T, topo, core, to, engines, sem, src, dst):
+    rid, pid = topo.addr(to, core)
+    return RemoteDMATransfer(dst_ids=[DstId(rid=rid, pnc=pid)], dma_engine_mask=bits(engines), remote_sem=T.sem[sem], src=src, dst=dst)
 
 
-def pieces_of(T, topo, r, t):
+def ways(T, topo, r):
     me = T.cores[r]
-    part, relays = routes(T, topo, r)
-    every, off = topo.engines(me, relays[1]["n"]), topo.engines(me, T.cores[part[0]])
+    others = sorted((q for q in range(len(T.cores)) if q != r), key=lambda q: topo.may_write(me, T.cores[q]))
+    can = [c for c in topo.cores_of(me) if c != me and all(topo.may_write(c, T.cores[q]) for q in others)]
+    return others, sorted(can, key=lambda c: topo.die(c) != topo.die(me))
+
+
+def calls_of(T, topo, r):
+    others, relays = ways(T, topo, r)
+    every, off = topo.engines(T.cores[r], relays[0]), topo.engines(T.cores[r], T.cores[others[2]])
     rest = [e for e in every if e not in off]
-    sets = {"all": every, "off": off, "rest": rest}
-    out = {}
-    for k, w in enumerate(ROUTE[t].split()):
-        head, n, name = w.split(":")
-        slot = int(head[0])
-        lo = out[slot][-1][1] if slot in out else 0
-        engines = sets[name[:-1]][int(name[-1])::2] if name[-1] in "01" else sets[name]
-        out.setdefault(slot, []).append((lo, lo + int(n), relays[slot][head[1]], engines, "rin%d" % (10 * t + k)))
+    out = []
+    for call in CALLS.split()[1:]:
+        tiles = [w.split(":") for w in call.split(",")]
+        n = len(tiles)
+        both = lambda name: name in WHOLE and name + ":d" not in CALLS
+        out.append([(name, None, [], off[i::n]) if k == "d" else
+                    (name, relays[int(k)], (rest if both(name) else every)[i::n], off[i::n] if both(name) else [])
+                    for i, (name, k) in enumerate(tiles)])
     return out
 
 
+def onward(T, topo, r, relay, name):
+    others = ways(T, topo, r)[0]
+    off = topo.engines(relay, T.cores[others[0]])
+    if name in WHOLE:
+        return {others[0]: off[0::2], others[1]: off[1::2]}
+    half = len(off) // 2
+    return {others[0]: off[1::2], others[1]: off[0:half:2], others[2]: off[half::2]}
+
+
+def first_call(T, topo, r):
+    others, relays = ways(T, topo, r)
+    me, there = T.cores[r], T.cores[others[2]]
+    off = topo.engines(me, there)
+    rest = [e for e in topo.engines(me, relays[0]) if e not in off]
+    return [(q, part, to, es) for part in (0, 1)
+            for q, to, es in ((others[0], relays[2 * part], [rest[4 * part]]), (others[1], relays[2 * part + 1], [rest[4 * part + 2]]),
+                              (others[2], there, [off[2 * part]]))]
+
+
 def relay_program(g, core, T, topo):
-    for r, me in enumerate(T.cores):
-        part, relays = routes(T, topo, r)
+    n = len(T.cores)
+    for r in range(n):
         sent = 0
-        if not any(core in ways.values() for ways in relays.values()):
-            continue
-        for t in range(SWEEPS):
-            mine = [(x[4], slot) + x[:4] for slot, trs in pieces_of(T, topo, r, t).items() for x in trs if x[2] == core]
-            for _ in (0,):
-                for sem, slot, lo, hi, to, engines in sorted(mine):
-                    dst = T.cores[part[slot]]
-                    rid, pid = topo.addr(dst, core)
-                    g.wait_ge(T.sem[sem], len(engines))
-                    o = t * 1152 + slot * 384
-                    g.remote_dma(T.ld[:, o + lo:o + hi], T.ld[:, o + lo:o + hi], T.sem["ar%d" % (3 * t + slot)],
-                                 T.sem.sent, pid, rid, topo.mask(core, dst))
-                    sent += len(topo.engines(core, dst))
+        for q, part, to, engines in first_call(T, topo, r):
+            if to == core:
+                g.wait_ge(T.sem.rin0, len(engines))
+                one, piece = topo.engines(core, T.cores[q])[:1], T.tk[(2 * part + 1) * n + r]
+                g.remote_dma_fused([transfer(T, topo, core, T.cores[q], one, "kar%d" % part, piece, piece)], local_sem=T.sem.sent)
+                sent += 1
+        for call in calls_of(T, topo, r):
+            for name, to, engines, _ in call:
+                if to != core:
+                    continue
+                k, t, whole = NAMES.index(name), T["t" + name], name in WHOLE
+                if whole:
+                    g.wait_ge(T.sem["rin%d" % k], len(engines))
+                else:
+                    g.sync.wait_ge(T.sem["rin%d" % k], len(engines))
+                    g.sync.dma_start(t[0:n], T["u" + name][:]).then_inc(T.sem["d%d" % k], 16)
+                    g.wait_ge(T.sem["d%d" % k], 16)
+                legs = onward(T, topo, r, core, name)
+                trs = [transfer(T, topo, core, T.cores[q], es, "ar%d" % k, t[r if whole else q], t[r if whole else n + r])
+                       for q, es in legs.items()]
+                g.remote_dma_fused(trs, local_sem=T.sem.sent)
+                sent += sum(len(es) for es in legs.values())
         if sent:
             g.wait_ge(T.sem.sent, sent)
 
@@ -189,16 +195,18 @@ def arrange(ops):
     for i, (o, met) in enumerate(zip(ops, meetings(ops))):
         need = {j: (HOP if ops[j]["q"] != o["q"] else SELF) if waited else 0 for j, waited in met.items()}
         need.update({j: HOP for j in o["after"] + o["soft"]})
-        t = max([begin[j] + ops[j]["takes"] + lag for j, lag in need.items()] + [0])
+        t = max([begin[j] + ops[j]["takes"] + lag for j, lag in need.items()] + [begin[j] + ISSUE for j in o["behind"]] + [0])
         if o["q"] is not None:
-            if o["stay"] or any(v[0] == "ld" for v in o["r"]):
-                t = max([t] + [hi for lo, hi in busy[o["q"]]])
-            for lo, hi in sorted(busy.setdefault(o["q"], [])):
+            mine = busy.setdefault(o["q"], [])
+            if o["stay"]:
+                t = max([t] + [hi for lo, hi in mine])
+            for lo, hi in sorted(mine):
                 if t + o["holds"] <= lo:
                     break
                 t = max(t, hi)
-            busy[o["q"]].append((t, t + o["holds"]))
+            mine.append((t, t + o["holds"]))
         begin[i] = t
+        o["at"] = t
     return [ops[i] for i in sorted(range(len(ops)), key=lambda i: (begin[i], i))]
 
 
@@ -258,8 +266,8 @@ def rank_program(g, core, T, topo):
     if rank is None:
         relay_program(g, core, T, topo)
         return
-    part, relays = routes(T, topo, rank)
-    ops, floor, small = [], [], []
+    others = ways(T, topo, rank)[0]
+    ops = []
 
     def vw(name, lo, hi, step=1, parts=(0, 128)):
         return (name, lo, hi, step, parts)
@@ -267,6 +275,8 @@ def rank_program(g, core, T, topo):
     def ap(v):
         if len(v) == 2:
             return ap(v[0]).indirect(ap(v[1]))
+        if SCRATCH[v[0]][0] == "dram":
+            return T[v[0]][v[1]:v[2]]
         if v[3] == 1:
             return T[v[0]][v[4][0]:v[4][1], v[1]:v[2]]
         return T[v[0]][v[4][0]:v[4][1], v[1]:v[2]:v[3]]
@@ -295,23 +305,31 @@ def rank_program(g, core, T, topo):
             r += span(out)[1:]
         holds = cycles(q, ins, out) if holds is None else holds
         ops.append({"n": len(ops), "q": q, "fn": fn, "r": r, "w": w, "own": own, "dma": dma, "after": list(after),
-                    "soft": list(soft) + floor, "stay": False, "holds": holds, "takes": holds if takes is None else takes})
+                    "soft": list(soft), "behind": [], "stay": False, "holds": holds, "takes": holds if takes is None else takes})
         return len(ops) - 1
 
-    loaded = [0]
+    dmas = [0]
 
-    def load(q, out, src):
-        loaded[0] += 150 + (out[2] - out[1]) * (out[4][1] - out[4][0]) // LOAD
-        add(q, lambda e: e.dma_start(ap(out), src), [], out, ("d%d" % len(ops), 16), True, holds=1, takes=DMA + loaded[0])
+    def dma(q, out, src, takes):
+        dmas[0] += 1
+        views = [isinstance(v, tuple) for v in (out, src)]
+        n = add(q, lambda e: e.dma_start(ap(out) if views[0] else out, ap(src) if views[1] else src), [src] if views[1] else [],
+                out if views[0] else None, ("d%d" % (dmas[0] - 1), 16), True, holds=50, takes=DMA + takes)
+        ops[-1]["stay"] = True
+        return n
 
-    def store(q, dst, src, sem):
-        return add(q, lambda e: e.dma_start(dst, ap(src)), [src], None, (sem, 16), True, holds=1, takes=DMA)
+    def together(n):
+        dmas[0] -= n - 1
+        for o in ops[-n:]:
+            o["own"] = ("d%d" % (dmas[0] - 1), 16 * n)
 
     def tt(out, a, b, op):
         add("v", lambda e: e.tensor_tensor(ap(out), ap(a), ap(b), op), [a, b], out)
 
     def ts(out, a, s1, op0, s2=None, op1=None):
-        if op1 is None:
+        if isinstance(s1, tuple):
+            add("v", lambda e: e.tensor_scalar(ap(out), ap(a), ap(s1), None, op0), [a, s1], out, holds=100)
+        elif op1 is None:
             add("v", lambda e: e.tensor_scalar(ap(out), ap(a), s1, None, op0), [a], out)
         else:
             add("v", lambda e: e.tensor_scalar(ap(out), ap(a), s1, s2, op0, op1), [a], out)
@@ -322,12 +340,6 @@ def rank_program(g, core, T, topo):
         else:
             add("s", lambda e: e.activation(ap(out), ap(a), ACT.Copy), [a], out)
 
-    def affine(out, a, scale, bias, func=ACT.Identity):
-        add("s", lambda e: e.activation(ap(out), ap(a), func, bias=float(bias), scale=float(scale)), [a], out)
-
-    def negate(out, a):
-        affine(out, a, -1, 0)
-
     def square(out, a):
         add("s", lambda e: e.activation(ap(out), ap(a), ACT.Square), [a], out)
 
@@ -337,11 +349,11 @@ def rank_program(g, core, T, topo):
     def mm(out, lhs, rhs, start, stop):
         add("t", lambda e: e.matmul(ap(out), ap(lhs), ap(rhs), start, stop), [lhs, rhs], out)
 
-    def select(out, src, pattern, base, after=()):
-        return add("g", lambda e: e.affine_select(ap(out), ap(src), pattern, ALU.is_equal, 0.0, base, 1), [src], out, after=after)
+    def select(out, src, pattern, base):
+        return add("g", lambda e: e.affine_select(ap(out), ap(src), pattern, ALU.is_equal, 0.0, base, 1), [src], out)
 
-    def count(out, pattern, base):
-        return add("g", lambda e: e.iota(ap(out), pattern, base, 0, allow_small_or_imprecise_dtypes=True), [], out)
+    def count(out, pattern, base, step=0):
+        return add("g", lambda e: e.iota(ap(out), pattern, base, step, allow_small_or_imprecise_dtypes=True), [], out)
 
     def clamp(out, a):
         ts(out, a, -0.25, ALU.max, 0.25, ALU.min)
@@ -352,27 +364,25 @@ def rank_program(g, core, T, topo):
     p7 = lambda lo, hi: vw("p7", lo, hi)
     ll = lambda lo, hi: vw("ll", lo, hi)
     eye = vw("eye", 0, 128)
-    cut = lambda v, k: vw(v[0], v[1] + 64 * k, v[1] + 64 * k + 64)
+    cut = lambda v, k: v if k is None else vw(v[0], v[1] + 64 * k, v[1] + 64 * k + 64)
+    quad = lambda q: (32 * q, 32 * q + 32)
+    both = (0, 64)
+    sel = lambda i: vw("sel", i * 128, i * 128 + 128, 1, both)
 
     def table_scatter(lo, hi, base):
-        ts((vw("tab", 0, V), vw("lu", lo, hi)), vw("ramp", 0, 16 * (hi - lo)), 1.0, ALU.mult, float(base - B0), ALU.add)
+        ts((vw("tab", 0, V), vw("lo", lo, hi)), vw("ramp", 0, 16 * (hi - lo)), 1.0, ALU.mult, float(base), ALU.add)
 
     def table_gather(at, lo, hi):
-        cp("v", vw("rv", at, at + 16 * (hi - lo)), (vw("tab", 0, V), vw("lu", lo, hi)))
+        cp("v", vw("rv", at, at + 16 * (hi - lo)), (vw("tab", 0, V), vw("lo", lo, hi)))
 
-    def to_lists(col, at, n, q="v", bank="p7"):
+    def to_lists(col, at, n, src="rv", mask="wv"):
         for a in range(16):
-            mm(vw(bank, col, col + n), vw("wv", 15 - a, 143 - a), vw("r" + q, at + a, at + 16 * n, 16), a == 0, a == 15)
-
-    OWN, JOINT = (0, 32), (32, 64)
-
-    def spread(out, block, name, parts):
-        return (out, vw("sel", block * 128, block * 128 + 128, 1, parts), vw(name, 0, 128, 1, parts))
+            mm(p7(col, col + n), vw(mask, 15 - a, 143 - a), vw(src, at + a, at + 16 * n, 16), a == 0, a == 15)
 
     def pieces(c, win, lst, drawn=False):
         def at(name, p, h, o=0):
-            if name in ("dd", "sq") and not drawn:
-                return vw(name, h * 384 + p * 128, h * 384 + p * 128 + 128)
+            if name in ("xb", "zb"):
+                name, o = "xz", p * S + (S if name == "zb" else 0)
             o += p * S
             return vw(name, o, o + S) if h is None else vw(name, o + h * 128, o + h * 128 + 128)
 
@@ -380,12 +390,11 @@ def rank_program(g, core, T, topo):
             o = lst[1] + 16 * z
             return (win(p), vw(lst[0], o, o + 16) if h is None else vw(lst[0], o + 8 * h, o + 8 * h + 8))
 
-        mcol = lambda p, h: at("p5", p, h) if p < 2 else at("p6", 0, h)
+        mcol = lambda p, h: at("p5", p, h) if p < 2 else at("p4", 1, h)
         to = lambda p, z, h: at("st%d" % p, 0, h, (A0, B0)[c] + z * S)
-        move = lambda p, h, sign: at("mw", 0, h, p * MW + 8 + sign * S)
         acc = lambda h: vw("p%d" % (2 + h), 0, 128)
         xx, zz, cc = ("xb", "zb", "cc") if drawn else ("xx", "zz", "p4")
-        diff = lambda p, h: at("dd", p, h) if not drawn else at("p1", p, h) if p < 2 else at("p0", 0, h)
+        diff = lambda p, h: at("dd", p, h) if not drawn else at(("p0", "p1", "p6")[p], 0, h)
 
         def d(p, h=None):
             if drawn:
@@ -400,344 +409,285 @@ def rank_program(g, core, T, topo):
             "W": lambda p, h=None: cp("v", at(xx, p, h), ends(p, 0, h)),
             "d": d,
             "q": lambda p, h=None: square(at("sq", p, h), diff(p, h)),
-            "Q": lambda p, h: square(vw("sq", h * 384 + p * 128, h * 384 + p * 128 + 256), vw("dd", h * 384 + p * 128, h * 384 + p * 128 + 256)),
-            "r": lambda h: mm(*spread(acc(h), 2 * c + h, "rn", OWN), not drawn, False),
-            "a": lambda p, h: mm(acc(h), eye, at("sq", p, h), drawn and p == 0, False),
+            "r": lambda h: mm(acc(h), sel(2 * c + h), vw("rn", 0, 128, 1, both), True, False),
+            "s": lambda p, h: tt(at("sq", p, h), diff(p, h), diff(p, h), ALU.mult),
+            "F": lambda h, k=None: tt(cut(at("p5", 1, h), k), cut(acc(h), k), cut(at("sq", 1, h), k), ALU.add),
+            "G": lambda h, k=None: tt(cut(at("p5", 0, h), k), cut(at("p5", 1, h), k), cut(at("sq", 2, h), k), ALU.add),
+            "Q": lambda: square(at("p5", 0, None), diff(0, None)),
+            "D": lambda: tt(at("p5", 1, None), at("p5", 0, None), at("sq", 1, None), ALU.add),
+            "K": lambda h: tt(at("p5", 0, h), at("p4", 0, h), at("uu", 0, h), ALU.add),
+            "L": lambda h: clamp(at(cc, 0, h), at("p5", 0, h)),
+            "E": lambda h: tt(at("p5", 0, h), at("p5", 1, h), at("sq", 2, h), ALU.add),
+            "a": lambda p, h: mm(acc(h), eye, at("sq", p, h), False, False),
             "e": lambda p, h: mm(acc(h), eye, at("sq", p, h), False, True),
-            "A": lambda h: tt(at("p4", 1, h), acc(h), at("sq", 2, h), ALU.add),
-            "U": lambda h: tt(at("uu", 0, h), at("p4", 1, h), at("kwo", c, h), ALU.mult),
             "u": lambda h: tt(at("uu", 0, h), acc(h), at("kwo", c, h), ALU.mult),
             "c": lambda h: clamp(at(cc, 0, h), at("uu", 0, h)),
-            "m": lambda p, h: tt(mcol(p, h), at(cc, 0, h), diff(p, h), ALU.mult),
+            "m": lambda p, h=None: tt(mcol(p, h), at(cc, 0, h), diff(p, h), ALU.mult),
             "x": lambda p, h=None: tt(to(p, 0, h), at(xx, p, h), mcol(p, h), ALU.add),
             "z": lambda p, h=None: tt(to(p, 1, h), at(zz, p, h), mcol(p, h), ALU.subtract),
-            "B": lambda h, k: tt(cut(at("p4", 1, h), k), cut(acc(h), k), cut(at("sq", 2, h), k), ALU.add),
-            "V": lambda h, k: tt(cut(at("uu", 0, h), k), cut(at("p4", 1, h), k), cut(at("kwo", c, h), k), ALU.mult),
-            "v": lambda h, k: tt(cut(at("uu", 0, h), k), cut(acc(h), k), cut(at("kwo", c, h), k), ALU.mult),
+            "B": lambda h, k: tt(cut(at("p5", 0, h), k), cut(acc(h), k), cut(at("sq", 2, h), k), ALU.add),
+            "V": lambda h, k=None: tt(cut(at("uu", 0, h), k), cut(at("p5", 0, h), k), cut(at("kwo", c, h), k), ALU.mult),
             "C": lambda h, k: clamp(cut(at(cc, 0, h), k), cut(at("uu", 0, h), k)),
-            "M": lambda p, h: tt(move(p, h, 0), at(cc, 0, h), diff(p, h), ALU.mult),
-            "N": lambda p, h=None: negate(move(p, h, 1), move(p, h, 0)),
-            "P": lambda p, h=None: cp("s", mcol(p, h), move(p, h, 0)),
         }
 
     def run(f, text, hooks=None):
         for w in text.split():
-            if w == ".":
-                if small:
-                    small.pop(0)()
-                    ops[-1]["stay"] = True
-                continue
             if w[0] == "@":
                 hooks[w[1:]]()
-                continue
-            if w[0] == "!":
-                hooks["!"](w[1:])
-                continue
-            f[w[0]](*[int(ch) if ch.isdigit() else "ab".index(ch) for ch in w[1:]])
+            else:
+                f[w[0]](*[int(ch) if ch.isdigit() else "ab".index(ch) for ch in w[1:]])
 
     def into(f, words):
         return {"n%d" % p: (lambda text: lambda: run(f, text))(words[p]) for p in range(3)}
 
-    sent = [0]
+    def half(name, p, h, o=0, width=384):
+        o += p * width + h * 192
+        return vw(name, o, o + 192)
 
-    def send(t, last):
-        slot, o, dcore = last, t * 1152 + last * 384, T.cores[part[last]]
-        groups, n = [], 0
-        for lo, hi, to, engines, sem in pieces_of(T, topo, rank, t)[slot]:
-            rid, pid = topo.addr(to, core)
-            tr = RemoteDMATransfer(dst_ids=[DstId(rid=rid, pnc=pid)], dma_engine_mask=bits(engines),
-                                   remote_sem=T.sem["ar%d" % (3 * t + slot) if to == dcore else sem],
-                                   src=T.sb[:, o + lo:o + hi], dst=T.ld[:, o + lo:o + hi])
-            if groups and groups[-1][0] == hi - lo == 192 and not set(groups[-1][1]) & set(engines):
-                groups[-1] = (hi - lo, groups[-1][1] + engines, groups[-1][2] + [tr], groups[-1][3] + [vw("sb", o + lo, o + hi)])
-            else:
-                groups.append((hi - lo, engines, [tr], [vw("sb", o + lo, o + hi)]))
-            sent[0] += len(engines)
-            n += len(engines) if to == dcore else len(topo.engines(to, dcore))
-        for _, _, trs, srcs in groups:
-            call = add("g", (lambda l: lambda e: e.remote_dma_fused(l, local_sem=T.sem.sent))(trs), srcs, None, ("sent", 0),
-                       holds=ISSUE)
-            ops[-1]["soft"] = []
-        add(None, None, [], vw("ld", o, o + 384), ("ar%d" % (3 * t + slot), n), soft=[call], holds=WRITE[slot] + (COLD if t == 0 else 0))
-        if slot == 1:
-            floor[:] = [call]
+    bank = lambda p, h: half(("p0", "p1", "p6")[p], 0, h)
+    near = lambda p: half("p7", 0, p) if p < 2 else half(NEAR, 0, 0)
+    part = lambda v, k, n=96: vw(v[0], v[1] + n * k, v[1] + n * k + n)
 
-    def sends(t):
-        def border(q, slot, p):
-            o = t * 1152 + slot * 384 + p * 128
-            cp(q, vw("sb", o, o + 128), (st(p, J0, WIN), ll(32 + 8 * slot, 40 + 8 * slot)))
-        return into({"G": lambda slot, p: border("s", slot, p), "H": lambda slot, p: border("v", slot, p),
-                     "s": lambda slot: send(t, slot)}, SENDS[t])
+    def border(q, p, lo, hi):
+        cp(q, vw("gb", p * 384 + lo * 192, p * 384 + hi * 192), (st(p, J0, WIN), ll(32 + 12 * lo, 32 + 12 * hi)))
 
-    def moves(t, f):
-        def before(q, p, lo, hi):
-            cp(q, vw("pb", p * 384 + lo * 128, p * 384 + hi * 128), (st(p, J0, WIN), ll(176 + 8 * lo, 176 + 8 * hi)))
+    def across(out, src):
+        for s in range(3):
+            mm(part(out, s, 64), vw("qq", s * 128, s * 128 + 128), part(src, s, 64), True, True)
 
-        def border(slot, p):
-            o, b = t * 1152 + slot * 384 + p * 128, p * 384 + slot * 128
-            tt(vw("sb", o, o + 128), (vw("mw", p * MW, (p + 1) * MW), ll(152 + 8 * slot, 160 + 8 * slot)),
-               vw("pb", b, b + 128), ALU.add)
-        return dict(f, E=lambda p, lo, hi: before("s", p, lo, hi), F=lambda p, lo, hi: before("v", p, lo, hi),
-                    b=border, s=lambda slot: send(t, slot))
+    wcol = lambda name, p: vw(name, p * 128, p * 128 + 128)
+    sj = lambda p: half("sj", p, 0)
+    joint = {
+        "g": lambda p: border("s", p, 0, 1), "t": lambda p: border("s", p, 1, 2),
+        "H": lambda p: border("v", p, 0, 1), "T": lambda p: border("v", p, 1, 2),
+        "P": lambda p: across(bank(p, 0), half("gb", p, 1)),
+        "D": lambda p: tt(half("dj", p, 0), half("gb", p, 0), bank(p, 0), ALU.subtract),
+        "d": lambda k: tt(part(half("dj", 2, 0), k), part(half("gb", 2, 0), k), part(bank(2, 0), k), ALU.subtract),
+        "q": lambda p: square(sj(p), half("dj", p, 0)),
+        "s": lambda k: tt(part(sj(2), k), part(half("dj", 2, 0), k), part(half("dj", 2, 0), k), ALU.mult),
+        "S": lambda k: square(part(sj(2), k), part(half("dj", 2, 0), k)),
+        "A": lambda p: tt(half("p5", 0, p), half("p2", 0, 1, 128) if p == 0 else half("p5", 0, 0), sj(p), ALU.add),
+        "o": lambda p: cp("s", near(p), half("gb", p, 0)),
+        "B": lambda k: tt(part(half("cc", 0, 0), k), part(half("p5", 0, 1), k), part(sj(2), k), ALU.add),
+        "V": lambda k: tt(part(half("uu", 0, 0), k), part(half("p2", 0, 0, 128), k), part(half("cc", 0, 0), k), ALU.mult),
+        "C": lambda k: clamp(part(half("p4", 0, 1), k), part(half("uu", 0, 0), k)),
+        "m": lambda p: tt(half("dj", p, 1), half("p4", 0, 1), half("dj", p, 0), ALU.mult),
+        "R": lambda p: across(bank(p, 1), half("dj", p, 1)),
+        "x": lambda p: tt(st(p, J0, J0 + 192), near(p), half("dj", p, 1), ALU.add),
+        "z": lambda p: tt(st(p, J0 + 192, B0), half("gb", p, 1), bank(p, 1), ALU.subtract),
+    }
+    last = {"w": lambda p: cp("s", wcol("yb", p), (st(p, 0, WIN), ll(120, 128))),
+            "u": lambda p: cp("v", wcol("yb", p), (st(p, 0, WIN), ll(120, 128)))}
 
-    xbank = ("p3", "p0", "p1")
+    calls_at, issued = {}, []
 
-    def own_side(t, slot):
-        o = t * 1152 + slot * 384
-        if slot in BYPE[t]:
-            mm(vw(xbank[slot], 0, 384), eye, vw("sb", o, o + 384), True, True)
-        else:
-            cp("s", vw(xbank[slot], 0, 384), vw("sb", o, o + 384))
+    def issue(names, trs, reads, engines):
+        sem = "out%d" % len(issued)
+        issued.append(len(ops))
+        n = add("g", lambda e: e.remote_dma_fused(trs, local_sem=T.sem[sem]), reads, None, (sem, engines), holds=ISSUE, takes=1800)
+        ops[-1]["behind"] = issued[-2:-1]
+        calls_at.update({name: n for name in names})
 
-    def joint(t, between, rest, done):
-        col = lambda name, p, b: vw(name, b + p * 128, b + p * 128 + 128)
-        acc = lambda slot: vw(("p2", ("p6", "p7")[t], "p2")[slot], 256, 384)
+    def send(first, again=0):
+        if first == "k":
+            legs = first_call(T, topo, rank)
+            return issue(["k"], [transfer(T, topo, core, to, es, "kar%d" % part if to in T.cores else "rin0", T.tk[8 * part + q],
+                                          T.tk[8 * part + 4 + rank]) for q, part, to, es in legs], [], len(legs))
+        call = [c for c in calls_of(T, topo, rank) if c[0][0] == first][again]
+        trs = []
+        for name, to, es, direct in call:
+            src, k = ap(vw(*TILES[name])), NAMES.index(name)
+            if es:
+                trs.append(transfer(T, topo, core, to, es, "rin%d" % k, src, T["t" + name][rank] if name in WHOLE else T["u" + name][:]))
+            if direct:
+                trs.append(transfer(T, topo, core, T.cores[others[2]], direct, "ar%d" % k, src, T["t" + name][rank]))
+        issue([c[0] for c in call], trs, [vw(*TILES[c[0]]) for c in call], sum(len(c[2]) + len(c[3]) for c in call))
 
-        def differ(slot, p):
-            tt(col("dj", p, slot * 384), col(xbank[slot], p, 0), col("ld", p, t * 1152 + slot * 384), ALU.subtract)
-            square(col("sj", p, slot * 384), col("dj", p, slot * 384))
+    def landed(name):
+        n = sum(len(direct) * (ways(T, topo, q)[0][2] == rank) + (len(onward(T, topo, q, to, name).get(rank, [])) if es else 0)
+                for q in others for c in calls_of(T, topo, q) for w, to, es, direct in c if w == name)
+        come = add(None, None, [], None, ("ar%d" % NAMES.index(name), n), holds=WAY.get(name.upper(), TURN))
+        ops[-1]["behind"] = [calls_at[name]]
+        t = T["t" + name]
+        return [(lo, hi, t[lo:hi, 32 * rank:32 * rank + 32, :] if name in WHOLE else t[4 + lo:4 + hi], come)
+                for lo, hi in ((0, rank), (rank + 1, 4)) if lo < hi]
 
-        def x(slot, p):
-            tt(st(p, J0 + slot * 128, J0 + slot * 128 + 128), col("sb", p, t * 1152 + slot * 384), col("p4", p, 0), ALU.add)
-            if slot == 2:
-                done(p)
+    mine_first = lambda s: (0, 1) if rank < rank ^ s else (1, 0)
+    staged = [dma("s", T.tk[8 * (k // 2):8 * (k // 2) + 4, 64 * (k % 2):64 * (k % 2) + 64, :], src[:, :], 100)
+              for k, src in enumerate((T.inv, T.stiff, T.jinv, T.jstiff))]
+    dma("s", vw("li", 0, 64), T.ends[:, :], 200)
+    for p in range(3):
+        dma("y", pos(p), T.pos[:, p * V:(p + 1) * V], LOAD * (p + 1))
+    dma("y", vw("li", 72, 104), T.bord[:, :], 3 * LOAD + 200)
+    dma("y", vw("li", 64, 72), T.watch[:, :], 3 * LOAD + 400)
+    together(2)
+    send("k")
+    ops[-1]["after"] += staged
 
-        def wide(slot, lo, hi):
-            w = lambda name, b: vw(name, b + lo * 128, b + hi * 128)
-            tt(w("dj", slot * 384), w(xbank[slot], 0), w("ld", t * 1152 + slot * 384), ALU.subtract)
-            square(w("sj", slot * 384), w("dj", slot * 384))
-
-        run({"d": differ, "x": x, "D": wide,
-             "B": lambda slot, k: tt(cut(col("p4", 2, 0), k), cut(col("p4", 1, 0), k), cut(col("sj", 2, slot * 384), k), ALU.add),
-             "V": lambda slot, k: tt(cut(vw("uu", 0, 128), k), cut(col("p4", 2, 0), k), cut(col("kwj", slot, 8), k), ALU.mult),
-             "v": lambda slot, k: tt(cut(vw("uu", 0, 128), k), cut(acc(slot), k), cut(col("kwj", slot, 8), k), ALU.mult),
-             "C": lambda slot, k: clamp(cut(vw("p4", 384, 512), k), cut(vw("uu", 0, 128), k)),
-             "r": lambda slot: mm(*spread(acc(slot), part[slot], "rn", JOINT), True, False),
-             "R": lambda slot: mm(*spread(acc(slot), part[slot], "rn", JOINT), True, True),
-             "a": lambda slot, p: mm(acc(slot), eye, col("sj", p, slot * 384), False, False),
-             "e": lambda slot, p: mm(acc(slot), eye, col("sj", p, slot * 384), False, True),
-             "s": lambda slot, p: tt(col("p4", p, 0), acc(slot), col("sj", p, slot * 384), ALU.add),
-             "S": lambda slot, p: tt(col("p4", p, 0), col("p4", p - 1, 0), col("sj", p, slot * 384), ALU.add),
-             "u": lambda slot: tt(vw("uu", 0, 128), acc(slot), col("kwj", slot, 8), ALU.mult),
-             "U": lambda slot: tt(vw("uu", 0, 128), col("p4", 2, 0), col("kwj", slot, 8), ALU.mult),
-             "c": lambda slot: clamp(vw("p4", 384, 512), vw("uu", 0, 128)),
-             "m": lambda slot, p: tt(col("p4", p, 0), vw("p4", 384, 512), col("dj", p, slot * 384), ALU.mult)},
-            JOINTS, {"": between, "!": rest, "1": scalar_lists if t == 0 else lambda: None, "2": scalar_lists2 if t == 0 else lambda: None})
-
-    both, one = (0, 64), (0, 1)
-    load("y", vw("li", 0, 64), T.ends[:, :])
-    load("s", vw("wc", 0, 128, 1, OWN), T.inv[:, :])
-    load("y", vw("wc", 0, 128, 1, JOINT), T.jinv[:, :])
-    load("s", vw("kc", 0, 128, 1, OWN), T.stiff[:, :])
-    load("s", vw("kc", 0, 128, 1, JOINT), T.jstiff[:, :])
-    for w in LOADS.split():
-        if w == "b":
-            for s in range(3):
-                load("y", vw("li", 72 + 8 * s, 80 + 8 * s), T.bord[:, 8 * part[s]:8 * part[s] + 8])
-        elif w == "w":
-            load("y", vw("li", 64, 72), T.watch[:, :])
-        else:
-            load("y", pos(int(w)), T.pos[:, int(w) * V:(int(w) + 1) * V])
-    fill(vw("ones", 0, 128), 1.0)
-    count(vw("ramp", 0, 512), [[1, 512]], B0)
+    fill(vw("tab", 0, 512), 0.0)
     fill(vw("oneb", 0, 144), 1.0)
-    fill(vw("oneb", 144, 272), -1.0)
-    fill(vw("tab", 0, ZERO), 0.0)
-    fill(vw("tab", ZERO, V - ZERO), 0.0)
-    cp("s", vw("tab", V - ZERO, V), vw("tab", 0, ZERO))
-    for a in range(4):
-        select(vw("sel", a * 128, a * 128 + 128, 1, OWN), vw("ones", 0, 128, 1, OWN), [[-4, 8], [0, 16]], -a)
-    for k in (0, 1):
-        select(vw("eyeb", k * 128, k * 128 + 128), vw("oneb", k * 144, k * 144 + 128), [[-1, 128]], 0)
+    fill(vw("tab", 512, 1280), 0.0)
+    cp("s", vw("tab", 1280, 1792), vw("tab", 0, 512))
+    cp("s", vw("tab", 1792, 2048), vw("tab", 0, 256))
+    count(vw("ramp", 0, 512), [[1, 512]], 0)
+    cp("v", vw("lo", 0, 64), vw("li", 0, 64))
+    kept = dma("s", T.tk[4 + rank:16:8], T.tk[rank:16:8], 0)
+    ops[-1]["after"] += staged
+    ops[-1]["stay"] = False
+    count(vw("ki", 0, 2), [[0, 2]], 0, 1)
+    count(sm(64, 96), [[16, 32]], 0)
     select(vw("wv", 0, 144), vw("oneb", 0, 144), [[-16, 9], [256, 16]], -15 * 256)
-    count(vw("row", 0, 128, 1, one), [[0, 8], [1, 16]], 0)
-    count(vw("row", 128, 160, 1, one), [[16, 32]], B0)
-    select(eye, vw("ones", 0, 128), [[-1, 128]], 0)
-    for name in ("kwj", "rj"):
-        last = count(vw(name, 0, 8), [[0, 8]], 0)
-    for p in range(3 if len(PLAIN) < 3 else 0):
-        count(vw("aw", 0, 8), [[0, 8]], 0)
-        count(vw("aw", 520, MW), [[1, 512]], A0)
-        count(vw("mw", p * MW, p * MW + 8), [[0, 8]], 0)
-        last = count(vw("mw", p * MW + 520, (p + 1) * MW), [[0, 512]], 0)
-    for a in range(4):
-        select(vw("sel", a * 128, a * 128 + 128, 1, JOINT), vw("ones", 0, 128, 1, JOINT), [[-4, 8], [0, 16]], -a, [last])
-    cp("v", vw("lu", 0, 64), vw("li", 0, 64))
-    wn, wc, rn = (vw(n, 0, 128, 1, both) for n in ("wn", "wc", "rn"))
-    if WN == "s":
-        add("s", lambda e: e.activation(ap(wn), ap(wc), ACT.Identity, bias=-EPS, scale=-1.0), [wc], wn)
-    else:
-        ts(wn, wc, -1.0, ALU.mult, -EPS, ALU.add)
 
-    def product():
-        tt(vw("kn", 0, 128, 1, both), vw("kc", 0, 128, 1, both), wn, ALU.mult)
-        for a in range(4):
-            mm(*spread(vw("p0", a * 128, a * 128 + 128), a, "kn", OWN), True, True)
+    def drawn(words):
+        for w in words.split():
+            p = int(w[1])
+            name, o, col = {"x": ("xz", p * 512, 0), "B": ("st%d" % p, B0, 32), "J": ("st%d" % p, W0, 64)}[w[0]]
+            for lo, hi in ((0, 16), (16, 32)) if w in ("B0", "x2") else ((0, 32),):
+                cp("v" if (w, lo) == ("x2", 0) else "s", vw(name, o + 16 * lo, o + 16 * hi), (pos(p), vw("lo", col + lo, col + hi)))
 
-    def first_list():
-        to_lists(0, 0, 32, "s" if "@G1" in FIRST else "v")
-        mm(p7(32, 64), vw("row", 0, 128, 1, one), vw("oneb", 0, 32, 1, one), True, False)
-        mm(p7(32, 64), vw("oneb", 0, 128, 1, one), vw("row", 128, 160, 1, one), False, True)
+    table_scatter(0, 32, A0)
+    table_gather(0, 32, 64)
+    fill(vw("oneb", 144, 272), -1.0)
+    to_lists(0, 0, 32)
+    ts(vw("ki", 4, 6), vw("ki", 0, 2), 15, ALU.bitwise_and)
+    cp("v", sm(96, 98), vw("ki", 4, 6))
+    ts(sm(128, 160), sm(64, 96), sm(96, 97), ALU.add)
+    ts(sm(0, 32), sm(128, 160), float(B0), ALU.add)
+    ts(sm(32, 56), sm(128, 152), float(J0), ALU.add)
+    drawn("x0 x1 x2")
+    tt(sm(64, 96), p7(0, 32), sm(0, 32), ALU.max)
+    cp("v", sm(200, 232), p7(0, 32))
+    ts(ll(0, 32), sm(64, 96), float(B0), ALU.subtract)
+    for s in (1, 2, 3):
+        for k, h in enumerate(mine_first(s)):
+            o = 72 + 8 * (rank ^ s) + 4 * h
+            cp("v", vw("lo", 68 + 12 * k + 4 * s, 72 + 12 * k + 4 * s), vw("li", o, o + 4))
+    cp("v", vw("lo", 64, 72), vw("li", 64, 72))
+    drawn("B0 B1 B2 J0 J1 J2")
+    table_scatter(32, 64, B0)
+    table_gather(640, 72, 96)
+    to_lists(40, 640, 24)
+    table_scatter(72, 96, J0)
+    tt(sm(96, 120), p7(40, 64), sm(32, 56), ALU.max)
+    ts(ll(32, 56), sm(96, 120), float(J0), ALU.subtract)
+    for call in CALLS.split()[1:-8]:
+        send(call[:2], call[3] == "d")
+    fresh = []
 
-    def first_places():
-        if "@G1" in FIRST:
-            affine(sm(0, 32), p7(0, 32), 1, 1280)
-            cp("s", sm(32, 64), p7(32, 64))
-        else:
-            cp("s", sm(0, 64), p7(0, 64))
-        small.extend([lambda: tt(sm(64, 96), sm(0, 32), sm(32, 64), ALU.max),
-                      lambda: ts(ll(0, 32), sm(64, 96), float(B0), ALU.subtract),
-                      lambda: ts(sm(96, 120), sm(32, 56), float(J0 - B0), ALU.add)])
+    count(sm(168, 200), [[0, 32]], 0)
 
-    def border_list():
-        small.extend([lambda: tt(sm(120, 144), p7(72, 96), sm(96, 120), ALU.max),
-                      lambda: ts(ll(32, 56), sm(120, 144), float(J0), ALU.subtract)])
-
-    def later_lists():
-        small.append(lambda: ts(ll(56, 88), p7(96, 128), float(J0), ALU.subtract))
-
-    def scalar_lists():
-        affine(vw("rs", 0, 512), (vw("tab", 0, V), vw("lu", 32, 64)), 1, -384)
-        ops[-1]["stay"] = STAY[0]
-
-    def scalar_lists2():
-        if len(PLAIN) == 3:
-            return to_lists(0, 0, 32, "s", "p5")
-        affine(vw("rs", 512, 1024), (vw("aw", 0, MW), ll(144, 176)), 1, -1280)
-        ops[-1]["stay"] = STAY[1]
-        to_lists(0, 0, 64, "s", "p5")
+    def lookups():
+        for lo in range(0, 72, 12):
+            cp("s", vw("rf", 16 * lo, 16 * lo + 192), (vw("tab", 0, V), vw("lo", lo, lo + 12)))
+        for lo in (0, 384, 768):
+            src, out = vw("rf", lo, lo + 384), vw("rv", 1024 + lo, 1408 + lo)
+            add("g", (lambda out, src: lambda e: e.affine_select(ap(out), ap(src), [[0, 384]], ALU.is_equal, 0.0, 0, 0))(out, src), [src], out)
 
     def last_lists():
-        affine(sm(176, 208), vw("p5", 0, 32), 1, 384)
+        to_lists(64, 1024, 72)
+        ops[-16]["stay"] = True
+        tt(sm(0, 72), p7(64, 136), sm(168, 240), ALU.max)
+        cp("v", ll(56, 128), sm(0, 72))
+        send("md")
+        land("md")
+
+    for k in (0, 1):
+        select(vw("eyeb", k * 128, k * 128 + 128), vw("oneb", k * 144, k * 144 + 128), [[-1, 128]], 0)
+    for i in range(4):
+        select(vw("selb", i * 128, i * 128 + 128, 1, both), vw("oneb", 0, 128, 1, both), [[-4, 8], [0, 16]], -i)
+    for part_ in (0, 1):
+        come = add(None, None, [], None, ("kar%d" % part_, len(others)), holds=WAY["K"])
+        ops[-1]["behind"] = [calls_at["k"]]
+        for k, name in enumerate(("wc", "kc")):
+            dma("y", vw(name, 0, 128, 1, quad(part_)), T.tk[8 * part_ + 4:8 * part_ + 8, 64 * k:64 * k + 64, :], 100)
+            ops[-1]["after"] += [come, kept]
+            ops[-1]["stay"] = False
+    for c in (0, 1):
+        for bank_, name in ((("p3", "p2")[c], "wc"), (("p4", "p2")[c], "kc")):
+            for a in (c * S, c * S + 128):
+                o = a % S if name == "wc" else a
+                mm(vw(bank_, o, o + 128), vw("selb", a, a + 128, 1, quad(0)), vw(name, 0, 128, 1, quad(0)), True, True)
+    wn, wc, rn, kn = (vw(n, 0, 128, 1, both) for n in ("wn", "wc", "rn", "kn"))
+    add("s", lambda e: e.activation(ap(wn), ap(wc), ACT.Identity, bias=-EPS, scale=-1.0), [wc], wn)
+
+    def own_constants(c):
+        w, k, t, out = vw(("p3", "p2")[c], 0, S), vw(("p4", "p2")[c], c * S, c * S + S), vw("zz", c * S, c * S + S), vw("kwo", c * S, c * S + S)
+        add("s", lambda e: e.activation(ap(t), ap(w), ACT.Identity, bias=-EPS, scale=-1.0), [w], t)
+        tt(out, k, t, ALU.mult)
+
+    add("v", lambda e: e.reciprocal(ap(rn), ap(wn)), [wn], rn, holds=200 + 6 * 128)
+    own_constants(0)
+    own_constants(1)
+    cp("s", sm(232, 240), sm(128, 136))
+
+    def joint_product():
+        tt(kn, vw("kc", 0, 128, 1, both), wn, ALU.mult)
         ops[-1]["stay"] = True
-        affine(sm(208, 240), vw("p5", 0, 32), 16, -127 * 16, ACT.Relu)
-        small.extend([lambda: tt(sm(240, 272), sm(176, 208), sm(208, 240), ALU.add),
-                      lambda: tt(sm(328, 360), sm(240, 272), sm(32, 64), ALU.min),
-                      lambda: tt(sm(144, 176), sm(328, 360), sm(0, 32), ALU.max),
-                      lambda: ts(ll(88, 120), sm(144, 176), float(J0), ALU.subtract)])
-        if len(PLAIN) == 3:
-            return
-        affine(sm(272, 304), vw("p5", 32, 64), 1, 1280)
-        small.extend([lambda: tt(sm(304, 328), sm(280, 304), sm(96, 120), ALU.max),
-                      lambda: ts(ll(176, 200), sm(304, 328), float(J0), ALU.subtract)])
 
-    def start(p, region, n, col, q="s"):
-        cp(q, st(p, region, region + 16 * n), (pos(p), vw("lu", col, col + n)))
+    def late_masks():
+        for i in (2, 3):
+            select(sel(i), vw("oneb", 0, 128, 1, both), [[-4, 8], [0, 16]], -i)
+        select(eye, vw("oneb", 0, 128), [[-1, 128]], 0)
+        for s in (1, 2, 3):
+            for h in (0, 1):
+                for b in (0, 2):
+                    row = [32 + 8 * q + (q ^ s) + 1000 * ((q > q ^ s) != h) for q in (b, b + 1)]
+                    o = (2 + 2 * s + h) * 128 + 32 * b
+                    select(vw("sel", o, o + 64, 1, both), vw("oneb", 0, 64, 1, both), [[row[0] - row[1], 2], [-4, 2], [0, 16]], -row[0])
 
-    hooks = {
-        "sA": lambda: table_scatter(0, 32, A0), "sB": lambda: table_scatter(32, 64, B0),
-        "g1": lambda: table_gather(0, 32, 64), "g2": lambda: table_gather(512, 64, 96),
-        "G2": lambda: table_gather(512, 64, 96, "s"), "T2": lambda: to_lists(64, 512, 32, "s"),
-        "+": lambda: floor.append(len(ops) - 1), "-": floor.clear,
-        "g3": lambda: table_gather(640, 72, 96), "t3": lambda: to_lists(72, 640, 24),
-        "G1": lambda: affine(vw("rs", 0, 512), (vw("tab", 0, V), vw("lu", 32, 64)), 1, -1280),
-        "t1": first_list, "t2": lambda: to_lists(64, 512, 32), "l1": first_places, "bl": border_list,
-        "kn": product, "kw": lambda: cp("s", vw("kwo", 0, 512), vw("p0", 0, 512)),
-        "rn": lambda: add("v", lambda e: e.reciprocal(ap(rn), ap(wn)), [wn], rn, holds=200 + 6 * 128),
-        "ol": lambda: cp("v", vw("lu", 64, 96), vw("li", 64, 96)),
-    }
-    for p in range(3):
-        for q in "sv":
-            hooks["BC"[q == "v"] + str(p)] = (lambda p, q: lambda: start(p, B0, 32, 32, q))(p, q)
-            hooks["JK"[q == "v"] + str(p)] = (lambda p, q: lambda: start(p, J0, 24, 72, q))(p, q)
+    def last_masks():
+        for s in (1, 2, 3):
+            select(vw("qq", s * 128 - 128, s * 128), vw("oneb", 0, 128), [[128 * (s >> 1) - 64, 2], [64 * (s & 1) - 32, 2], [-1, 32]], -32 * s)
+        for i in (0, 1):
+            select(sel(i), vw("oneb", 0, 128, 1, both), [[-4, 8], [0, 16]], -i)
 
-    c0 = pieces(0, pos, ("lu", 0), True)
+    def land(names):
+        for name in names.replace(",", " ").split():
+            runs = landed(name)
+            for lo, hi, src, come in runs:
+                dma("y", vw(*TILES[name], 1, (32 * lo, 32 * hi)), src, 300)
+                ops[-1]["after"].append(come)
+                if name == "Z2":
+                    fresh.append(len(ops) - 1)
+            together(len(runs))
+
+    land(LANDS)
+
+    def late_gathers():
+        send("J0")
+        ops[-1]["after"] += fresh
+        send("J1")
+        send("J2")
+        land("J0,j0 J1,j1 J2,j2")
+        late_masks()
+
+    def joint_constants(k, name):
+        for s in (1, 2, 3):
+            for h in (0, 1):
+                mm(part(half("p2", 0, k, 128), s - 1, 64), sel(2 + 2 * s + h), vw(name, 64 * h, 64 * h + 64, 1, both), h == 0, h == 1)
+
+    hooks = {"jr": lambda: joint_constants(1, "rn"), "jk": lambda: joint_constants(0, "kn"),
+             "j2": late_gathers, "lk": lambda: (lookups(), last_masks()), "ll": last_lists, "kn": joint_product}
+
+    c0 = pieces(0, None, None, True)
     c1 = pieces(1, lambda p: st(p, B0, WIN), ("ll", 0))
-    run(c0, FIRST + FTAIL, dict(hooks, **into(c1, PRE)))
+    run(c0, FIRST, dict(hooks, **into(c1, PRE)))
     for t in range(SWEEPS):
         if t > 0:
-            run(c0, JHEAD)
-            if t == 1:
-                last_lists()
-            run(c0, TAIL, into(c1, PRE))
-        if t in PLAIN:
-            run(c1, HEAD + (SECOND + " " if t == 0 else "") + TAIL, dict(hooks, **sends(t)))
-        else:
-            run(moves(t, c1), HEAD + MOVES[t])
-        if t == SWEEPS - 1:
-            break
-        if t == 0 and len(PLAIN) < 3:
-            mm(vw("p5", 0, 512), vw("eyeb", 0, 128), vw("rv", 0, 512), True, True)
-            cp("s", vw("aw", 8, 520), vw("p5", 0, 512))
-        if t == 0:
-            if "@g3" in FIRST + SECOND:
-                table_gather(512, 64, 72)
-                to_lists(64, 512, 8)
-            for s in range(3):
-                mm(*spread(vw("p0", s * 128, s * 128 + 128), part[s], "kn", JOINT), True, True)
-            table_scatter(72, 96, J0)
-        if t in PLAIN:
-            own_side(t, 0)
-        if t == 0:
-            cp("s", vw("kwj", 8, 392), vw("p0", 0, 384))
-            own_side(t, 1)
-            if len(PLAIN) < 3:
-                ts(ll(144, 176), p7(64, 96), float(B0 - 8), ALU.subtract, 0.0, ALU.max)
-            table_gather(1024, 0, 32)
-            table_gather(1536, 64, 72)
-            to_lists(96, 1024, 40)
-            own_side(t, 2)
-        elif t in PLAIN:
-            own_side(t, 1)
-            own_side(t, 2)
-        else:
-            run(dict(c1, o=lambda slot: own_side(t, slot)), SHADE)
-        c0 = pieces(0, lambda p: st(p, J0, WIN), ("ll", 56))
+            run(c0, JHEAD + TAIL, into(c1, PRE))
+        run(c1, HEAD + ("@kn " + TAIL.replace("m0a", "@ll @jk m0a") if t == 0 else TAIL), dict(hooks, **into(joint, BORDER)))
+        c0 = pieces(0, lambda p: st(p, 0, WIN), ("ll", 56))
+        c1 = pieces(1, lambda p: st(p, 0, WIN), ("ll", 88))
+        run(joint, JOINT, into(c0, JPRE) if t < SWEEPS - 1 else into(last, LAST))
 
-        def rest(w):
-            if t not in PLAIN:
-                run(dict(c1, o=lambda slot: own_side(t, slot)), w)
-                ops[-1]["stay"] = True
-        joint(t, later_lists if t == 0 else (lambda: None), rest, lambda p: run(c0, JPRE[p]))
-        c1 = pieces(1, lambda p: st(p, J0, WIN), ("ll", 88))
-
-    for s in range(3):
-        mm(*spread(vw("p1", s * 128, s * 128 + 128), part[s], "rn", JOINT), True, True)
-    cp("s", vw("rj", 8, 392), vw("p1", 0, 384))
-    for p in range(3):
-        start(p, W0, 8, 64)
-    late = p7(128, 136)
-    ts(sm(64, 72), sm(32, 40), float(W0 - B0), ALU.add)
-    ts(sm(72, 80), late, float(B0), ALU.is_lt)
-    tt(sm(80, 88), p7(64, 72) if 2 in PLAIN else sm(272, 280), sm(64, 72), ALU.max)
-    tt(sm(96, 104), late, sm(72, 80), ALU.mult)
-    tt(sm(88, 96), late, sm(80, 88), ALU.max)
-    ts(ll(128, 136), sm(96, 104), float(J0 - 8), ALU.subtract, 0.0, ALU.max)
-    cp("v", ll(120, 128), sm(88, 96))
-    ts(sm(104, 112), sm(96, 104), float(J0), ALU.subtract, 0.0, ALU.max)
-    ts(sm(112, 120), sm(96, 104), float(J0 + 128), ALU.is_ge, 256.0, ALU.mult)
-    ts(sm(120, 128), sm(96, 104), float(J0 + 256), ALU.is_ge, 256.0, ALU.mult)
-    tt(sm(128, 136), sm(104, 112), sm(112, 120), ALU.add)
-    tt(sm(136, 144), sm(128, 136), sm(120, 128), ALU.add)
-    cp("v", ll(136, 144), sm(136, 144))
-
-    o = (SWEEPS - 1) * 1152
-    col = lambda name, p: vw(name, p * 128, p * 128 + 128)
-    cp("v", vw("rw", 0, 128), (vw("rj", 0, 392), ll(128, 136)))
-    cp("v", vw("kww", 0, 128), (vw("kwj", 0, 392), ll(128, 136)))
-    for p in range(3):
-        cp("s", col("xx" if 2 in PLAIN else "zz", p), (st(p, 0, WIN), ll(120, 128)))
-        if 2 not in PLAIN:
-            tt(col("xx", p), (vw("mw", p * MW, (p + 1) * MW), ll(144, 152)), col("zz", p), ALU.add)
-    cp("v", vw("p2", 0, 128), vw("rw", 0, 128))
-    for p in range(3):
-        tt(col("dj", p), (vw("ld", o + p * 128, o + p * 128 + 896), ll(136, 144)), col("xx", p), ALU.subtract)
-        square(col("sj", p), col("dj", p))
-    tt(vw("p4", 0, 128), vw("p2", 0, 128), col("sj", 0), ALU.add)
-    tt(vw("p4", 128, 256), vw("p4", 0, 128), col("sj", 1), ALU.add)
-    half = lambda name, o, h: vw(name, o + 64 * h, o + 64 * h + 64)
-    for h in (0, 1):
-        tt(half("p4", 256, h), half("p4", 128, h), half("sj", 256, h), ALU.add)
-    for h in (0, 1):
-        tt(half("uu", 0, h), half("p4", 256, h), half("kww", 0, h), ALU.mult)
-    for h in (0, 1):
-        clamp(half("p4", 384, h), half("uu", 0, h))
-    m = lambda p: tt(col("p5", p), vw("p4", 384, 512), col("dj", p), ALU.mult)
-    x = lambda p: tt(col("yb", p), col("xx", p), col("p5", p), ALU.subtract)
-    m(0); m(1); x(0); m(2); x(1); x(2)
-    done = [store(q, T.y[:, lo:hi], vw("yb", lo, hi), "d%d" % (12 + k)) for k, (q, lo, hi) in enumerate(STORES)]
-    stored = done[-1]
+    for name in ("y0", "y1", "y2"):
+        send(name)
+    send("y2", 1)
+    done = [dma("s", T.y[32 * rank:32 * rank + 32, :], vw("yb", 0, 384, 1, quad(rank)), 0)]
+    for i, name in enumerate(("y0", "y1", "y2", "y3")):
+        for k, (lo, hi, src, come) in enumerate(landed(name)):
+            done.append(dma("ys"[i % 2], T.y[32 * lo:32 * hi, TILES[name][1]:TILES[name][2]], src, 200))
+            ops[-1]["after"].append(come)
     add("y", None, [], None, after=done, holds=1)
-    total = add(None, None, [], None, ("sent", sent[0]), soft=[stored], holds=1)
-    add("g", None, [], None, after=[total], holds=1)
+    add("g", None, [], None, after=issued, soft=done, holds=1)
     emit(g, T, arrange(ops))

@@ -6,20 +6,27 @@ W0, J0, B0, A0, WIN = 0, 128, 512, 1024, 1536
 EPS = 1e-22
 SWEEPS = 3
 F = "float32"
+THEIRS = (0, 96)
 GATHER, SCATTER, MATMUL, FIXED, HOP, SELF = 1.56, 3.8, 3, {"v": 30, "s": 140}, 170, 60
 DMA, ISSUE, LOAD, TURN = 1150, 250, 1330, 3900
-TILES = {"mc": ("ll", 0, 32), "mb": ("ll", 32, 56), "md": ("ll", 56, 128)}
+TILES = {"mc": ("lm", 0, 32), "mb": ("lm", 32, 56), "md": ("lm", 56, 128)}
 for _p in range(3):
     TILES.update({"X%d" % _p: ("xz", _p * 512, _p * 512 + S), "Z%d" % _p: ("xz", _p * 512 + S, _p * 512 + 512),
-                  "B%d" % _p: ("st%d" % _p, B0, B0 + S), "b%d" % _p: ("st%d" % _p, B0 + S, A0),
-                  "J%d" % _p: ("st%d" % _p, W0, S), "j%d" % _p: ("st%d" % _p, S, B0), "y%d" % _p: ("yb", _p * 128, _p * 128 + 128)})
-TILES.update({"y2": ("yb", 256, 320), "y3": ("yb", 320, 384)})
-WHOLE = ("md", "y2", "y3")
+                  "B%d" % _p: ("bb", _p * 512, _p * 512 + S), "b%d" % _p: ("bb", _p * 512 + S, _p * 512 + 512),
+                  "J%d" % _p: ("jb", _p * 512, _p * 512 + S), "j%d" % _p: ("jb", _p * 512 + S, _p * 512 + 512), "y%d" % _p: ("yb", _p * 128, _p * 128 + 128)})
+TILES.update({"y2": ("yb", 256, 320), "y3": ("yb", 320, 384), "W2": ("xz", 1024, 1536)})
+del TILES["X2"], TILES["Z2"]
+WHOLE = ("mc", "mb", "md", "y2", "y3")
+CUT = ("y0", "y1")
 
 SCRATCH = {
     "posb": ("sbuf", [128, 3 * V], "bfloat16"),
     "li": ("sbuf", [128, 104], "int32"),
     "lo": ("sbuf", [128, 96], "uint16"),
+    "lh": ("sbuf", [128, 136], "float16"),
+    "ls": ("sbuf", [128, 288], "uint16"),
+    "lm": ("sbuf", [128, 128], "uint16"),
+    "xin": ("sbuf", [128, 1536], "bfloat16"),
     "ki": ("sbuf", [128, 8], "int32"),
     "sm": ("sbuf", [128, 256], F),
     "tab": ("sbuf", [128, V], F),
@@ -34,12 +41,17 @@ SCRATCH = {
     "kn": ("sbuf", [128, 128], F),
     "tk": ("dram", [16, 128, 16], "bfloat16"),
     "xz": ("sbuf", [128, 1536], "bfloat16"),
+    "bb": ("sbuf", [128, 3, 512], "bfloat16"),
+    "jb": ("sbuf", [128, 3, 512], "bfloat16"),
+    "hm": ("sbuf", [128, 384], "bfloat16"),
+    "gm": ("sbuf", [128, 192], "bfloat16"),
     "ll": ("sbuf", [128, 128], "uint16"),
     "selb": ("sbuf", [128, 512], "bfloat16"),
-    "oneb": ("sbuf", [128, 272], "bfloat16"),
+    "oneb": ("sbuf", [128, 512], "bfloat16"),
     "eyeb": ("sbuf", [128, 256], "bfloat16"),
     "eye": ("sbuf", [128, 128], F),
-    "sel": ("sbuf", [128, 10 * 128], F),
+    "sel": ("sbuf", [128, 512], F),
+    "sej": ("sbuf", [128, 512], F),
     "qq": ("sbuf", [128, 384], F),
     "kwo": ("sbuf", [128, 512], F),
     "st0": ("sbuf", [128, WIN], F),
@@ -59,30 +71,42 @@ SCRATCH = {
 for _k in range(8):
     SCRATCH["p%d" % _k] = ("psum", [128, 512], F)
 for _k, (_b, _lo, _hi) in TILES.items():
-    if _k in WHOLE:
-        SCRATCH["t" + _k] = ("dram", [4, 128, _hi - _lo], SCRATCH[_b][2])
-    else:
+    if _k in CUT:
         SCRATCH["t" + _k] = ("dram", [8, 128, (_hi - _lo) // 4], SCRATCH[_b][2])
         SCRATCH["u" + _k] = ("dram", [128, _hi - _lo], SCRATCH[_b][2])
+    else:
+        SCRATCH["t" + (_k if _k in WHOLE else _k[0])] = ("dram", [4, 128, _hi - _lo], SCRATCH[_b][2])
 
-SEMAPHORES = (["qv", "qs", "qt", "qg", "sent", "kar0", "kar1"] + ["d%d" % k for k in range(56)]
-              + [w + str(k) for w in ("ar", "rin") for k in range(len(TILES) + 1)] + ["out%d" % k for k in range(20)])
+SEMAPHORES = (["qv", "qs", "qt", "qg", "sent", "kar", "rink"] + ["d%d" % k for k in range(60)]
+              + [w + k for w in ("ar", "rin") for k in TILES] + ["ary%d_%d" % (k, s) for k in (2, 3) for s in range(3)]
+              + ["out%d" % k for k in range(21)])
 
-FIRST = "d0 Q d1 q1 d2a d2b q2a q2b D Ea Eb Va Vb Ka Kb La Lb m0 @j2 @jr @lk m1 x0 z0 @n0 m2 x1 z1 @n1 x2 z2 @n2"
-HEAD = "ra rb d0a q0a d1a q1a a0a Z2b d2a q2a e1a d0b q0b d1b q1b a0b a1b d2b q2b e2b "
-JHEAD = "ra rb Y0b d0a Z1b q0a d1a q1a a0a d2a Z2b q2a e1a d0b q0b d1b q1b a0b a1b d2b q2b e2b "
-FTAIL = "Ba0 Ba1 Va0 Va1 Ca0 Ca1 m0a m1a m2a ub x0a cb z0a m0b m1b x0b z0b @n0 m2b x1 z1 @n1 x2 z2 @n2"
+SETUP = ("one part ramp hm eye zero02 low more1 col more2 zeros46 zeros68 half0 ends slabs0 zero24 ones neg nil slabbed0 k places wv gm putA *x0 >X0 "
+         "half1 order *x1 >X1 getc gneg selb02 *B0 >B0 bord slabs1 turnc *x2 >W2 putB0 slabbed1 putB1 own *B1 >B1 listc *B2 >B2 "
+         ">mc ident getb kland in2 diff2 putJ *J2v seek0 *J0 sel in0 diff0 *J1 keep >J0 >J1 >J2 spread0 wn look1 w0 rn kw0 sej in1 qq")
+FIRST = ("d0 Q d1 q1 d2 q2a q2b @look2 @turnb @kn @kwb @jr D Ea Eb Va Vb Ka Kb La Lb @listb @>mb @landc @landB @landJ @landb "
+         "m0 @wideB0 @wideB2 @wideB1 @r @turnd @wideJ0 @wideJ1 @wideJ2 m1 x0 z0 @n0 m2 x1 z1 @n1 x2 z2 @n2")
+HEAD = "ra rb < d0a q0a d0b d1a Z2b q1a a0a d2a q2a e1a q0b d1b q1b a0b a1b d2b q2b e2b > "
+JHEAD = "ra rb Y0b d0a Z1b q0a d1a d0b q1a a0a d2a Z2b q2a e1a q0b d1b q1b a0b a1b d2b q2b e2b "
+FTAIL = "Ba0 Ba1 Va0 Va1 Ca0 Ca1 m0a m1a m2a < ub x0a cb z0a m0b > m1b x0b z0b @n0 m2b x1 z1 @n1 x2 z2 @n2"
 TAIL = "X0 X1 X2 " + FTAIL
 PRE = ("Z0", "Z1", "Z2a")
 JPRE = ("Z0a", "Z1a", "Z2a")
-BORDER = ("t0 P0 g0", "t1 P1 g1", "T2 P2 g2 D0 q0 D1 q1 A0 d0 d1 S1 A1 s0 o0 o1 o2")
-JOINT = "B0 B1 V0 V1 C0 C1 m0 R0 m1 R1 m2 R2 x0 x1 z0 @n0 x2 z1 @n1 z2 @n2"
+BORDER = ("t0 P0 g0", "t1 P1 g1", "< T0 U0 T1 U1 D0 T2 U2 g2 q0 D1 q1 A0 d0 d1 S0 S1 A1 o0 o1 o2 >")
+JOINT = "B0 B1 V0 V1 C0 C1 M0 M1 R0 m1 R1 m2 R2 "
+JTAIL = "x0 x1 z0 @n0 x2 z1 @n1 z2 @n2"
+JLAST = "< x0 z0 @n0 x1 z1 @n1 x2 z2 @n2 >"
 LAST = ("w0", "w1", "u2")
 NEAR = "p3"
-CALLS = "k X0:0,Z0:2 X1:1,Z1:3 X2:0,Z2:2 B0:1,b0:3 mc:0 B1:0,b1:2 B2:1,b2:3 mb:1 J0:0,j0:2 J1:1,j1:3 J2:0,j2:2 md:0 y0:1 y1:3 y2:0,y3:2 y2:d,y3:d"
-LANDS = "X0,Z0 X1,Z1 X2,Z2 mc B0,b0 B1,b1 B2,b2 mb"
-WAY = {"MD": 3000, "Y0": 3600, "Y1": 3500, "Y2": 2600, "Y3": 2600, "K": 7500, "X0": 6000, "Z0": 6000, "X1": 5000, "Z1": 5000, "X2": 4500, "Z2": 4500, "B0": 5500, "B1": 5500, "B2": 5500, "J0": 5500, "J1": 5500, "J2": 6500}
-NAMES = ["k"] + list(TILES)
+CALLS = ("k X0:0,Z0:2 X1:1,Z1:3 B0:0,b0:2 W2:d B1:1,b1:3 B2:2,b2:3 mc:0 J0:0,j0:2 J1:1,j1:3 J2:0,j2:2 mb:1 md:0 "
+         "y0:1 y1:3 y2:0,y3:2 y2:d,y3:d")
+ARRIVALS = (0, 2, 1)
+WAY = {"MC": 4000, "MB": 4000, "MD": 3000, "Y0": 3600, "Y1": 3500, "Y2": 2600, "Y3": 2600, "K": 7000, "X0": 5500, "Z0": 5500, "X1": 5500,
+       "Z1": 5500, "W2": 3000, "B0": 5500, "B1": 5500, "B2": 5500, "J0": 5500, "J1": 5500, "J2": 6500}
+
+
+def slot(q, holder):
+    return q ^ holder ^ 3
 
 
 def bits(engines):
@@ -99,7 +123,7 @@ def transfer(T, topo, core, to, engines, sem, src, dst):
 
 def ways(T, topo, r):
     me = T.cores[r]
-    others = sorted((q for q in range(len(T.cores)) if q != r), key=lambda q: topo.may_write(me, T.cores[q]))
+    others = sorted((q for q in range(len(T.cores)) if q != r), key=lambda q: (topo.may_write(me, T.cores[q]), q ^ r))
     can = [c for c in topo.cores_of(me) if c != me and all(topo.may_write(c, T.cores[q]) for q in others)]
     return others, sorted(can, key=lambda c: topo.die(c) != topo.die(me))
 
@@ -114,7 +138,7 @@ def calls_of(T, topo, r):
         n = len(tiles)
         both = lambda name: name in WHOLE and name + ":d" not in CALLS
         out.append([(name, None, [], off[i::n]) if k == "d" else
-                    (name, relays[int(k)], (rest if both(name) else every)[i::n], off[i::n] if both(name) else [])
+                    (name, relays[int(k[0])], (rest if both(name) or k[1:] else every)[i::n], off[i::n] if both(name) else [])
                     for i, (name, k) in enumerate(tiles)])
     return out
 
@@ -124,8 +148,26 @@ def onward(T, topo, r, relay, name):
     off = topo.engines(relay, T.cores[others[0]])
     if name in WHOLE:
         return {others[0]: off[0::2], others[1]: off[1::2]}
+    if name not in CUT:
+        return {others[int(name[1])]: off}
     half = len(off) // 2
     return {others[0]: off[1::2], others[1]: off[0:half:2], others[2]: off[half::2]}
+
+
+def landing(T, r, q, name):
+    j = slot(r, q)
+    if name in CUT:
+        return T["t" + name][4 + r], "ar" + name
+    if name in WHOLE:
+        return T["t" + name][j], "ar" + name + ("_%d" % j if name[0] == "y" else "")
+    if name[0] in "XZW":
+        o = 512 * j + S * (name[0] == "Z")
+        return T.xin[:, o:o + TILES[name][2] - TILES[name][1]], "ar" + name
+    return T["t" + name[0]][j], "ar" + name
+
+
+def relayed(T, name):
+    return T["u" + name][:] if name in CUT else T["t" + name][3] if name in WHOLE else T["t" + name[0]][int(name[1])]
 
 
 def first_call(T, topo, r):
@@ -144,23 +186,24 @@ def relay_program(g, core, T, topo):
         sent = 0
         for q, part, to, engines in first_call(T, topo, r):
             if to == core:
-                g.wait_ge(T.sem.rin0, len(engines))
-                one, piece = topo.engines(core, T.cores[q])[:1], T.tk[(2 * part + 1) * n + r]
-                g.remote_dma_fused([transfer(T, topo, core, T.cores[q], one, "kar%d" % part, piece, piece)], local_sem=T.sem.sent)
+                g.wait_ge(T.sem.rink, len(engines))
+                one, piece = topo.engines(core, T.cores[q])[:1], T.tk[(2 + part) * n + slot(r, q)]
+                g.remote_dma_fused([transfer(T, topo, core, T.cores[q], one, "kar", piece, piece)], local_sem=T.sem.sent)
                 sent += 1
         for call in calls_of(T, topo, r):
             for name, to, engines, _ in call:
                 if to != core:
                     continue
-                k, t, whole = NAMES.index(name), T["t" + name], name in WHOLE
-                if whole:
-                    g.wait_ge(T.sem["rin%d" % k], len(engines))
+                if name in CUT:
+                    cut = T.sem["d%d" % CUT.index(name)]
+                    g.sync.wait_ge(T.sem["rin" + name], len(engines))
+                    g.sync.dma_start(T["t" + name][0:n], relayed(T, name)).then_inc(cut, 16)
+                    g.wait_ge(cut, 16)
                 else:
-                    g.sync.wait_ge(T.sem["rin%d" % k], len(engines))
-                    g.sync.dma_start(t[0:n], T["u" + name][:]).then_inc(T.sem["d%d" % k], 16)
-                    g.wait_ge(T.sem["d%d" % k], 16)
+                    g.wait_ge(T.sem["rin" + name], len(engines))
                 legs = onward(T, topo, r, core, name)
-                trs = [transfer(T, topo, core, T.cores[q], es, "ar%d" % k, t[r if whole else q], t[r if whole else n + r])
+                trs = [transfer(T, topo, core, T.cores[q], es, landing(T, r, q, name)[1],
+                                T["t" + name][slot(q, r)] if name in CUT else relayed(T, name), landing(T, r, q, name)[0])
                        for q, es in legs.items()]
                 g.remote_dma_fused(trs, local_sem=T.sem.sent)
                 sent += sum(len(es) for es in legs.values())
@@ -180,7 +223,8 @@ def meetings(ops):
                     over = (w2 or write) and lo < hi2 and lo2 < hi and pa < pb2 and pa2 < pb
                     if p["q"] == o["q"] and p["own"] is None and o["own"] is None:
                         if over or (bank and o["q"] == "t"):
-                            met[j] = met.get(j, False) or (o["q"] != "t" and over)
+                            apart = o["q"] == "t" and bank and o["r"][0][3] != p["r"][0][3] and pa < pb2 and pa2 < pb
+                            met[j] = met.get(j, False) or (o["q"] != "t" and over) or apart
                     elif bank or over:
                         met[j] = True
         for write, views in ((False, o["r"]), (True, o["w"])):
@@ -267,7 +311,7 @@ def rank_program(g, core, T, topo):
         relay_program(g, core, T, topo)
         return
     others = ways(T, topo, rank)[0]
-    ops = []
+    ops, ordered = [], [False]
 
     def vw(name, lo, hi, step=1, parts=(0, 128)):
         return (name, lo, hi, step, parts)
@@ -277,6 +321,8 @@ def rank_program(g, core, T, topo):
             return ap(v[0]).indirect(ap(v[1]))
         if SCRATCH[v[0]][0] == "dram":
             return T[v[0]][v[1]:v[2]]
+        if len(SCRATCH[v[0]][1]) == 3:
+            return T[v[0]][v[4][0]:v[4][1], v[1] // 512, v[1] % 512:(v[2] - 1) % 512 + 1]
         if v[3] == 1:
             return T[v[0]][v[4][0]:v[4][1], v[1]:v[2]]
         return T[v[0]][v[4][0]:v[4][1], v[1]:v[2]:v[3]]
@@ -305,7 +351,7 @@ def rank_program(g, core, T, topo):
             r += span(out)[1:]
         holds = cycles(q, ins, out) if holds is None else holds
         ops.append({"n": len(ops), "q": q, "fn": fn, "r": r, "w": w, "own": own, "dma": dma, "after": list(after),
-                    "soft": list(soft), "behind": [], "stay": False, "holds": holds, "takes": holds if takes is None else takes})
+                    "soft": list(soft), "behind": [], "stay": ordered[0], "holds": holds, "takes": holds if takes is None else takes})
         return len(ops) - 1
 
     dmas = [0]
@@ -379,6 +425,22 @@ def rank_program(g, core, T, topo):
         for a in range(16):
             mm(p7(col, col + n), vw(mask, 15 - a, 143 - a), vw(src, at + a, at + 16 * n, 16), a == 0, a == 15)
 
+    def difference(p, k):
+        b = 3 if k is None else slot(others[k], rank)
+        for z in (0, 1):
+            o = 512 * (p if k is None else b) + S * z
+            mask = vw("eyeb", 128 * z + 96, 128 * z + 128, 1, quad(3)) if k is None else vw("gm", 96 * z + 32 * p, 96 * z + 32 * p + 32, 1, THEIRS)
+            mm(vw(("p0", "p1", "p6")[p], 0, S, 1, quad(b)), mask, vw("xz" if k is None else "xin", o, o + S, 1, mask[4]), z == 0, z == 1)
+
+    def to_slabs(at, lo, hi):
+        for k in range(3):
+            out = lambda parts: vw("p5", at + k * (hi - lo), at + (k + 1) * (hi - lo), 1, parts)
+            mm(out(THEIRS), vw("hm", 96 * others[k], 96 * others[k] + 96), vw("lh", lo, hi), True, True)
+            mm(out(quad(3)), vw("eyeb", 32 * rank, 32 * rank + 32), vw("lh", lo, hi), True, True)
+
+    def slabbed(lo, hi):
+        cp("v", vw("ls", lo, hi), vw("p5", lo, hi))
+
     def pieces(c, win, lst, drawn=False):
         def at(name, p, h, o=0):
             if name in ("xb", "zb"):
@@ -398,14 +460,13 @@ def rank_program(g, core, T, topo):
 
         def d(p, h=None):
             if drawn:
-                mm(diff(p, h), vw("eyeb", 0, 128), at(xx, p, h), True, False)
-                mm(diff(p, h), vw("eyeb", 128, 256), at(zz, p, h), False, True)
+                difference(p, ARRIVALS[-1])
             else:
                 tt(diff(p, h), ends(p, 0, h), at(zz, p, h), ALU.subtract)
         return {
             "Z": lambda p, h=None: cp("s", at(zz, p, h), ends(p, 1, h)),
             "Y": lambda p, h=None: cp("v", at(zz, p, h), ends(p, 1, h)),
-            "X": lambda p, h=None: cp("s", at(xx, p, h), ends(p, 0, h)),
+            "X": lambda p, h=None: (cp("s", at(xx, p, h), ends(p, 0, h)), ops[-1].update(stay=True)),
             "W": lambda p, h=None: cp("v", at(xx, p, h), ends(p, 0, h)),
             "d": d,
             "q": lambda p, h=None: square(at("sq", p, h), diff(p, h)),
@@ -432,7 +493,9 @@ def rank_program(g, core, T, topo):
 
     def run(f, text, hooks=None):
         for w in text.split():
-            if w[0] == "@":
+            if w in "<>":
+                ordered[0] = w == "<"
+            elif w[0] == "@":
                 hooks[w[1:]]()
             else:
                 f[w[0]](*[int(ch) if ch.isdigit() else "ab".index(ch) for ch in w[1:]])
@@ -459,7 +522,13 @@ def rank_program(g, core, T, topo):
     sj = lambda p: half("sj", p, 0)
     joint = {
         "g": lambda p: border("s", p, 0, 1), "t": lambda p: border("s", p, 1, 2),
-        "H": lambda p: border("v", p, 0, 1), "T": lambda p: border("v", p, 1, 2),
+        "T": lambda s: cp("v", part(half("gb", 2, 1), s, 64), (st(2, J0, WIN), ll(44 + 4 * s, 48 + 4 * s))),
+        "U": lambda s: mm(part(bank(2, 0), s, 64), vw("qq", s * 128, s * 128 + 128), part(half("gb", 2, 1), s, 64), True, True),
+        "e": lambda s: tt(part(half("dj", 2, 0), s, 64), part(half("gb", 2, 0), s, 64), part(bank(2, 0), s, 64), ALU.subtract),
+        "E": lambda: square(sj(2), half("dj", 2, 0)), "H": lambda p: border("v", p, 1, 2),
+        "Q": lambda p: tt(sj(p), half("dj", p, 0), half("dj", p, 0), ALU.mult),
+        "u": lambda a, b: cp("s", vw("gb", 192 + 64 * a, 192 + 64 * b), (st(0, J0, WIN), ll(44 + 4 * a, 44 + 4 * b))),
+        "M": lambda k: tt(part(half("dj", 0, 1), k), part(half("p4", 0, 1), k), part(half("dj", 0, 0), k), ALU.mult),
         "P": lambda p: across(bank(p, 0), half("gb", p, 1)),
         "D": lambda p: tt(half("dj", p, 0), half("gb", p, 0), bank(p, 0), ALU.subtract),
         "d": lambda k: tt(part(half("dj", 2, 0), k), part(half("gb", 2, 0), k), part(bank(2, 0), k), ALU.subtract),
@@ -491,203 +560,242 @@ def rank_program(g, core, T, topo):
     def send(first, again=0):
         if first == "k":
             legs = first_call(T, topo, rank)
-            return issue(["k"], [transfer(T, topo, core, to, es, "kar%d" % part if to in T.cores else "rin0", T.tk[8 * part + q],
-                                          T.tk[8 * part + 4 + rank]) for q, part, to, es in legs], [], len(legs))
+            return issue(["k"], [transfer(T, topo, core, to, es, "kar" if to in T.cores else "rink", T.tk[4 * part + q],
+                                          T.tk[8 + 4 * part + slot(rank, q)]) for q, part, to, es in legs], [], len(legs))
         call = [c for c in calls_of(T, topo, rank) if c[0][0] == first][again]
         trs = []
         for name, to, es, direct in call:
-            src, k = ap(vw(*TILES[name])), NAMES.index(name)
+            src, (dst, sem) = ap(vw(*TILES[name])), landing(T, rank, others[2], name)
             if es:
-                trs.append(transfer(T, topo, core, to, es, "rin%d" % k, src, T["t" + name][rank] if name in WHOLE else T["u" + name][:]))
+                trs.append(transfer(T, topo, core, to, es, "rin" + name, src, relayed(T, name)))
             if direct:
-                trs.append(transfer(T, topo, core, T.cores[others[2]], direct, "ar%d" % k, src, T["t" + name][rank]))
+                trs.append(transfer(T, topo, core, T.cores[others[2]], direct, sem, src, dst))
         issue([c[0] for c in call], trs, [vw(*TILES[c[0]]) for c in call], sum(len(c[2]) + len(c[3]) for c in call))
 
-    def landed(name):
+    def landed(name, senders=others, into=None):
         n = sum(len(direct) * (ways(T, topo, q)[0][2] == rank) + (len(onward(T, topo, q, to, name).get(rank, [])) if es else 0)
-                for q in others for c in calls_of(T, topo, q) for w, to, es, direct in c if w == name)
-        come = add(None, None, [], None, ("ar%d" % NAMES.index(name), n), holds=WAY.get(name.upper(), TURN))
+                for q in senders for c in calls_of(T, topo, q) for w, to, es, direct in c if w == name)
+        come = add(None, None, [], into, (landing(T, senders[0], rank, name)[1], n), holds=WAY.get(name.upper(), TURN))
         ops[-1]["behind"] = [calls_at[name]]
-        t = T["t" + name]
-        return [(lo, hi, t[lo:hi, 32 * rank:32 * rank + 32, :] if name in WHOLE else t[4 + lo:4 + hi], come)
-                for lo, hi in ((0, rank), (rank + 1, 4)) if lo < hi]
+        return come
 
     mine_first = lambda s: (0, 1) if rank < rank ^ s else (1, 0)
-    staged = [dma("s", T.tk[8 * (k // 2):8 * (k // 2) + 4, 64 * (k % 2):64 * (k % 2) + 64, :], src[:, :], 100)
+    dma("s", vw("li", 0, 64), T.ends[:, :], 600)
+    staged = [dma("sy"[k // 2], T.tk[4 * (k // 2):4 * (k // 2) + 4, 64 * (k % 2):64 * (k % 2) + 64, :], src[:, :], 600)
               for k, src in enumerate((T.inv, T.stiff, T.jinv, T.jstiff))]
-    dma("s", vw("li", 0, 64), T.ends[:, :], 200)
-    for p in range(3):
-        dma("y", pos(p), T.pos[:, p * V:(p + 1) * V], LOAD * (p + 1))
-    dma("y", vw("li", 72, 104), T.bord[:, :], 3 * LOAD + 200)
-    dma("y", vw("li", 64, 72), T.watch[:, :], 3 * LOAD + 400)
-    together(2)
-    send("k")
-    ops[-1]["after"] += staged
+    for k in range(3):
+        dma("y", vw("posb", k * V, (k + 1) * V, 1, THEIRS), T.pos[32 * others[k]:32 * others[k] + 32, :], LOAD * (k + 1))
+        dma("y" if k else "s", vw("posb", k * V, (k + 1) * V, 1, quad(3)), T.pos[32 * rank:32 * rank + 32, k * V:(k + 1) * V], LOAD * (k + 1))
+        together(2)
+        if k == 1:
+            dma("y", vw("li", 72, 104), T.bord[:, :], 2 * LOAD + 200)
+            dma("y", vw("li", 64, 72), T.watch[:, :], 2 * LOAD + 400)
+            together(2)
 
-    fill(vw("tab", 0, 512), 0.0)
-    fill(vw("oneb", 0, 144), 1.0)
-    fill(vw("tab", 512, 1280), 0.0)
-    cp("s", vw("tab", 1280, 1792), vw("tab", 0, 512))
-    cp("s", vw("tab", 1792, 2048), vw("tab", 0, 256))
-    count(vw("ramp", 0, 512), [[1, 512]], 0)
-    cp("v", vw("lo", 0, 64), vw("li", 0, 64))
-    kept = dma("s", T.tk[4 + rank:16:8], T.tk[rank:16:8], 0)
-    ops[-1]["after"] += staged
-    ops[-1]["stay"] = False
-    count(vw("ki", 0, 2), [[0, 2]], 0, 1)
-    count(sm(64, 96), [[16, 32]], 0)
-    select(vw("wv", 0, 144), vw("oneb", 0, 144), [[-16, 9], [256, 16]], -15 * 256)
+    def shift_by(out, a, bias):
+        add("s", lambda e: e.activation(ap(out), ap(a), ACT.Identity, bias=ap(bias) if isinstance(bias, tuple) else bias),
+            [a] + [bias] * isinstance(bias, tuple), out)
 
-    def drawn(words):
-        for w in words.split():
-            p = int(w[1])
-            name, o, col = {"x": ("xz", p * 512, 0), "B": ("st%d" % p, B0, 32), "J": ("st%d" % p, W0, 64)}[w[0]]
-            for lo, hi in ((0, 16), (16, 32)) if w in ("B0", "x2") else ((0, 32),):
-                cp("v" if (w, lo) == ("x2", 0) else "s", vw(name, o + 16 * lo, o + 16 * hi), (pos(p), vw("lo", col + lo, col + hi)))
+    def drawn(w):
+        p = int(w[1])
+        name, o, col = {"x": ("xz", p * 512, 64 * p), "B": ("bb", p * 512, 64 * p + 32), "J": ("jb", p * 512, 192 + 32 * p)}[w[0]]
+        cp("v" if w[2:] else "s", vw(name, o, o + 512), (pos(p), vw("ls", col, col + 32)))
 
-    table_scatter(0, 32, A0)
-    table_gather(0, 32, 64)
-    fill(vw("oneb", 144, 272), -1.0)
-    to_lists(0, 0, 32)
-    ts(vw("ki", 4, 6), vw("ki", 0, 2), 15, ALU.bitwise_and)
-    cp("v", sm(96, 98), vw("ki", 4, 6))
-    ts(sm(128, 160), sm(64, 96), sm(96, 97), ALU.add)
-    ts(sm(0, 32), sm(128, 160), float(B0), ALU.add)
-    ts(sm(32, 56), sm(128, 152), float(J0), ALU.add)
-    drawn("x0 x1 x2")
-    tt(sm(64, 96), p7(0, 32), sm(0, 32), ALU.max)
-    cp("v", sm(200, 232), p7(0, 32))
-    ts(ll(0, 32), sm(64, 96), float(B0), ALU.subtract)
-    for s in (1, 2, 3):
-        for k, h in enumerate(mine_first(s)):
-            o = 72 + 8 * (rank ^ s) + 4 * h
-            cp("v", vw("lo", 68 + 12 * k + 4 * s, 72 + 12 * k + 4 * s), vw("li", o, o + 4))
-    cp("v", vw("lo", 64, 72), vw("li", 64, 72))
-    drawn("B0 B1 B2 J0 J1 J2")
-    table_scatter(32, 64, B0)
-    table_gather(640, 72, 96)
-    to_lists(40, 640, 24)
-    table_scatter(72, 96, J0)
-    tt(sm(96, 120), p7(40, 64), sm(32, 56), ALU.max)
-    ts(ll(32, 56), sm(96, 120), float(J0), ALU.subtract)
-    for call in CALLS.split()[1:-8]:
-        send(call[:2], call[3] == "d")
-    fresh = []
+    lm = lambda lo, hi: vw("lm", lo, hi)
+    marks = {}
 
-    count(sm(168, 200), [[0, 32]], 0)
+    def own_places():
+        shift_by(sm(128, 160), vw("ramp", 0, 512, 16), sm(96, 97))
+        shift_by(sm(0, 32), sm(128, 160), float(B0))
+        shift_by(sm(32, 56), sm(128, 152), float(J0))
+        cp("s", sm(232, 240), sm(128, 136))
 
-    def lookups():
-        for lo in range(0, 72, 12):
-            cp("s", vw("rf", 16 * lo, 16 * lo + 192), (vw("tab", 0, V), vw("lo", lo, lo + 12)))
-        for lo in (0, 384, 768):
-            src, out = vw("rf", lo, lo + 384), vw("rv", 1024 + lo, 1408 + lo)
-            add("g", (lambda out, src: lambda e: e.affine_select(ap(out), ap(src), [[0, 384]], ALU.is_equal, 0.0, 0, 0))(out, src), [src], out)
+    def constants_leave():
+        send("k")
+        ops[-1]["after"] += staged
+        marks["kept"] = dma("s", T.tk[11:16:4], T.tk[rank:8:4], 0)
+        ops[-1]["after"] += staged
+        marks["k"] = add(None, None, [], None, ("kar", 2 * len(others)), holds=WAY["K"])
+        ops[-1]["behind"] = [calls_at["k"]]
+
+    def border_order():
+        mm(vw("p5", 320, 328), vw("eyeb", 0, 128), vw("lh", 64, 72), True, True)
+        for s in (1, 2, 3):
+            for k, h in enumerate(mine_first(s)):
+                o = 72 + 8 * (rank ^ s) + 4 * h
+                mm(vw("p5", 324 + 12 * k + 4 * s, 328 + 12 * k + 4 * s), vw("eyeb", 0, 128), vw("lh", o, o + 4), True, True)
+
+    def finish_list(out, found, own, base, scratch):
+        tt(scratch, found, own, ALU.max)
+        ts(out, scratch, float(base), ALU.subtract)
+
+    def convert(out, src):
+        add("g", lambda e: e.affine_select(ap(out), ap(src), [[0, src[2] - src[1]]], ALU.is_equal, 0.0, 0, 0), [src], out)
+
+    def lookups(i):
+        cp("s", vw("rf", 384 * i, 384 * i + 384), (vw("tab", 0, V), vw("lo", 24 * i, 24 * i + 24)))
+
+        convert(vw("rv", 1024 + 384 * i, 1408 + 384 * i), vw("rf", 384 * i, 384 * i + 384))
 
     def last_lists():
-        to_lists(64, 1024, 72)
-        ops[-16]["stay"] = True
         tt(sm(0, 72), p7(64, 136), sm(168, 240), ALU.max)
-        cp("v", ll(56, 128), sm(0, 72))
+        ops[-1]["stay"] = True
+        cp("v", lm(56, 128), sm(0, 72))
         send("md")
-        land("md")
+        land_list("md")
 
-    for k in (0, 1):
-        select(vw("eyeb", k * 128, k * 128 + 128), vw("oneb", k * 144, k * 144 + 128), [[-1, 128]], 0)
-    for i in range(4):
-        select(vw("selb", i * 128, i * 128 + 128, 1, both), vw("oneb", 0, 128, 1, both), [[-4, 8], [0, 16]], -i)
-    for part_ in (0, 1):
-        come = add(None, None, [], None, ("kar%d" % part_, len(others)), holds=WAY["K"])
-        ops[-1]["behind"] = [calls_at["k"]]
+    def widen(q, kind, p):
+        name, to = {"B": ("bb", B0), "J": ("jb", W0)}[kind]
+        out, src = st(p, to, to + 512), vw(name, 512 * p, 512 * p + 512)
+        convert(out, src) if q == "g" else cp(q, out, src)
+
+    def constants_land():
         for k, name in enumerate(("wc", "kc")):
-            dma("y", vw(name, 0, 128, 1, quad(part_)), T.tk[8 * part_ + 4:8 * part_ + 8, 64 * k:64 * k + 64, :], 100)
-            ops[-1]["after"] += [come, kept]
-            ops[-1]["stay"] = False
-    for c in (0, 1):
-        for bank_, name in ((("p3", "p2")[c], "wc"), (("p4", "p2")[c], "kc")):
+            dma("y", vw(name, 0, 128, 1, both), T.tk[8:16, 64 * k:64 * k + 64, :], 400)
+            ops[-1]["after"] += [marks["k"], marks["kept"]]
+
+    def spread(c):
+        for bank_, name in (("p3", "wc"), ("p4", "kc")):
             for a in (c * S, c * S + 128):
-                o = a % S if name == "wc" else a
-                mm(vw(bank_, o, o + 128), vw("selb", a, a + 128, 1, quad(0)), vw(name, 0, 128, 1, quad(0)), True, True)
+                mm(vw(bank_, a, a + 128), vw("selb", a, a + 128, 1, quad(0)), vw(name, 0, 128, 1, quad(0)), True, True)
+
     wn, wc, rn, kn = (vw(n, 0, 128, 1, both) for n in ("wn", "wc", "rn", "kn"))
-    add("s", lambda e: e.activation(ap(wn), ap(wc), ACT.Identity, bias=-EPS, scale=-1.0), [wc], wn)
 
-    def own_constants(c):
-        w, k, t, out = vw(("p3", "p2")[c], 0, S), vw(("p4", "p2")[c], c * S, c * S + S), vw("zz", c * S, c * S + S), vw("kwo", c * S, c * S + S)
-        add("s", lambda e: e.activation(ap(t), ap(w), ACT.Identity, bias=-EPS, scale=-1.0), [w], t)
-        tt(out, k, t, ALU.mult)
-
-    add("v", lambda e: e.reciprocal(ap(rn), ap(wn)), [wn], rn, holds=200 + 6 * 128)
-    own_constants(0)
-    own_constants(1)
-    cp("s", sm(232, 240), sm(128, 136))
+    def negated(out, w):
+        add("s", lambda e: e.activation(ap(out), ap(w), ACT.Identity, bias=-EPS, scale=-1.0), [w], out)
 
     def joint_product():
         tt(kn, vw("kc", 0, 128, 1, both), wn, ALU.mult)
         ops[-1]["stay"] = True
 
-    def late_masks():
-        for i in (2, 3):
-            select(sel(i), vw("oneb", 0, 128, 1, both), [[-4, 8], [0, 16]], -i)
-        select(eye, vw("oneb", 0, 128), [[-1, 128]], 0)
-        for s in (1, 2, 3):
-            for h in (0, 1):
-                for b in (0, 2):
-                    row = [32 + 8 * q + (q ^ s) + 1000 * ((q > q ^ s) != h) for q in (b, b + 1)]
-                    o = (2 + 2 * s + h) * 128 + 32 * b
-                    select(vw("sel", o, o + 64, 1, both), vw("oneb", 0, 64, 1, both), [[row[0] - row[1], 2], [-4, 2], [0, 16]], -row[0])
+    def spreading(name, lo, hi):
+        select(vw(name, 128 * lo, 128 * hi, 1, both), vw("oneb", 0, 128 * (hi - lo), 1, both), [[-1, hi - lo], [-4, 8], [0, 16]], -lo)
 
     def last_masks():
         for s in (1, 2, 3):
             select(vw("qq", s * 128 - 128, s * 128), vw("oneb", 0, 128), [[128 * (s >> 1) - 64, 2], [64 * (s & 1) - 32, 2], [-1, 32]], -32 * s)
-        for i in (0, 1):
-            select(sel(i), vw("oneb", 0, 128, 1, both), [[-4, 8], [0, 16]], -i)
 
-    def land(names):
-        for name in names.replace(",", " ").split():
-            runs = landed(name)
-            for lo, hi, src, come in runs:
-                dma("y", vw(*TILES[name], 1, (32 * lo, 32 * hi)), src, 300)
-                ops[-1]["after"].append(come)
-                if name == "Z2":
-                    fresh.append(len(ops) - 1)
-            together(len(runs))
+    def land_list(name):
+        _, lo, hi = TILES[name]
+        come = landed(name)
+        dma("y", vw("ll", lo, hi, 1, quad(3)), vw("lm", lo, hi, 1, quad(rank)), 100)
+        dma("y", vw("ll", lo, hi, 1, (0, 96)), T["t" + name][0:3, 32 * rank:32 * rank + 32, :], 200)
+        ops[-1]["after"].append(come)
+        together(2)
 
-    land(LANDS)
+    def land(kinds):
+        come = {w: [landed(w + str(k), [others[k]]) for k in range(3)] for w in kinds}
+        for h, w in enumerate(kinds):
+            name = TILES[w + "0"][0]
+            dma("y", T[name][0:96, :, S * h:S * h + S], T["t" + w][0:3, 0:96, :], 700)
+            ops[-1]["after"] += come[w]
+            ops[-1]["w"] = [span(vw(*TILES[w + str(p)], 1, THEIRS))[0] for p in range(3)]
+        together(2)
 
-    def late_gathers():
-        send("J0")
-        ops[-1]["after"] += fresh
-        send("J1")
-        send("J2")
-        land("J0,j0 J1,j1 J2,j2")
-        late_masks()
+    def arrived(k):
+        j = slot(others[k], rank)
+        for z, name in enumerate(w + str(k) for w in "XZW" if w + str(k) in TILES):
+            o = 512 * j + S * z
+            marks[name] = landed(name, [others[k]], vw("xin", o, o + TILES[name][2] - TILES[name][1]))
+        dma("y", vw("xz", 0, 1536, 1, quad(j)), vw("xin", 512 * j, 512 * j + 512, 1, THEIRS), 400)
 
-    def joint_constants(k, name):
-        for s in (1, 2, 3):
-            for h in (0, 1):
-                mm(part(half("p2", 0, k, 128), s - 1, 64), sel(2 + 2 * s + h), vw(name, 64 * h, 64 * h + 64, 1, both), h == 0, h == 1)
+    steps = {
+        "one": lambda: fill(vw("oneb", 0, 384), 1.0), "ones": lambda: fill(vw("oneb", 384, 512), 1.0),
+        "neg": lambda: ts(vw("eyeb", 128, 256), vw("eyeb", 0, 128), -1.0, ALU.mult),
+        "hm": lambda: select(vw("hm", 0, 384), vw("oneb", 0, 384), [[-16, 8], [0, 3], [-1, 16]], 0),
+        "gm": lambda: select(vw("gm", 0, 96), vw("oneb", 0, 96), [[-1, 3], [-3, 32]], 0),
+        "gneg": lambda: ts(vw("gm", 96, 192), vw("gm", 0, 96), -1.0, ALU.mult),
+        "zero": lambda a, b: fill(vw("tab", 256 * a, 256 * b), 0.0),
+        "zeros": lambda a, b: cp("s", vw("tab", 256 * a, 256 * b), vw("tab", 0, 256 * (b - a))),
+        "nil": lambda: fill(sm(168, 200), 0.0),
+        "putB": lambda h: table_scatter(32 + 16 * h, 48 + 16 * h, B0 + S * h),
+        "turnd": lambda: to_lists(64, 1024, 72),
+        "look": lookups, "seek": lambda i: table_gather(1024 + 384 * i, 24 * i, 24 * i + 24), "qq": last_masks, "wideB": lambda p: widen("ssg"[p], "B", p), "wideJ": lambda p: widen("g", "J", p),
+        "part": lambda: count(vw("ki", 0, 2), [[0, 2]], 0, 1), "ramp": lambda: count(vw("ramp", 0, 128), [[1, 128]], 0),
+        "more": lambda n: ts(vw("ramp", 128 * n, 256 * n), vw("ramp", 0, 128 * n), 128.0 * n, ALU.add),
+        "low": lambda: ts(vw("ki", 4, 6), vw("ki", 0, 2), 15, ALU.bitwise_and), "col": lambda: cp("v", sm(96, 98), vw("ki", 4, 6)),
+        "eye": lambda: select(vw("eyeb", 0, 128), vw("oneb", 0, 128), [[-1, 128]], 0),
+        "wv": lambda: select(vw("wv", 0, 144), vw("oneb", 0, 144), [[-16, 9], [256, 16]], -15 * 256),
+        "selb": lambda a, b: spreading("selb", a, b), "sel": lambda: spreading("sel", 0, 4),
+        "sej": lambda: dma("y", vw("sej", 0, 512, 1, quad(1)), vw("sel", 0, 512, 1, quad(0)), 200),
+        "ident": lambda: select(eye, vw("oneb", 0, 128), [[-1, 128]], 0),
+        "places": own_places, "k": constants_leave, "kland": constants_land, "spread": spread,
+        "half": lambda i: cp("v", vw("lh", 64 * i, 64 + 40 * i), vw("li", 64 * i, 64 + 40 * i)),
+        "ends": lambda: cp("v", vw("lo", 0, 64), vw("li", 0, 64)), "order": border_order,
+        "bord": lambda: (cp("v", vw("lh", 104, 136), vw("p5", 320, 352)), cp("v", vw("lo", 64, 96), vw("p5", 320, 352))),
+        "slabs": lambda i: to_slabs(192 * i, 104 * i, 64 + 72 * i), "slabbed": lambda i: slabbed(192 * i, 192 + 96 * i),
+        "putA": lambda: table_scatter(0, 32, A0), "putJ": lambda: table_scatter(72, 96, J0),
+        "getc": lambda: table_gather(0, 32, 64), "getb": lambda: table_gather(640, 72, 96),
+        "turnc": lambda: to_lists(0, 0, 32), "turnb": lambda: to_lists(40, 640, 24), "keep": lambda: cp("s", sm(200, 232), p7(0, 32)),
+        "listc": lambda: finish_list(lm(0, 32), p7(0, 32), sm(0, 32), B0, sm(64, 96)),
+        "listb": lambda: finish_list(lm(32, 56), p7(40, 64), sm(32, 56), J0, sm(96, 120)),
+        "wn": lambda: negated(wn, wc), "w": lambda c: negated(vw("zz", c * S, c * S + S), vw("p3", c * S, c * S + S)),
+        "kwb": lambda: ([mm(vw("p3", S + 128 * h, S + 128 * h + 128), sel(2 + h), kn, True, True) for h in (0, 1)],
+                        cp("s", vw("kwo", S, 2 * S), vw("p3", S, 2 * S))),
+        "kw": lambda c: tt(vw("kwo", c * S, c * S + S), vw("p4", c * S, c * S + S), vw("zz", c * S, c * S + S), ALU.mult),
+        "rn": lambda: add("v", lambda e: e.reciprocal(ap(rn), ap(wn)), [wn], rn, holds=200 + 6 * 128),
+        "in": arrived, "own": lambda: [difference(p, None) for p in range(3)], "diff": lambda k: [difference(p, k) for p in range(3)],
+        "landc": lambda: land_list("mc"), "landb": lambda: land_list("mb"), "landB": lambda: land("Bb"), "landJ": lambda: land("Jj"),
+    }
 
-    hooks = {"jr": lambda: joint_constants(1, "rn"), "jk": lambda: joint_constants(0, "kn"),
-             "j2": late_gathers, "lk": lambda: (lookups(), last_masks()), "ll": last_lists, "kn": joint_product}
+    def step(w):
+        if w[0] == ">":
+            send(w[1:])
+        elif w[0] == "*":
+            drawn(w[1:])
+        else:
+            name = w.rstrip("0123456789")
+            steps[name](*[int(ch) for ch in w[len(name):]])
 
+    def joint_constants(k, name, slots):
+        for s in slots:
+            for b in range(4):
+                q = slot(b, rank)
+                o, h, out = 128 * (q ^ s) + 32 * b, int(q > q ^ s), part(half("p2", 0, k, 128), s - 1, 64)
+                mm(vw("p2", out[1], out[2], 1, quad(b)), vw("sej", o, o + 32, 1, quad(1)), vw(name, 64 * h, 64 * h + 64, 1, quad(1)), True, True)
+
+    hooks = {"jr": lambda: joint_constants(1, "rn", (1, 2, 3)), "jk": lambda: joint_constants(0, "kn", (1, 2)), "jl": lambda: joint_constants(0, "kn", (3,)),
+             "ll": last_lists, "kn": joint_product}
+    hooks.update({w: (lambda w: lambda: step(w))(w) for w in (x[1:] for x in FIRST.split() if x[0] == "@") if w not in hooks and w not in ("n0", "n1", "n2", "r")})
+
+    ordered[0] = True
+    for w in SETUP.split():
+        step(w)
     c0 = pieces(0, None, None, True)
     c1 = pieces(1, lambda p: st(p, B0, WIN), ("ll", 0))
-    run(c0, FIRST, dict(hooks, **into(c1, PRE)))
+    run(c0, FIRST, dict(hooks, r=lambda: run(c1, HEAD[:6]), **into(c1, PRE)))
+    ordered[0] = False
+
     for t in range(SWEEPS):
         if t > 0:
             run(c0, JHEAD + TAIL, into(c1, PRE))
-        run(c1, HEAD + ("@kn " + TAIL.replace("m0a", "@ll @jk m0a") if t == 0 else TAIL), dict(hooks, **into(joint, BORDER)))
+        run(c1, HEAD[6 * (t == 0):] + ("@ll " + TAIL.replace("m0a", "@jk m0a") if t == 0 else TAIL), dict(hooks, **into(joint, BORDER)))
         c0 = pieces(0, lambda p: st(p, 0, WIN), ("ll", 56))
         c1 = pieces(1, lambda p: st(p, 0, WIN), ("ll", 88))
-        run(joint, JOINT, into(c0, JPRE) if t < SWEEPS - 1 else into(last, LAST))
+        run(joint, "@jl " * (t == 0) + JOINT + (JTAIL if t < SWEEPS - 1 else JLAST),
+            dict(hooks, **(into(c0, JPRE) if t < SWEEPS - 1 else into(last, LAST))))
 
     for name in ("y0", "y1", "y2"):
         send(name)
     send("y2", 1)
-    done = [dma("s", T.y[32 * rank:32 * rank + 32, :], vw("yb", 0, 384, 1, quad(rank)), 0)]
-    for i, name in enumerate(("y0", "y1", "y2", "y3")):
-        for k, (lo, hi, src, come) in enumerate(landed(name)):
-            done.append(dma("ys"[i % 2], T.y[32 * lo:32 * hi, TILES[name][1]:TILES[name][2]], src, 200))
-            ops[-1]["after"].append(come)
+    done = [dma("s", T.y[32 * rank:32 * rank + 32, :], vw("yb", 0, 384, 1, quad(3)), 0)]
+
+    def store(i, name, lo, hi, src, come):
+        done.append(dma("ys"[i % 2], T.y[32 * lo:32 * hi, TILES[name][1]:TILES[name][2]], src, 200))
+        ops[-1]["after"].append(come)
+
+    def store_whole(q):
+        for i, name in enumerate(("y2", "y3")):
+            j = slot(q, rank)
+            store(i, name, q, q + 1, T["t" + name][j, 32 * j:32 * j + 32, :], landed(name, [q]))
+
+    for k in (2, 0, 1):
+        store_whole(others[k])
+    for i, name in enumerate(CUT):
+        come = landed(name)
+        for lo, hi in ((0, rank), (rank + 1, 4)):
+            if lo < hi:
+                store(i, name, lo, hi, T["t" + name][4 + lo:4 + hi], come)
     add("y", None, [], None, after=done, holds=1)
     add("g", None, [], None, after=issued, soft=done, holds=1)
     emit(g, T, arrange(ops))

from concourse.bass import DstId, RemoteDMATransfer
from concourse.mybir import AluOpType as ALU, ActivationFunctionType as ACT

V, S = 2048, 256
W0, J0, B0, A0, WIN = 0, 128, 512, 1024, 1536
EPS = 1e-22
SWEEPS = 3
F = "float32"
THEIRS = (0, 96)
GATHER, SCATTER, MATMUL, FIXED, HOP, SELF = 1.56, 3.8, 3, {"v": 30, "s": 140}, 170, 60
DMA, ISSUE, LOAD, TURN = 1150, 250, 1330, 3900
TILES = {"mc": ("lm", 0, 32), "mb": ("lm", 32, 56), "md": ("lm", 56, 128)}
for _p in range(3):
    TILES.update({"X%d" % _p: ("xz", _p * 512, _p * 512 + S), "Z%d" % _p: ("xz", _p * 512 + S, _p * 512 + 512),
                  "B%d" % _p: ("bb", _p * 512, _p * 512 + S), "b%d" % _p: ("bb", _p * 512 + S, _p * 512 + 512),
                  "J%d" % _p: ("jb", _p * 512, _p * 512 + S), "j%d" % _p: ("jb", _p * 512 + S, _p * 512 + 512), "y%d" % _p: ("yb", _p * 128, _p * 128 + 128)})
TILES.update({"y2": ("yb", 256, 320), "y3": ("yb", 320, 384), "W2": ("xz", 1024, 1536)})
del TILES["X2"], TILES["Z2"]
WHOLE = ("mc", "mb", "md", "y2", "y3")
CUT = ("y0", "y1")

SCRATCH = {
    "posb": ("sbuf", [128, 3 * V], "bfloat16"),
    "li": ("sbuf", [128, 104], "int32"),
    "lo": ("sbuf", [128, 96], "uint16"),
    "lh": ("sbuf", [128, 136], "float16"),
    "ls": ("sbuf", [128, 288], "uint16"),
    "lm": ("sbuf", [128, 128], "uint16"),
    "xin": ("sbuf", [128, 1536], "bfloat16"),
    "ki": ("sbuf", [128, 8], "int32"),
    "sm": ("sbuf", [128, 256], F),
    "tab": ("sbuf", [128, V], F),
    "ramp": ("sbuf", [128, 512], F),
    "rv": ("sbuf", [128, 2176], "float16"),
    "rf": ("sbuf", [128, 1152], F),
    "wv": ("sbuf", [128, 144], "bfloat16"),
    "kc": ("sbuf", [128, 128], "bfloat16"),
    "wc": ("sbuf", [128, 128], "bfloat16"),
    "wn": ("sbuf", [128, 128], F),
    "rn": ("sbuf", [128, 128], F),
    "kn": ("sbuf", [128, 128], F),
    "tk": ("dram", [16, 128, 16], "bfloat16"),
    "xz": ("sbuf", [128, 1536], "bfloat16"),
    "bb": ("sbuf", [128, 3, 512], "bfloat16"),
    "jb": ("sbuf", [128, 3, 512], "bfloat16"),
    "hm": ("sbuf", [128, 384], "bfloat16"),
    "gm": ("sbuf", [128, 192], "bfloat16"),
    "ll": ("sbuf", [128, 128], "uint16"),
    "selb": ("sbuf", [128, 512], "bfloat16"),
    "oneb": ("sbuf", [128, 512], "bfloat16"),
    "eyeb": ("sbuf", [128, 256], "bfloat16"),
    "eye": ("sbuf", [128, 128], F),
    "sel": ("sbuf", [128, 512], F),
    "sej": ("sbuf", [128, 512], F),
    "qq": ("sbuf", [128, 384], F),
    "kwo": ("sbuf", [128, 512], F),
    "st0": ("sbuf", [128, WIN], F),
    "st1": ("sbuf", [128, WIN], F),
    "st2": ("sbuf", [128, WIN], F),
    "zz": ("sbuf", [128, 768], F),
    "xx": ("sbuf", [128, 768], F),
    "dd": ("sbuf", [128, 768], F),
    "sq": ("sbuf", [128, 768], F),
    "gb": ("sbuf", [128, 1152], F),
    "sj": ("sbuf", [128, 1152], F),
    "uu": ("sbuf", [128, 256], F),
    "cc": ("sbuf", [128, 256], F),
    "dj": ("sbuf", [128, 1152], F),
    "yb": ("sbuf", [128, 384], F),
}
for _k in range(8):
    SCRATCH["p%d" % _k] = ("psum", [128, 512], F)
for _k, (_b, _lo, _hi) in TILES.items():
    if _k in CUT:
        SCRATCH["t" + _k] = ("dram", [8, 128, (_hi - _lo) // 4], SCRATCH[_b][2])
        SCRATCH["u" + _k] = ("dram", [128, _hi - _lo], SCRATCH[_b][2])
    else:
        SCRATCH["t" + (_k if _k in WHOLE else _k[0])] = ("dram", [4, 128, _hi - _lo], SCRATCH[_b][2])

SEMAPHORES = (["qv", "qs", "qt", "qg", "sent", "kar", "rink"] + ["d%d" % k for k in range(60)]
              + [w + k for w in ("ar", "rin") for k in TILES] + ["ary%d_%d" % (k, s) for k in (2, 3) for s in range(3)]
              + ["out%d" % k for k in range(21)])

SETUP = ("one part ramp hm eye zero02 low more1 col more2 zeros46 zeros68 half0 ends slabs0 zero24 ones neg nil slabbed0 k places wv gm putA *x0 >X0 "
         "half1 order *x1 >X1 getc gneg selb02 *B0 >B0 bord slabs1 turnc *x2 >W2 putB0 slabbed1 putB1 own *B1 >B1 listc *B2 >B2 "
         ">mc ident getb kland in2 diff2 putJ *J2v seek0 *J0 sel in0 diff0 *J1 keep >J0 >J1 >J2 spread0 wn look1 w0 rn kw0 sej in1 qq")
FIRST = ("d0 Q d1 q1 d2 q2a q2b @look2 @turnb @kn @kwb @jr D Ea Eb Va Vb Ka Kb La Lb @listb @>mb @landc @landB @landJ @landb "
         "m0 @wideB0 @wideB2 @wideB1 @r @turnd @wideJ0 @wideJ1 @wideJ2 m1 x0 z0 @n0 m2 x1 z1 @n1 x2 z2 @n2")
HEAD = "ra rb < d0a q0a d0b d1a Z2b q1a a0a d2a q2a e1a q0b d1b q1b a0b a1b d2b q2b e2b > "
JHEAD = "ra rb Y0b d0a Z1b q0a d1a d0b q1a a0a d2a Z2b q2a e1a q0b d1b q1b a0b a1b d2b q2b e2b "
FTAIL = "Ba0 Ba1 Va0 Va1 Ca0 Ca1 m0a m1a m2a < ub x0a cb z0a m0b > m1b x0b z0b @n0 m2b x1 z1 @n1 x2 z2 @n2"
TAIL = "X0 X1 X2 " + FTAIL
PRE = ("Z0", "Z1", "Z2a")
JPRE = ("Z0a", "Z1a", "Z2a")
BORDER = ("t0 P0 g0", "t1 P1 g1", "< T0 U0 T1 U1 D0 T2 U2 g2 q0 D1 q1 A0 d0 d1 S0 S1 A1 o0 o1 o2 >")
JOINT = "B0 B1 V0 V1 C0 C1 M0 M1 R0 m1 R1 m2 R2 "
JTAIL = "x0 x1 z0 @n0 x2 z1 @n1 z2 @n2"
JLAST = "< x0 z0 @n0 x1 z1 @n1 x2 z2 @n2 >"
LAST = ("w0", "w1", "u2")
NEAR = "p3"
CALLS = ("k X0:0,Z0:2 X1:1,Z1:3 B0:0,b0:2 W2:d B1:1,b1:3 B2:2,b2:3 mc:0 J0:0,j0:2 J1:1,j1:3 J2:0,j2:2 mb:1 md:0 "
         "y0:1 y1:3 y2:0,y3:2 y2:d,y3:d")
ARRIVALS = (0, 2, 1)
WAY = {"MC": 4000, "MB": 4000, "MD": 3000, "Y0": 3600, "Y1": 3500, "Y2": 2600, "Y3": 2600, "K": 7000, "X0": 5500, "Z0": 5500, "X1": 5500,
       "Z1": 5500, "W2": 3000, "B0": 5500, "B1": 5500, "B2": 5500, "J0": 5500, "J1": 5500, "J2": 6500}


def slot(q, holder):
    return q ^ holder ^ 3


def bits(engines):
    m = 0
    for e in engines:
        m |= 1 << e
    return m


def transfer(T, topo, core, to, engines, sem, src, dst):
    rid, pid = topo.addr(to, core)
    return RemoteDMATransfer(dst_ids=[DstId(rid=rid, pnc=pid)], dma_engine_mask=bits(engines), remote_sem=T.sem[sem], src=src, dst=dst)


def ways(T, topo, r):
    me = T.cores[r]
    others = sorted((q for q in range(len(T.cores)) if q != r), key=lambda q: (topo.may_write(me, T.cores[q]), q ^ r))
    can = [c for c in topo.cores_of(me) if c != me and all(topo.may_write(c, T.cores[q]) for q in others)]
    return others, sorted(can, key=lambda c: topo.die(c) != topo.die(me))


def calls_of(T, topo, r):
    others, relays = ways(T, topo, r)
    every, off = topo.engines(T.cores[r], relays[0]), topo.engines(T.cores[r], T.cores[others[2]])
    rest = [e for e in every if e not in off]
    out = []
    for call in CALLS.split()[1:]:
        tiles = [w.split(":") for w in call.split(",")]
        n = len(tiles)
        both = lambda name: name in WHOLE and name + ":d" not in CALLS
        out.append([(name, None, [], off[i::n]) if k == "d" else
                    (name, relays[int(k[0])], (rest if both(name) or k[1:] else every)[i::n], off[i::n] if both(name) else [])
                    for i, (name, k) in enumerate(tiles)])
    return out


def onward(T, topo, r, relay, name):
    others = ways(T, topo, r)[0]
    off = topo.engines(relay, T.cores[others[0]])
    if name in WHOLE:
        return {others[0]: off[0::2], others[1]: off[1::2]}
    if name not in CUT:
        return {others[int(name[1])]: off}
    half = len(off) // 2
    return {others[0]: off[1::2], others[1]: off[0:half:2], others[2]: off[half::2]}


def landing(T, r, q, name):
    j = slot(r, q)
    if name in CUT:
        return T["t" + name][4 + r], "ar" + name
    if name in WHOLE:
        return T["t" + name][j], "ar" + name + ("_%d" % j if name[0] == "y" else "")
    if name[0] in "XZW":
        o = 512 * j + S * (name[0] == "Z")
        return T.xin[:, o:o + TILES[name][2] - TILES[name][1]], "ar" + name
    return T["t" + name[0]][j], "ar" + name


def relayed(T, name):
    return T["u" + name][:] if name in CUT else T["t" + name][3] if name in WHOLE else T["t" + name[0]][int(name[1])]


def first_call(T, topo, r):
    others, relays = ways(T, topo, r)
    me, there = T.cores[r], T.cores[others[2]]
    off = topo.engines(me, there)
    rest = [e for e in topo.engines(me, relays[0]) if e not in off]
    return [(q, part, to, es) for part in (0, 1)
            for q, to, es in ((others[0], relays[2 * part], [rest[4 * part]]), (others[1], relays[2 * part + 1], [rest[4 * part + 2]]),
                              (others[2], there, [off[2 * part]]))]


def relay_program(g, core, T, topo):
    n = len(T.cores)
    for r in range(n):
        sent = 0
        for q, part, to, engines in first_call(T, topo, r):
            if to == core:
                g.wait_ge(T.sem.rink, len(engines))
                one, piece = topo.engines(core, T.cores[q])[:1], T.tk[(2 + part) * n + slot(r, q)]
                g.remote_dma_fused([transfer(T, topo, core, T.cores[q], one, "kar", piece, piece)], local_sem=T.sem.sent)
                sent += 1
        for call in calls_of(T, topo, r):
            for name, to, engines, _ in call:
                if to != core:
                    continue
                if name in CUT:
                    cut = T.sem["d%d" % CUT.index(name)]
                    g.sync.wait_ge(T.sem["rin" + name], len(engines))
                    g.sync.dma_start(T["t" + name][0:n], relayed(T, name)).then_inc(cut, 16)
                    g.wait_ge(cut, 16)
                else:
                    g.wait_ge(T.sem["rin" + name], len(engines))
                legs = onward(T, topo, r, core, name)
                trs = [transfer(T, topo, core, T.cores[q], es, landing(T, r, q, name)[1],
                                T["t" + name][slot(q, r)] if name in CUT else relayed(T, name), landing(T, r, q, name)[0])
                       for q, es in legs.items()]
                g.remote_dma_fused(trs, local_sem=T.sem.sent)
                sent += sum(len(es) for es in legs.values())
        if sent:
            g.wait_ge(T.sem.sent, sent)


def meetings(ops):
    hist, out = {}, []
    for i, o in enumerate(ops):
        met = {}
        for write, views in ((False, o["r"]), (True, o["w"])):
            for (name, lo, hi, pa, pb) in views:
                bank = SCRATCH[name][0] == "psum"
                for (j, w2, lo2, hi2, pa2, pb2) in hist.get(name, ()):
                    p = ops[j]
                    over = (w2 or write) and lo < hi2 and lo2 < hi and pa < pb2 and pa2 < pb
                    if p["q"] == o["q"] and p["own"] is None and o["own"] is None:
                        if over or (bank and o["q"] == "t"):
                            apart = o["q"] == "t" and bank and o["r"][0][3] != p["r"][0][3] and pa < pb2 and pa2 < pb
                            met[j] = met.get(j, False) or (o["q"] != "t" and over) or apart
                    elif bank or over:
                        met[j] = True
        for write, views in ((False, o["r"]), (True, o["w"])):
            for v in views:
                hist.setdefault(v[0], []).append((i, write) + v[1:])
        out.append(met)
    return out


def arrange(ops):
    begin, busy = {}, {}
    for i, (o, met) in enumerate(zip(ops, meetings(ops))):
        need = {j: (HOP if ops[j]["q"] != o["q"] else SELF) if waited else 0 for j, waited in met.items()}
        need.update({j: HOP for j in o["after"] + o["soft"]})
        t = max([begin[j] + ops[j]["takes"] + lag for j, lag in need.items()] + [begin[j] + ISSUE for j in o["behind"]] + [0])
        if o["q"] is not None:
            mine = busy.setdefault(o["q"], [])
            if o["stay"]:
                t = max([t] + [hi for lo, hi in mine])
            for lo, hi in sorted(mine):
                if t + o["holds"] <= lo:
                    break
                t = max(t, hi)
            mine.append((t, t + o["holds"]))
        begin[i] = t
        o["at"] = t
    return [ops[i] for i in sorted(range(len(ops)), key=lambda i: (begin[i], i))]


def emit(g, T, ops):
    queues = {"v": g.vector, "s": g.scalar, "t": g.tensor, "g": g, "y": g.sync}
    known, waits, clocks, place, counts, marked = {q: {} for q in queues}, [], [], [], {}, set()
    at = {o["n"]: i for i, o in enumerate(ops)}
    for i, (o, met) in enumerate(zip(ops, meetings(ops))):
        q, own = o["q"], o["own"]
        deps = set(at[n] for n in o["after"]) | set(j for j, waited in met.items() if waited)
        ws = []
        if q is not None:
            k = known[q]
            for j in sorted(deps, reverse=True):
                key, pos = place[j]
                if k.get(key, -1) >= pos:
                    continue
                ws.append(j)
                marked.add(j)
                for a, b in clocks[j].items():
                    if k.get(a, -1) < b:
                        k[a] = b
                k[key] = pos
            clocks.append(dict(k))
        else:
            clocks.append({})
        waits.append(ws)
        if own is None:
            counts[q] = counts.get(q, 0) + 1
            place.append((q, counts[q]))
        else:
            place.append((("op", i), 0))
    n, value = {}, {}
    for i, o in enumerate(ops):
        if o["own"] is not None:
            value[i] = o["own"]
        elif i in marked:
            n[o["q"]] = n.get(o["q"], 0) + 1
            value[i] = ("q" + o["q"], n[o["q"]])
    for i, o in enumerate(ops):
        if o["q"] is None:
            continue
        e = queues[o["q"]]
        for j in waits[i]:
            e.wait_ge(T.sem[value[j][0]], value[j][1])
        if o["fn"] is None:
            continue
        ins = o["fn"](e)
        if o["dma"]:
            ins.then_inc(T.sem[o["own"][0]], 16)
        elif o["own"] is None and i in marked:
            ins.then_inc(T.sem[value[i][0]], 1)


def rank_program(g, core, T, topo):
    rank = T.rank_of(core)
    if rank is None:
        relay_program(g, core, T, topo)
        return
    others = ways(T, topo, rank)[0]
    ops, ordered = [], [False]

    def vw(name, lo, hi, step=1, parts=(0, 128)):
        return (name, lo, hi, step, parts)

    def ap(v):
        if len(v) == 2:
            return ap(v[0]).indirect(ap(v[1]))
        if SCRATCH[v[0]][0] == "dram":
            return T[v[0]][v[1]:v[2]]
        if len(SCRATCH[v[0]][1]) == 3:
            return T[v[0]][v[4][0]:v[4][1], v[1] // 512, v[1] % 512:(v[2] - 1) % 512 + 1]
        if v[3] == 1:
            return T[v[0]][v[4][0]:v[4][1], v[1]:v[2]]
        return T[v[0]][v[4][0]:v[4][1], v[1]:v[2]:v[3]]

    def span(v):
        return [span(v[0])[0], span(v[1])[0]] if len(v) == 2 else [v[0:3] + v[4]]

    def cycles(q, ins, out):
        if len(out) == 2:
            return 60 + SCATTER * 16 * (out[1][2] - out[1][1])
        n = (out[2] - out[1] + out[3] - 1) // out[3]
        if any(len(v) == 2 for v in ins):
            return 60 + GATHER * n
        if q == "t":
            return (MATMUL if SCRATCH[ins[0][0]][2] == F else MATMUL / 4) * max(64, n)
        if q == "g":
            return 200 + 2 * n
        return FIXED[q] + max(64, n * (2 if [SCRATCH[v[0]][0] for v in ins] == ["sbuf", "sbuf"] else 1))

    def add(q, fn, ins, out, own=None, dma=False, after=(), soft=(), holds=None, takes=None):
        r, w = [], []
        for v in ins:
            r += span(v)
        if out is not None:
            w += span(out)[0:1]
            r += span(out)[1:]
        holds = cycles(q, ins, out) if holds is None else holds
        ops.append({"n": len(ops), "q": q, "fn": fn, "r": r, "w": w, "own": own, "dma": dma, "after": list(after),
                    "soft": list(soft), "behind": [], "stay": ordered[0], "holds": holds, "takes": holds if takes is None else takes})
        return len(ops) - 1

    dmas = [0]

    def dma(q, out, src, takes):
        dmas[0] += 1
        views = [isinstance(v, tuple) for v in (out, src)]
        n = add(q, lambda e: e.dma_start(ap(out) if views[0] else out, ap(src) if views[1] else src), [src] if views[1] else [],
                out if views[0] else None, ("d%d" % (dmas[0] - 1), 16), True, holds=50, takes=DMA + takes)
        ops[-1]["stay"] = True
        return n

    def together(n):
        dmas[0] -= n - 1
        for o in ops[-n:]:
            o["own"] = ("d%d" % (dmas[0] - 1), 16 * n)

    def tt(out, a, b, op):
        add("v", lambda e: e.tensor_tensor(ap(out), ap(a), ap(b), op), [a, b], out)

    def ts(out, a, s1, op0, s2=None, op1=None):
        if isinstance(s1, tuple):
            add("v", lambda e: e.tensor_scalar(ap(out), ap(a), ap(s1), None, op0), [a, s1], out, holds=100)
        elif op1 is None:
            add("v", lambda e: e.tensor_scalar(ap(out), ap(a), s1, None, op0), [a], out)
        else:
            add("v", lambda e: e.tensor_scalar(ap(out), ap(a), s1, s2, op0, op1), [a], out)

    def cp(q, out, a):
        if q == "v":
            add("v", lambda e: e.tensor_copy(ap(out), ap(a)), [a], out)
        else:
            add("s", lambda e: e.activation(ap(out), ap(a), ACT.Copy), [a], out)

    def square(out, a):
        add("s", lambda e: e.activation(ap(out), ap(a), ACT.Square), [a], out)

    def fill(out, c):
        add("v", lambda e: e.memset(ap(out), c), [], out)

    def mm(out, lhs, rhs, start, stop):
        add("t", lambda e: e.matmul(ap(out), ap(lhs), ap(rhs), start, stop), [lhs, rhs], out)

    def select(out, src, pattern, base):
        return add("g", lambda e: e.affine_select(ap(out), ap(src), pattern, ALU.is_equal, 0.0, base, 1), [src], out)

    def count(out, pattern, base, step=0):
        return add("g", lambda e: e.iota(ap(out), pattern, base, step, allow_small_or_imprecise_dtypes=True), [], out)

    def clamp(out, a):
        ts(out, a, -0.25, ALU.max, 0.25, ALU.min)

    st = lambda p, lo, hi: vw("st%d" % p, lo, hi)
    pos = lambda p: vw("posb", p * V, (p + 1) * V)
    sm = lambda lo, hi: vw("sm", lo, hi)
    p7 = lambda lo, hi: vw("p7", lo, hi)
    ll = lambda lo, hi: vw("ll", lo, hi)
    eye = vw("eye", 0, 128)
    cut = lambda v, k: v if k is None else vw(v[0], v[1] + 64 * k, v[1] + 64 * k + 64)
    quad = lambda q: (32 * q, 32 * q + 32)
    both = (0, 64)
    sel = lambda i: vw("sel", i * 128, i * 128 + 128, 1, both)

    def table_scatter(lo, hi, base):
        ts((vw("tab", 0, V), vw("lo", lo, hi)), vw("ramp", 0, 16 * (hi - lo)), 1.0, ALU.mult, float(base), ALU.add)

    def table_gather(at, lo, hi):
        cp("v", vw("rv", at, at + 16 * (hi - lo)), (vw("tab", 0, V), vw("lo", lo, hi)))

    def to_lists(col, at, n, src="rv", mask="wv"):
        for a in range(16):
            mm(p7(col, col + n), vw(mask, 15 - a, 143 - a), vw(src, at + a, at + 16 * n, 16), a == 0, a == 15)

    def difference(p, k):
        b = 3 if k is None else slot(others[k], rank)
        for z in (0, 1):
            o = 512 * (p if k is None else b) + S * z
            mask = vw("eyeb", 128 * z + 96, 128 * z + 128, 1, quad(3)) if k is None else vw("gm", 96 * z + 32 * p, 96 * z + 32 * p + 32, 1, THEIRS)
            mm(vw(("p0", "p1", "p6")[p], 0, S, 1, quad(b)), mask, vw("xz" if k is None else "xin", o, o + S, 1, mask[4]), z == 0, z == 1)

    def to_slabs(at, lo, hi):
        for k in range(3):
            out = lambda parts: vw("p5", at + k * (hi - lo), at + (k + 1) * (hi - lo), 1, parts)
            mm(out(THEIRS), vw("hm", 96 * others[k], 96 * others[k] + 96), vw("lh", lo, hi), True, True)
            mm(out(quad(3)), vw("eyeb", 32 * rank, 32 * rank + 32), vw("lh", lo, hi), True, True)

    def slabbed(lo, hi):
        cp("v", vw("ls", lo, hi), vw("p5", lo, hi))

    def pieces(c, win, lst, drawn=False):
        def at(name, p, h, o=0):
            if name in ("xb", "zb"):
                name, o = "xz", p * S + (S if name == "zb" else 0)
            o += p * S
            return vw(name, o, o + S) if h is None else vw(name, o + h * 128, o + h * 128 + 128)

        def ends(p, z, h):
            o = lst[1] + 16 * z
            return (win(p), vw(lst[0], o, o + 16) if h is None else vw(lst[0], o + 8 * h, o + 8 * h + 8))

        mcol = lambda p, h: at("p5", p, h) if p < 2 else at("p4", 1, h)
        to = lambda p, z, h: at("st%d" % p, 0, h, (A0, B0)[c] + z * S)
        acc = lambda h: vw("p%d" % (2 + h), 0, 128)
        xx, zz, cc = ("xb", "zb", "cc") if drawn else ("xx", "zz", "p4")
        diff = lambda p, h: at("dd", p, h) if not drawn else at(("p0", "p1", "p6")[p], 0, h)

        def d(p, h=None):
            if drawn:
                difference(p, ARRIVALS[-1])
            else:
                tt(diff(p, h), ends(p, 0, h), at(zz, p, h), ALU.subtract)
        return {
            "Z": lambda p, h=None: cp("s", at(zz, p, h), ends(p, 1, h)),
            "Y": lambda p, h=None: cp("v", at(zz, p, h), ends(p, 1, h)),
            "X": lambda p, h=None: (cp("s", at(xx, p, h), ends(p, 0, h)), ops[-1].update(stay=True)),
            "W": lambda p, h=None: cp("v", at(xx, p, h), ends(p, 0, h)),
            "d": d,
            "q": lambda p, h=None: square(at("sq", p, h), diff(p, h)),
            "r": lambda h: mm(acc(h), sel(2 * c + h), vw("rn", 0, 128, 1, both), True, False),
            "s": lambda p, h: tt(at("sq", p, h), diff(p, h), diff(p, h), ALU.mult),
            "F": lambda h, k=None: tt(cut(at("p5", 1, h), k), cut(acc(h), k), cut(at("sq", 1, h), k), ALU.add),
            "G": lambda h, k=None: tt(cut(at("p5", 0, h), k), cut(at("p5", 1, h), k), cut(at("sq", 2, h), k), ALU.add),
            "Q": lambda: square(at("p5", 0, None), diff(0, None)),
            "D": lambda: tt(at("p5", 1, None), at("p5", 0, None), at("sq", 1, None), ALU.add),
            "K": lambda h: tt(at("p5", 0, h), at("p4", 0, h), at("uu", 0, h), ALU.add),
            "L": lambda h: clamp(at(cc, 0, h), at("p5", 0, h)),
            "E": lambda h: tt(at("p5", 0, h), at("p5", 1, h), at("sq", 2, h), ALU.add),
            "a": lambda p, h: mm(acc(h), eye, at("sq", p, h), False, False),
            "e": lambda p, h: mm(acc(h), eye, at("sq", p, h), False, True),
            "u": lambda h: tt(at("uu", 0, h), acc(h), at("kwo", c, h), ALU.mult),
            "c": lambda h: clamp(at(cc, 0, h), at("uu", 0, h)),
            "m": lambda p, h=None: tt(mcol(p, h), at(cc, 0, h), diff(p, h), ALU.mult),
            "x": lambda p, h=None: tt(to(p, 0, h), at(xx, p, h), mcol(p, h), ALU.add),
            "z": lambda p, h=None: tt(to(p, 1, h), at(zz, p, h), mcol(p, h), ALU.subtract),
            "B": lambda h, k: tt(cut(at("p5", 0, h), k), cut(acc(h), k), cut(at("sq", 2, h), k), ALU.add),
            "V": lambda h, k=None: tt(cut(at("uu", 0, h), k), cut(at("p5", 0, h), k), cut(at("kwo", c, h), k), ALU.mult),
            "C": lambda h, k: clamp(cut(at(cc, 0, h), k), cut(at("uu", 0, h), k)),
        }

    def run(f, text, hooks=None):
        for w in text.split():
            if w in "<>":
                ordered[0] = w == "<"
            elif w[0] == "@":
                hooks[w[1:]]()
            else:
                f[w[0]](*[int(ch) if ch.isdigit() else "ab".index(ch) for ch in w[1:]])

    def into(f, words):
        return {"n%d" % p: (lambda text: lambda: run(f, text))(words[p]) for p in range(3)}

    def half(name, p, h, o=0, width=384):
        o += p * width + h * 192
        return vw(name, o, o + 192)

    bank = lambda p, h: half(("p0", "p1", "p6")[p], 0, h)
    near = lambda p: half("p7", 0, p) if p < 2 else half(NEAR, 0, 0)
    part = lambda v, k, n=96: vw(v[0], v[1] + n * k, v[1] + n * k + n)

    def border(q, p, lo, hi):
        cp(q, vw("gb", p * 384 + lo * 192, p * 384 + hi * 192), (st(p, J0, WIN), ll(32 + 12 * lo, 32 + 12 * hi)))

    def across(out, src):
        for s in range(3):
            mm(part(out, s, 64), vw("qq", s * 128, s * 128 + 128), part(src, s, 64), True, True)

    wcol = lambda name, p: vw(name, p * 128, p * 128 + 128)
    sj = lambda p: half("sj", p, 0)
    joint = {
        "g": lambda p: border("s", p, 0, 1), "t": lambda p: border("s", p, 1, 2),
        "T": lambda s: cp("v", part(half("gb", 2, 1), s, 64), (st(2, J0, WIN), ll(44 + 4 * s, 48 + 4 * s))),
        "U": lambda s: mm(part(bank(2, 0), s, 64), vw("qq", s * 128, s * 128 + 128), part(half("gb", 2, 1), s, 64), True, True),
        "e": lambda s: tt(part(half("dj", 2, 0), s, 64), part(half("gb", 2, 0), s, 64), part(bank(2, 0), s, 64), ALU.subtract),
        "E": lambda: square(sj(2), half("dj", 2, 0)), "H": lambda p: border("v", p, 1, 2),
        "Q": lambda p: tt(sj(p), half("dj", p, 0), half("dj", p, 0), ALU.mult),
        "u": lambda a, b: cp("s", vw("gb", 192 + 64 * a, 192 + 64 * b), (st(0, J0, WIN), ll(44 + 4 * a, 44 + 4 * b))),
        "M": lambda k: tt(part(half("dj", 0, 1), k), part(half("p4", 0, 1), k), part(half("dj", 0, 0), k), ALU.mult),
        "P": lambda p: across(bank(p, 0), half("gb", p, 1)),
        "D": lambda p: tt(half("dj", p, 0), half("gb", p, 0), bank(p, 0), ALU.subtract),
        "d": lambda k: tt(part(half("dj", 2, 0), k), part(half("gb", 2, 0), k), part(bank(2, 0), k), ALU.subtract),
        "q": lambda p: square(sj(p), half("dj", p, 0)),
        "s": lambda k: tt(part(sj(2), k), part(half("dj", 2, 0), k), part(half("dj", 2, 0), k), ALU.mult),
        "S": lambda k: square(part(sj(2), k), part(half("dj", 2, 0), k)),
        "A": lambda p: tt(half("p5", 0, p), half("p2", 0, 1, 128) if p == 0 else half("p5", 0, 0), sj(p), ALU.add),
        "o": lambda p: cp("s", near(p), half("gb", p, 0)),
        "B": lambda k: tt(part(half("cc", 0, 0), k), part(half("p5", 0, 1), k), part(sj(2), k), ALU.add),
        "V": lambda k: tt(part(half("uu", 0, 0), k), part(half("p2", 0, 0, 128), k), part(half("cc", 0, 0), k), ALU.mult),
        "C": lambda k: clamp(part(half("p4", 0, 1), k), part(half("uu", 0, 0), k)),
        "m": lambda p: tt(half("dj", p, 1), half("p4", 0, 1), half("dj", p, 0), ALU.mult),
        "R": lambda p: across(bank(p, 1), half("dj", p, 1)),
        "x": lambda p: tt(st(p, J0, J0 + 192), near(p), half("dj", p, 1), ALU.add),
        "z": lambda p: tt(st(p, J0 + 192, B0), half("gb", p, 1), bank(p, 1), ALU.subtract),
    }
    last = {"w": lambda p: cp("s", wcol("yb", p), (st(p, 0, WIN), ll(120, 128))),
            "u": lambda p: cp("v", wcol("yb", p), (st(p, 0, WIN), ll(120, 128)))}

    calls_at, issued = {}, []

    def issue(names, trs, reads, engines):
        sem = "out%d" % len(issued)
        issued.append(len(ops))
        n = add("g", lambda e: e.remote_dma_fused(trs, local_sem=T.sem[sem]), reads, None, (sem, engines), holds=ISSUE, takes=1800)
        ops[-1]["behind"] = issued[-2:-1]
        calls_at.update({name: n for name in names})

    def send(first, again=0):
        if first == "k":
            legs = first_call(T, topo, rank)
            return issue(["k"], [transfer(T, topo, core, to, es, "kar" if to in T.cores else "rink", T.tk[4 * part + q],
                                          T.tk[8 + 4 * part + slot(rank, q)]) for q, part, to, es in legs], [], len(legs))
        call = [c for c in calls_of(T, topo, rank) if c[0][0] == first][again]
        trs = []
        for name, to, es, direct in call:
            src, (dst, sem) = ap(vw(*TILES[name])), landing(T, rank, others[2], name)
            if es:
                trs.append(transfer(T, topo, core, to, es, "rin" + name, src, relayed(T, name)))
            if direct:
                trs.append(transfer(T, topo, core, T.cores[others[2]], direct, sem, src, dst))
        issue([c[0] for c in call], trs, [vw(*TILES[c[0]]) for c in call], sum(len(c[2]) + len(c[3]) for c in call))

    def landed(name, senders=others, into=None):
        n = sum(len(direct) * (ways(T, topo, q)[0][2] == rank) + (len(onward(T, topo, q, to, name).get(rank, [])) if es else 0)
                for q in senders for c in calls_of(T, topo, q) for w, to, es, direct in c if w == name)
        come = add(None, None, [], into, (landing(T, senders[0], rank, name)[1], n), holds=WAY.get(name.upper(), TURN))
        ops[-1]["behind"] = [calls_at[name]]
        return come

    mine_first = lambda s: (0, 1) if rank < rank ^ s else (1, 0)
    dma("s", vw("li", 0, 64), T.ends[:, :], 600)
    staged = [dma("sy"[k // 2], T.tk[4 * (k // 2):4 * (k // 2) + 4, 64 * (k % 2):64 * (k % 2) + 64, :], src[:, :], 600)
              for k, src in enumerate((T.inv, T.stiff, T.jinv, T.jstiff))]
    for k in range(3):
        dma("y", vw("posb", k * V, (k + 1) * V, 1, THEIRS), T.pos[32 * others[k]:32 * others[k] + 32, :], LOAD * (k + 1))
        dma("y" if k else "s", vw("posb", k * V, (k + 1) * V, 1, quad(3)), T.pos[32 * rank:32 * rank + 32, k * V:(k + 1) * V], LOAD * (k + 1))
        together(2)
        if k == 1:
            dma("y", vw("li", 72, 104), T.bord[:, :], 2 * LOAD + 200)
            dma("y", vw("li", 64, 72), T.watch[:, :], 2 * LOAD + 400)
            together(2)

    def shift_by(out, a, bias):
        add("s", lambda e: e.activation(ap(out), ap(a), ACT.Identity, bias=ap(bias) if isinstance(bias, tuple) else bias),
            [a] + [bias] * isinstance(bias, tuple), out)

    def drawn(w):
        p = int(w[1])
        name, o, col = {"x": ("xz", p * 512, 64 * p), "B": ("bb", p * 512, 64 * p + 32), "J": ("jb", p * 512, 192 + 32 * p)}[w[0]]
        cp("v" if w[2:] else "s", vw(name, o, o + 512), (pos(p), vw("ls", col, col + 32)))

    lm = lambda lo, hi: vw("lm", lo, hi)
    marks = {}

    def own_places():
        shift_by(sm(128, 160), vw("ramp", 0, 512, 16), sm(96, 97))
        shift_by(sm(0, 32), sm(128, 160), float(B0))
        shift_by(sm(32, 56), sm(128, 152), float(J0))
        cp("s", sm(232, 240), sm(128, 136))

    def constants_leave():
        send("k")
        ops[-1]["after"] += staged
        marks["kept"] = dma("s", T.tk[11:16:4], T.tk[rank:8:4], 0)
        ops[-1]["after"] += staged
        marks["k"] = add(None, None, [], None, ("kar", 2 * len(others)), holds=WAY["K"])
        ops[-1]["behind"] = [calls_at["k"]]

    def border_order():
        mm(vw("p5", 320, 328), vw("eyeb", 0, 128), vw("lh", 64, 72), True, True)
        for s in (1, 2, 3):
            for k, h in enumerate(mine_first(s)):
                o = 72 + 8 * (rank ^ s) + 4 * h
                mm(vw("p5", 324 + 12 * k + 4 * s, 328 + 12 * k + 4 * s), vw("eyeb", 0, 128), vw("lh", o, o + 4), True, True)

    def finish_list(out, found, own, base, scratch):
        tt(scratch, found, own, ALU.max)
        ts(out, scratch, float(base), ALU.subtract)

    def convert(out, src):
        add("g", lambda e: e.affine_select(ap(out), ap(src), [[0, src[2] - src[1]]], ALU.is_equal, 0.0, 0, 0), [src], out)

    def lookups(i):
        cp("s", vw("rf", 384 * i, 384 * i + 384), (vw("tab", 0, V), vw("lo", 24 * i, 24 * i + 24)))

        convert(vw("rv", 1024 + 384 * i, 1408 + 384 * i), vw("rf", 384 * i, 384 * i + 384))

    def last_lists():
        tt(sm(0, 72), p7(64, 136), sm(168, 240), ALU.max)
        ops[-1]["stay"] = True
        cp("v", lm(56, 128), sm(0, 72))
        send("md")
        land_list("md")

    def widen(q, kind, p):
        name, to = {"B": ("bb", B0), "J": ("jb", W0)}[kind]
        out, src = st(p, to, to + 512), vw(name, 512 * p, 512 * p + 512)
        convert(out, src) if q == "g" else cp(q, out, src)

    def constants_land():
        for k, name in enumerate(("wc", "kc")):
            dma("y", vw(name, 0, 128, 1, both), T.tk[8:16, 64 * k:64 * k + 64, :], 400)
            ops[-1]["after"] += [marks["k"], marks["kept"]]

    def spread(c):
        for bank_, name in (("p3", "wc"), ("p4", "kc")):
            for a in (c * S, c * S + 128):
                mm(vw(bank_, a, a + 128), vw("selb", a, a + 128, 1, quad(0)), vw(name, 0, 128, 1, quad(0)), True, True)

    wn, wc, rn, kn = (vw(n, 0, 128, 1, both) for n in ("wn", "wc", "rn", "kn"))

    def negated(out, w):
        add("s", lambda e: e.activation(ap(out), ap(w), ACT.Identity, bias=-EPS, scale=-1.0), [w], out)

    def joint_product():
        tt(kn, vw("kc", 0, 128, 1, both), wn, ALU.mult)
        ops[-1]["stay"] = True

    def spreading(name, lo, hi):
        select(vw(name, 128 * lo, 128 * hi, 1, both), vw("oneb", 0, 128 * (hi - lo), 1, both), [[-1, hi - lo], [-4, 8], [0, 16]], -lo)

    def last_masks():
        for s in (1, 2, 3):
            select(vw("qq", s * 128 - 128, s * 128), vw("oneb", 0, 128), [[128 * (s >> 1) - 64, 2], [64 * (s & 1) - 32, 2], [-1, 32]], -32 * s)

    def land_list(name):
        _, lo, hi = TILES[name]
        come = landed(name)
        dma("y", vw("ll", lo, hi, 1, quad(3)), vw("lm", lo, hi, 1, quad(rank)), 100)
        dma("y", vw("ll", lo, hi, 1, (0, 96)), T["t" + name][0:3, 32 * rank:32 * rank + 32, :], 200)
        ops[-1]["after"].append(come)
        together(2)

    def land(kinds):
        come = {w: [landed(w + str(k), [others[k]]) for k in range(3)] for w in kinds}
        for h, w in enumerate(kinds):
            name = TILES[w + "0"][0]
            dma("y", T[name][0:96, :, S * h:S * h + S], T["t" + w][0:3, 0:96, :], 700)
            ops[-1]["after"] += come[w]
            ops[-1]["w"] = [span(vw(*TILES[w + str(p)], 1, THEIRS))[0] for p in range(3)]
        together(2)

    def arrived(k):
        j = slot(others[k], rank)
        for z, name in enumerate(w + str(k) for w in "XZW" if w + str(k) in TILES):
            o = 512 * j + S * z
            marks[name] = landed(name, [others[k]], vw("xin", o, o + TILES[name][2] - TILES[name][1]))
        dma("y", vw("xz", 0, 1536, 1, quad(j)), vw("xin", 512 * j, 512 * j + 512, 1, THEIRS), 400)

    steps = {
        "one": lambda: fill(vw("oneb", 0, 384), 1.0), "ones": lambda: fill(vw("oneb", 384, 512), 1.0),
        "neg": lambda: ts(vw("eyeb", 128, 256), vw("eyeb", 0, 128), -1.0, ALU.mult),
        "hm": lambda: select(vw("hm", 0, 384), vw("oneb", 0, 384), [[-16, 8], [0, 3], [-1, 16]], 0),
        "gm": lambda: select(vw("gm", 0, 96), vw("oneb", 0, 96), [[-1, 3], [-3, 32]], 0),
        "gneg": lambda: ts(vw("gm", 96, 192), vw("gm", 0, 96), -1.0, ALU.mult),
        "zero": lambda a, b: fill(vw("tab", 256 * a, 256 * b), 0.0),
        "zeros": lambda a, b: cp("s", vw("tab", 256 * a, 256 * b), vw("tab", 0, 256 * (b - a))),
        "nil": lambda: fill(sm(168, 200), 0.0),
        "putB": lambda h: table_scatter(32 + 16 * h, 48 + 16 * h, B0 + S * h),
        "turnd": lambda: to_lists(64, 1024, 72),
        "look": lookups, "seek": lambda i: table_gather(1024 + 384 * i, 24 * i, 24 * i + 24), "qq": last_masks, "wideB": lambda p: widen("ssg"[p], "B", p), "wideJ": lambda p: widen("g", "J", p),
        "part": lambda: count(vw("ki", 0, 2), [[0, 2]], 0, 1), "ramp": lambda: count(vw("ramp", 0, 128), [[1, 128]], 0),
        "more": lambda n: ts(vw("ramp", 128 * n, 256 * n), vw("ramp", 0, 128 * n), 128.0 * n, ALU.add),
        "low": lambda: ts(vw("ki", 4, 6), vw("ki", 0, 2), 15, ALU.bitwise_and), "col": lambda: cp("v", sm(96, 98), vw("ki", 4, 6)),
        "eye": lambda: select(vw("eyeb", 0, 128), vw("oneb", 0, 128), [[-1, 128]], 0),
        "wv": lambda: select(vw("wv", 0, 144), vw("oneb", 0, 144), [[-16, 9], [256, 16]], -15 * 256),
        "selb": lambda a, b: spreading("selb", a, b), "sel": lambda: spreading("sel", 0, 4),
        "sej": lambda: dma("y", vw("sej", 0, 512, 1, quad(1)), vw("sel", 0, 512, 1, quad(0)), 200),
        "ident": lambda: select(eye, vw("oneb", 0, 128), [[-1, 128]], 0),
        "places": own_places, "k": constants_leave, "kland": constants_land, "spread": spread,
        "half": lambda i: cp("v", vw("lh", 64 * i, 64 + 40 * i), vw("li", 64 * i, 64 + 40 * i)),
        "ends": lambda: cp("v", vw("lo", 0, 64), vw("li", 0, 64)), "order": border_order,
        "bord": lambda: (cp("v", vw("lh", 104, 136), vw("p5", 320, 352)), cp("v", vw("lo", 64, 96), vw("p5", 320, 352))),
        "slabs": lambda i: to_slabs(192 * i, 104 * i, 64 + 72 * i), "slabbed": lambda i: slabbed(192 * i, 192 + 96 * i),
        "putA": lambda: table_scatter(0, 32, A0), "putJ": lambda: table_scatter(72, 96, J0),
        "getc": lambda: table_gather(0, 32, 64), "getb": lambda: table_gather(640, 72, 96),
        "turnc": lambda: to_lists(0, 0, 32), "turnb": lambda: to_lists(40, 640, 24), "keep": lambda: cp("s", sm(200, 232), p7(0, 32)),
        "listc": lambda: finish_list(lm(0, 32), p7(0, 32), sm(0, 32), B0, sm(64, 96)),
        "listb": lambda: finish_list(lm(32, 56), p7(40, 64), sm(32, 56), J0, sm(96, 120)),
        "wn": lambda: negated(wn, wc), "w": lambda c: negated(vw("zz", c * S, c * S + S), vw("p3", c * S, c * S + S)),
        "kwb": lambda: ([mm(vw("p3", S + 128 * h, S + 128 * h + 128), sel(2 + h), kn, True, True) for h in (0, 1)],
                        cp("s", vw("kwo", S, 2 * S), vw("p3", S, 2 * S))),
        "kw": lambda c: tt(vw("kwo", c * S, c * S + S), vw("p4", c * S, c * S + S), vw("zz", c * S, c * S + S), ALU.mult),
        "rn": lambda: add("v", lambda e: e.reciprocal(ap(rn), ap(wn)), [wn], rn, holds=200 + 6 * 128),
        "in": arrived, "own": lambda: [difference(p, None) for p in range(3)], "diff": lambda k: [difference(p, k) for p in range(3)],
        "landc": lambda: land_list("mc"), "landb": lambda: land_list("mb"), "landB": lambda: land("Bb"), "landJ": lambda: land("Jj"),
    }

    def step(w):
        if w[0] == ">":
            send(w[1:])
        elif w[0] == "*":
            drawn(w[1:])
        else:
            name = w.rstrip("0123456789")
            steps[name](*[int(ch) for ch in w[len(name):]])

    def joint_constants(k, name, slots):
        for s in slots:
            for b in range(4):
                q = slot(b, rank)
                o, h, out = 128 * (q ^ s) + 32 * b, int(q > q ^ s), part(half("p2", 0, k, 128), s - 1, 64)
                mm(vw("p2", out[1], out[2], 1, quad(b)), vw("sej", o, o + 32, 1, quad(1)), vw(name, 64 * h, 64 * h + 64, 1, quad(1)), True, True)

    hooks = {"jr": lambda: joint_constants(1, "rn", (1, 2, 3)), "jk": lambda: joint_constants(0, "kn", (1, 2)), "jl": lambda: joint_constants(0, "kn", (3,)),
             "ll": last_lists, "kn": joint_product}
    hooks.update({w: (lambda w: lambda: step(w))(w) for w in (x[1:] for x in FIRST.split() if x[0] == "@") if w not in hooks and w not in ("n0", "n1", "n2", "r")})

    ordered[0] = True
    for w in SETUP.split():
        step(w)
    c0 = pieces(0, None, None, True)
    c1 = pieces(1, lambda p: st(p, B0, WIN), ("ll", 0))
    run(c0, FIRST, dict(hooks, r=lambda: run(c1, HEAD[:6]), **into(c1, PRE)))
    ordered[0] = False

    for t in range(SWEEPS):
        if t > 0:
            run(c0, JHEAD + TAIL, into(c1, PRE))
        run(c1, HEAD[6 * (t == 0):] + ("@ll " + TAIL.replace("m0a", "@jk m0a") if t == 0 else TAIL), dict(hooks, **into(joint, BORDER)))
        c0 = pieces(0, lambda p: st(p, 0, WIN), ("ll", 56))
        c1 = pieces(1, lambda p: st(p, 0, WIN), ("ll", 88))
        run(joint, "@jl " * (t == 0) + JOINT + (JTAIL if t < SWEEPS - 1 else JLAST),
            dict(hooks, **(into(c0, JPRE) if t < SWEEPS - 1 else into(last, LAST))))

    for name in ("y0", "y1", "y2"):
        send(name)
    send("y2", 1)
    done = [dma("s", T.y[32 * rank:32 * rank + 32, :], vw("yb", 0, 384, 1, quad(3)), 0)]

    def store(i, name, lo, hi, src, come):
        done.append(dma("ys"[i % 2], T.y[32 * lo:32 * hi, TILES[name][1]:TILES[name][2]], src, 200))
        ops[-1]["after"].append(come)

    def store_whole(q):
        for i, name in enumerate(("y2", "y3")):
            j = slot(q, rank)
            store(i, name, q, q + 1, T["t" + name][j, 32 * j:32 * j + 32, :], landed(name, [q]))

    for k in (2, 0, 1):
        store_whole(others[k])
    for i, name in enumerate(CUT):
        come = landed(name)
        for lo, hi in ((0, rank), (rank + 1, 4)):
            if lo < hi:
                store(i, name, lo, hi, T["t" + name][4 + lo:4 + hi], come)
    add("y", None, [], None, after=done, holds=1)
    add("g", None, [], None, after=issued, soft=done, holds=1)
    emit(g, T, arrange(ops))
